import numpy as np
import ml_dtypes


def mxq(x, axis, fmt="e4m3"):
    dtype, down = {"e4m3": (ml_dtypes.float8_e4m3fn, 7), "e5m2": (ml_dtypes.float8_e5m2, 14)}[fmt]
    v = np.moveaxis(np.asarray(x, np.float32).astype(ml_dtypes.bfloat16).astype(np.float64), axis, -1)
    blocks = v.reshape(v.shape[:-1] + (-1, 32))
    amax = np.abs(blocks).max(-1, keepdims=True)
    byte = np.maximum(np.where(amax > 0, np.frexp(amax)[1] - 1 + 127, 0) - down, 1)
    scale = np.exp2(byte - 127.0)
    codes = (blocks / scale).astype(np.float32).astype(dtype).astype(np.float64)
    return np.moveaxis((codes * scale).reshape(v.shape), -1, axis)


WIDE = False


def mx_kscale(k):
    if not WIDE:
        return np.ones(k)
    levels = np.array([10, -10, 5, -5, 0])
    if k % 512:
        return np.exp2(np.random.permutation(np.resize(levels, k // 32))).repeat(32)
    a = np.empty((k // 512, 16))
    for p in range(k // 512):
        a[p, :8] = np.random.permutation(np.resize(levels, 8))
        for g in range(8):
            far = levels[np.abs(levels - a[p, g]) >= 10]
            a[p, g + 8] = far[np.random.randint(len(far))]
    return np.exp2(a.ravel()).repeat(32)


def f64(x):
    return np.asarray(x).astype(np.float64)


def striped(idx):
    return np.tile(idx.reshape(-1, 16).T, (8, 1)).astype(np.uint16)


def unstriped(offs):
    return offs[:16].T.reshape(-1).astype(np.int64)


def pack_weight(w):
    k, n = w.shape
    w = f64(np.asarray(w, np.float32).astype(ml_dtypes.bfloat16)).reshape(k // 32, 32, n)
    amax = np.abs(w).max(1)
    byte = np.clip(np.where(amax > 0, np.frexp(amax)[1] - 1 + 127 - 7, 1), 1, 254)
    scaled = (w * np.exp2(127.0 - byte)[:, None, :]).reshape(k, n).astype(np.float32)
    words = np.ascontiguousarray(scaled.reshape(k // 512, 128, 4, n).transpose(0, 1, 3, 2)).astype(ml_dtypes.float8_e4m3fn).view(np.uint8)
    return words, np.ascontiguousarray(byte.astype(np.uint8).reshape(k // 512, 16, n))


def unpack_weight(words, scales):
    g, p, n, _ = words.shape
    vals = np.ascontiguousarray(words).view(ml_dtypes.float8_e4m3fn).astype(np.float64) * np.repeat(np.exp2(scales.astype(np.float64) - 127.0), 8, axis=1)[..., None]
    return vals.transpose(0, 1, 3, 2).reshape(g * 512, n)


K, T, S, V, R, W = 512, 2048, 512, 512, 256, 1024
P = 2 ** 7


def setup_inputs():
    n = np.random.standard_normal
    s = mx_kscale(K)[:, None]
    packed_xT = pack_weight(n((K, T)) * s)
    packed_eT = pack_weight(n((K, W)) * s)
    return {
        "x_words": packed_xT[0],
        "x_scales": packed_xT[1],
        "hT": (n((K, V)) / np.sqrt(K) / s).astype(np.float32),
        "e_words": packed_eT[0],
        "e_scales": packed_eT[1],
        "gain": (np.tile(np.random.uniform(0.3, 1.0, T), (P, 1))).astype(np.float32),
        "offs": striped(np.random.permutation(T)[:S]),
        "cent": striped(np.random.permutation(W)[:R]),
        "cell": striped(np.random.permutation(np.concatenate([np.arange(R), np.random.randint(0, R, S - R)]))),
    }


def reference(x_words, x_scales, hT, e_words, e_scales, gain, offs, cent, cell):
    hTq = mxq(f64(hT), 0, "e4m3")
    xq = unpack_weight(x_words, x_scales)[:, unstriped(offs)]
    y = hTq.T @ xq
    e_cent = unpack_weight(e_words, e_scales)[:, unstriped(cent)]
    z = hTq.T @ e_cent
    return np.tanh((y + z[:, unstriped(cell)]) * (f64(gain)[:1][:, unstriped(offs)]))

@@ -1,0 +1,176 @@
+from contextlib import ExitStack
+
+import concourse.mybir as mybir
+from concourse.masks import make_identity
+
+K, T, S, V, R, W = 512, 2048, 512, 512, 256, 1024
+FLOPS = 2 * K * V * (S + R)
+
+F32 = mybir.dt.float32
+BF16 = mybir.dt.bfloat16
+I32 = mybir.dt.int32
+U32 = mybir.dt.uint32
+U16 = mybir.dt.uint16
+U8 = mybir.dt.uint8
+FP8X4 = mybir.dt.float8_e4m3fn_x4
+ACT = mybir.ActivationFunctionType
+ALU = mybir.AluOpType
+P = 128
+NT = 4
+H = 256
+SPARE = 16
+VEC_UNITS = ((1, 0), (1, 1))
+
+
+def tile_picked_yivf_cal_p_kernel(tc, x_words, x_scales, hT, e_words, e_scales, gain, offs, cent, cell, out):
+    nc = tc.nc
+    with ExitStack() as ctx:
+        keep = ctx.enter_context(tc.tile_pool(name="keep", bufs=1))
+        psum = ctx.enter_context(tc.psum_pool(name="psum", bufs=2))
+
+        offs_t = keep.tile([P, S // 16], U16, name="offs_t")
+        cent_t = keep.tile([P, R // 16], U16, name="cent_t")
+        cell_t = keep.tile([P, S // 16], U16, name="cell_t")
+        xw = keep.tile([P, T], I32, name="xw", tag="xw", align_bytes=64)
+        xs = keep.tile([P, T], U8, name="xs", align_bytes=64)
+        ew = keep.tile([P, W], I32, name="ew", align_bytes=64)
+        es = keep.tile([P, W], U8, name="es", align_bytes=64)
+        gwin = keep.tile([P, T], F32, name="gwin", align_bytes=64)
+        hraw = [keep.tile([P, 4, H], F32, name=f"hraw{a}", align_bytes=64) for a in range(2)]
+        hb = [keep.tile([P, P, 4], BF16, name=f"hb{i}", tag=f"hb{i}", align_bytes=64) for i in range(NT)]
+        hq = [keep.tile([P, H], U32, name=f"hq{a}", align_bytes=64) for a in range(2)]
+        hs = [keep.tile([P, H], U8, name=f"hs{a}", align_bytes=64) for a in range(2)]
+        xg = keep.tile([P, S], U32, name="xg", align_bytes=64)
+        eg = keep.tile([P, R], U32, name="eg", align_bytes=64)
+        esg = keep.tile([P, R], U8, name="esg", align_bytes=64)
+        gg = keep.tile([P, S], F32, name="gg", align_bytes=64)
+        gcol = keep.tile([P, NT], F32, name="gcol", align_bytes=64)
+        ident = keep.tile([P, P], F32, name="ident", align_bytes=64)
+        warm = keep.tile([P, 16], F32, name="warm", align_bytes=64)
+        z = [keep.tile([P, R + SPARE], F32, name=f"z{i}", align_bytes=64) for i in range(NT)]
+        units = [(a, d) for a in range(2) for d in range(2)]
+        ygT = {u: keep.tile([P, 2, H], F32, name=f"ygT{u[0]}{u[1]}", align_bytes=64) for u in units}
+        uT = {u: keep.tile([P, 2, H], F32, name=f"uT{u[0]}{u[1]}", align_bytes=64) for u in units}
+        res = {u: keep.tile([P, 2, H], F32, name=f"res{u[0]}{u[1]}", align_bytes=64) for u in units}
+
+        nc.gpsimd.memset(es[:].bitcast(I32), 0)
+        nc.gpsimd.memset(warm[:, 0:1], 0.0)
+        nc.vector.memset(gwin[0 : P - 1, :], 0.0)
+        nc.vector.memset(xs[:].bitcast(I32), 0)
+
+        h_rows = hT.rearrange("(p j) t -> p j t", j=4)
+        nc.sync.dma_start(cent_t[:], cent)
+        nc.scalar.dma_start(ew[:], e_words[0].rearrange("p n t -> p (n t)").bitcast(I32))
+        nc.scalar.dma_start(hraw[0][:], h_rows[:, :, 0:H])
+        for q in range(4):
+            nc.sync.dma_start(es[32 * q : 32 * q + 4, :].bitcast(I32), e_scales[0, 4 * q : 4 * q + 4, :].bitcast(I32))
+        nc.sync.dma_start(offs_t[:], offs)
+        nc.sync.dma_start(gwin[P - 1 : P, :], gain[0:1, :])
+        nc.sync.dma_start(cell_t[:], cell)
+        for q in range(4):
+            nc.sync.dma_start(xs[32 * q : 32 * q + 4, :].bitcast(I32), x_scales[0, 4 * q : 4 * q + 4, :].bitcast(I32))
+        nc.scalar.activation(warm[:, 8:9], warm[:, 0:1], ACT.Tanh)
+        nc.scalar.dma_start(hraw[1][:], h_rows[:, :, H : 2 * H])
+        nc.scalar.dma_start(xw[:], x_words[0].rearrange("p n t -> p (n t)").bitcast(I32))
+
+        make_identity(nc, ident[:])
+        for i in range(NT):
+            nc.gpsimd.memset(z[i][:, R:], 0.0)
+
+        nc.vector.tensor_copy(esg[:], es[:].indirect(cent_t[:]))
+        nc.vector.tensor_copy(eg[:], ew[:].bitcast(U32).indirect(cent_t[:]))
+        nc.vector.tensor_copy(gg[:], gwin[:].indirect(offs_t[:]))
+
+        for i in range(NT):
+            a, b = divmod(i, 2)
+            cols = slice(P * b, P * (b + 1))
+            nc.scalar.copy(hb[i][:], hraw[a][:, :, cols].rearrange("p j t -> p t j"))
+            nc.vector.quantize_mx(out=hq[a][:, cols].bitcast(FP8X4), scales=hs[a][:, cols], in_=hb[i][:].rearrange("p t j -> p (t j)"))
+
+        def cell_scores(a):
+            zp = psum.tile([P, 2, R], F32, name="zp", tag=f"zp{a}", bufs=1)
+            for b in range(2):
+                cols = slice(P * b, P * (b + 1))
+                nc.tensor.matmul_mx(out=zp[:, b, :], lhsT=hq[a][:, cols].bitcast(FP8X4), lhsT_scale=hs[a][:, cols],
+                                    rhs=eg[:].bitcast(FP8X4), rhs_scale=esg[:], start=True, stop=True)
+            for b in range(2):
+                nc.scalar.copy(z[2 * a + b][:, 0:R], zp[:, b, :])
+
+        def gain_columns():
+            gT = psum.tile([P, NT, P], F32, name="gT", tag="zp0", bufs=1)
+            for c in range(NT):
+                nc.tensor.transpose(gT[:, c, :], gg[:, P * c : P * (c + 1)], ident[:])
+            nc.scalar.copy(gcol[:], gT[:, :, P - 1])
+
+        def y_side(u):
+            a, d = u
+            yp = psum.tile([P, 2, H], F32, name="yp", tag="yp", bufs=4)
+            for e in range(2):
+                cols = slice(H * d + P * e, H * d + P * (e + 1))
+                nc.tensor.matmul_mx(out=yp[:, e, :], lhsT=xg[:, cols].bitcast(FP8X4), lhsT_scale=xsg[:, cols],
+                                    rhs=hq[a][:].bitcast(FP8X4), rhs_scale=hs[a][:], start=True, stop=True)
+            for e in range(2):
+                c = 2 * d + e
+                nc.scalar.activation(ygT[u][:, e, :], yp[:, e, :], ACT.Copy, scale=gcol[:, c : c + 1])
+
+        fwd = {}
+
+        def gather_z(u):
+            a, d = u
+            for b in range(2):
+                nc.vector.tensor_copy(zg[u][:, b, :], z[2 * a + b][:].indirect(cell_t[:, 16 * d : 16 * (d + 1)]))
+            fwd[u] = psum.tile([P, 2, H], F32, name="fwd", tag=f"fwd{d}", bufs=1)
+            for b in range(2):
+                for e in range(2):
+                    nc.tensor.transpose(fwd[u][:, e, P * b : P * (b + 1)], zg[u][:, b, P * e : P * (e + 1)], ident[:])
+
+        def z_side(u):
+            a, d = u
+            for e in range(2):
+                c = 2 * d + e
+                if u in VEC_UNITS:
+                    nc.vector.scalar_tensor_tensor(uT[u][:, e, :], fwd[u][:, e, :], gcol[:, c : c + 1], ygT[u][:, e, :], ALU.mult, ALU.add)
+                else:
+                    nc.scalar.activation(uT[u][:, e, :], fwd[u][:, e, :], ACT.Copy, scale=gcol[:, c : c + 1])
+
+        out_v = out.rearrange("(i p) j -> p i j", p=P)
+
+        def finish(u):
+            a, d = u
+            back = psum.tile([P, 2, H], F32, name="back", tag=f"zp{1 - d}", bufs=1)
+            for e in range(2):
+                for b in range(2):
+                    dst = back[:, b, P * e : P * (e + 1)]
+                    cols = slice(P * b, P * (b + 1))
+                    if u in VEC_UNITS:
+                        nc.tensor.transpose(dst, uT[u][:, e, cols], ident[:])
+                    else:
+                        nc.tensor.matmul(dst, ygT[u][:, e, cols], ident[:], start=True, stop=False, is_transpose=True)
+                        nc.tensor.matmul(dst, uT[u][:, e, cols], ident[:], start=False, stop=True, is_transpose=True)
+            nc.scalar.activation(res[u][:], back[:], ACT.Tanh)
+            nc.sync.dma_start(out_v[:, 2 * a : 2 * a + 2, H * d : H * (d + 1)], res[u][:])
+
+        cell_scores(0)
+        cell_scores(1)
+        gain_columns()
+        xsg = keep.tile([P, S], U8, name="xsg", tag="hb3", align_bytes=64)
+        nc.vector.tensor_copy(xsg[:], xs[:].indirect(offs_t[:]))
+        nc.vector.tensor_copy(xg[:], xw[:].bitcast(U32).indirect(offs_t[:]))
+        zg_all = keep.tile([P, 4, 2, H], F32, name="zg_all", tag="xw", align_bytes=64)
+        zg = {u: zg_all[:, n] for n, u in enumerate(units)}
+        y_side((0, 0))
+        y_side((0, 1))
+        gather_z((0, 0))
+        z_side((0, 0))
+        y_side((1, 0))
+        gather_z((0, 1))
+        finish((0, 0))
+        z_side((0, 1))
+        y_side((1, 1))
+        finish((0, 1))
+        gather_z((1, 0))
+        gather_z((1, 1))
+        z_side((1, 0))
+        finish((1, 0))
+        z_side((1, 1))
+        finish((1, 1))

@@ -18,15 +18,15 @@ ALU = mybir.AluOpType
 P = 128
 NT = 4
 H = 256
-SPARE = 16
-VEC_UNITS = ((1, 0), (1, 1))
+ZW = R + 16
+POOL_TILES = (0, 1, 2)
 
 
 def tile_picked_yivf_cal_p_kernel(tc, x_words, x_scales, hT, e_words, e_scales, gain, offs, cent, cell, out):
     nc = tc.nc
     with ExitStack() as ctx:
         keep = ctx.enter_context(tc.tile_pool(name="keep", bufs=1))
-        psum = ctx.enter_context(tc.psum_pool(name="psum", bufs=2))
+        psum = ctx.enter_context(tc.psum_pool(name="psum", bufs=1))
 
         offs_t = keep.tile([P, S // 16], U16, name="offs_t")
         cent_t = keep.tile([P, R // 16], U16, name="cent_t")
@@ -38,37 +38,37 @@ def tile_picked_yivf_cal_p_kernel(tc, x_words, x_scales, hT, e_words, e_scales, 
         gwin = keep.tile([P, T], F32, name="gwin", align_bytes=64)
         hraw = [keep.tile([P, 4, H], F32, name=f"hraw{a}", align_bytes=64) for a in range(2)]
         hb = [keep.tile([P, P, 4], BF16, name=f"hb{i}", tag=f"hb{i}", align_bytes=64) for i in range(NT)]
-        hq = [keep.tile([P, H], U32, name=f"hq{a}", align_bytes=64) for a in range(2)]
-        hs = [keep.tile([P, H], U8, name=f"hs{a}", align_bytes=64) for a in range(2)]
+        hq = [keep.tile([P, P], U32, name=f"hq{i}", align_bytes=64) for i in range(NT)]
+        hs = [keep.tile([P, P], U8, name=f"hs{i}", align_bytes=64) for i in range(NT)]
         xg = keep.tile([P, S], U32, name="xg", align_bytes=64)
         eg = keep.tile([P, R], U32, name="eg", align_bytes=64)
         esg = keep.tile([P, R], U8, name="esg", align_bytes=64)
         gg = keep.tile([P, S], F32, name="gg", align_bytes=64)
         gcol = keep.tile([P, NT], F32, name="gcol", align_bytes=64)
+        gall = keep.tile([P, S], F32, name="gall", align_bytes=64)
         ident = keep.tile([P, P], F32, name="ident", align_bytes=64)
         warm = keep.tile([P, 16], F32, name="warm", align_bytes=64)
-        z = [keep.tile([P, R + SPARE], F32, name=f"z{i}", align_bytes=64) for i in range(NT)]
-        units = [(a, d) for a in range(2) for d in range(2)]
-        ygT = {u: keep.tile([P, 2, H], F32, name=f"ygT{u[0]}{u[1]}", align_bytes=64) for u in units}
-        uT = {u: keep.tile([P, 2, H], F32, name=f"uT{u[0]}{u[1]}", align_bytes=64) for u in units}
-        res = {u: keep.tile([P, 2, H], F32, name=f"res{u[0]}{u[1]}", align_bytes=64) for u in units}
+        z = [keep.tile([P, ZW], F32, name=f"z{i}", align_bytes=64) for i in range(NT)]
+        u = [keep.tile([P, S], F32, name=f"u{i}", align_bytes=64) for i in range(NT)]
+        v = [keep.tile([P, S], F32, name=f"v{i}", align_bytes=64) for i in range(NT)]
+        res = [keep.tile([P, S], F32, name=f"res{i}", align_bytes=64) for i in range(NT)]
 
         nc.gpsimd.memset(es[:].bitcast(I32), 0)
         nc.gpsimd.memset(warm[:, 0:1], 0.0)
+        nc.gpsimd.memset(xs[:].bitcast(I32), 0)
         nc.vector.memset(gwin[0 : P - 1, :], 0.0)
-        nc.vector.memset(xs[:].bitcast(I32), 0)
 
         h_rows = hT.rearrange("(p j) t -> p j t", j=4)
-        nc.sync.dma_start(cent_t[:], cent)
-        nc.scalar.dma_start(ew[:], e_words[0].rearrange("p n t -> p (n t)").bitcast(I32))
+        nc.sync.dma_start(offs_t[:], offs)
         nc.scalar.dma_start(hraw[0][:], h_rows[:, :, 0:H])
+        nc.sync.dma_start(gwin[P - 1 : P, :], gain[0:1, :])
+        nc.scalar.dma_start(ew[:], e_words[0].rearrange("p n t -> p (n t)").bitcast(I32))
+        nc.sync.dma_start(cent_t[:], cent)
         for q in range(4):
             nc.sync.dma_start(es[32 * q : 32 * q + 4, :].bitcast(I32), e_scales[0, 4 * q : 4 * q + 4, :].bitcast(I32))
-        nc.sync.dma_start(offs_t[:], offs)
-        nc.sync.dma_start(gwin[P - 1 : P, :], gain[0:1, :])
-        nc.sync.dma_start(cell_t[:], cell)
         for q in range(4):
-            nc.sync.dma_start(xs[32 * q : 32 * q + 4, :].bitcast(I32), x_scales[0, 4 * q : 4 * q + 4, :].bitcast(I32))
+            nc.sync.dma_start(xs[32 * q + 4 : 32 * q + 4 + 4, :].bitcast(I32), x_scales[0, 4 * q : 4 * q + 4, :].bitcast(I32))
+        nc.sync.dma_start(cell_t[:], cell)
         nc.scalar.activation(warm[:, 8:9], warm[:, 0:1], ACT.Tanh)
         nc.scalar.dma_start(hraw[1][:], h_rows[:, :, H : 2 * H])
         nc.scalar.dma_start(xw[:], x_words[0].rearrange("p n t -> p (n t)").bitcast(I32))
@@ -77,100 +77,74 @@ def tile_picked_yivf_cal_p_kernel(tc, x_words, x_scales, hT, e_words, e_scales, 
         for i in range(NT):
             nc.gpsimd.memset(z[i][:, R:], 0.0)
 
+        nc.vector.tensor_copy(gg[:], gwin[:].indirect(offs_t[:]))
         nc.vector.tensor_copy(esg[:], es[:].indirect(cent_t[:]))
         nc.vector.tensor_copy(eg[:], ew[:].bitcast(U32).indirect(cent_t[:]))
-        nc.vector.tensor_copy(gg[:], gwin[:].indirect(offs_t[:]))
 
         for i in range(NT):
             a, b = divmod(i, 2)
-            cols = slice(P * b, P * (b + 1))
-            nc.scalar.copy(hb[i][:], hraw[a][:, :, cols].rearrange("p j t -> p t j"))
-            nc.vector.quantize_mx(out=hq[a][:, cols].bitcast(FP8X4), scales=hs[a][:, cols], in_=hb[i][:].rearrange("p t j -> p (t j)"))
+            nc.scalar.copy(hb[i][:], hraw[a][:, :, P * b : P * (b + 1)].rearrange("p j t -> p t j"))
+            nc.vector.quantize_mx(out=hq[i][:].bitcast(FP8X4), scales=hs[i][:], in_=hb[i][:].rearrange("p t j -> p (t j)"))
 
-        def cell_scores(a):
-            zp = psum.tile([P, 2, R], F32, name="zp", tag=f"zp{a}", bufs=1)
-            for b in range(2):
-                cols = slice(P * b, P * (b + 1))
-                nc.tensor.matmul_mx(out=zp[:, b, :], lhsT=hq[a][:, cols].bitcast(FP8X4), lhsT_scale=hs[a][:, cols],
-                                    rhs=eg[:].bitcast(FP8X4), rhs_scale=esg[:], start=True, stop=True)
-            for b in range(2):
-                nc.scalar.copy(z[2 * a + b][:, 0:R], zp[:, b, :])
+        def cell_scores(i):
+            zp = psum.tile([P, R], F32, name="zp", tag=f"zp{i % 2}")
+            nc.tensor.matmul_mx(out=zp[:], lhsT=hq[i][:].bitcast(FP8X4), lhsT_scale=hs[i][:],
+                                rhs=eg[:].bitcast(FP8X4), rhs_scale=esg[:], start=True, stop=True)
+            nc.scalar.copy(z[i][:, 0:R], zp[:])
 
-        def gain_columns():
-            gT = psum.tile([P, NT, P], F32, name="gT", tag="zp0", bufs=1)
-            for c in range(NT):
-                nc.tensor.transpose(gT[:, c, :], gg[:, P * c : P * (c + 1)], ident[:])
-            nc.scalar.copy(gcol[:], gT[:, :, P - 1])
+        for i in range(NT):
+            cell_scores(i)
 
-        def y_side(u):
-            a, d = u
-            yp = psum.tile([P, 2, H], F32, name="yp", tag="yp", bufs=4)
-            for e in range(2):
-                cols = slice(H * d + P * e, H * d + P * (e + 1))
-                nc.tensor.matmul_mx(out=yp[:, e, :], lhsT=xg[:, cols].bitcast(FP8X4), lhsT_scale=xsg[:, cols],
-                                    rhs=hq[a][:].bitcast(FP8X4), rhs_scale=hs[a][:], start=True, stop=True)
-            for e in range(2):
-                c = 2 * d + e
-                nc.scalar.activation(ygT[u][:, e, :], yp[:, e, :], ACT.Copy, scale=gcol[:, c : c + 1])
+        gT = psum.tile([P, NT, P], F32, name="gT", tag="zp0")
+        for c in range(NT):
+            nc.tensor.transpose(gT[:, c, :], gg[:, P * c : P * (c + 1)], ident[:])
+        nc.scalar.copy(gcol[:], gT[:, :, P - 1])
+        gb = psum.tile([P, S], F32, name="gb", tag="gb")
+        for c in range(NT):
+            nc.tensor.transpose(gb[:, P * c : P * (c + 1)], gcol[:, c : c + 1].to_broadcast([P, P]), ident[:])
+        nc.scalar.copy(gall[:], gb[:])
 
-        fwd = {}
-
-        def gather_z(u):
-            a, d = u
-            for b in range(2):
-                nc.vector.tensor_copy(zg[u][:, b, :], z[2 * a + b][:].indirect(cell_t[:, 16 * d : 16 * (d + 1)]))
-            fwd[u] = psum.tile([P, 2, H], F32, name="fwd", tag=f"fwd{d}", bufs=1)
-            for b in range(2):
-                for e in range(2):
-                    nc.tensor.transpose(fwd[u][:, e, P * b : P * (b + 1)], zg[u][:, b, P * e : P * (e + 1)], ident[:])
-
-        def z_side(u):
-            a, d = u
-            for e in range(2):
-                c = 2 * d + e
-                if u in VEC_UNITS:
-                    nc.vector.scalar_tensor_tensor(uT[u][:, e, :], fwd[u][:, e, :], gcol[:, c : c + 1], ygT[u][:, e, :], ALU.mult, ALU.add)
-                else:
-                    nc.scalar.activation(uT[u][:, e, :], fwd[u][:, e, :], ACT.Copy, scale=gcol[:, c : c + 1])
-
-        out_v = out.rearrange("(i p) j -> p i j", p=P)
-
-        def finish(u):
-            a, d = u
-            back = psum.tile([P, 2, H], F32, name="back", tag=f"zp{1 - d}", bufs=1)
-            for e in range(2):
-                for b in range(2):
-                    dst = back[:, b, P * e : P * (e + 1)]
-                    cols = slice(P * b, P * (b + 1))
-                    if u in VEC_UNITS:
-                        nc.tensor.transpose(dst, uT[u][:, e, cols], ident[:])
-                    else:
-                        nc.tensor.matmul(dst, ygT[u][:, e, cols], ident[:], start=True, stop=False, is_transpose=True)
-                        nc.tensor.matmul(dst, uT[u][:, e, cols], ident[:], start=False, stop=True, is_transpose=True)
-            nc.scalar.activation(res[u][:], back[:], ACT.Tanh)
-            nc.sync.dma_start(out_v[:, 2 * a : 2 * a + 2, H * d : H * (d + 1)], res[u][:])
-
-        cell_scores(0)
-        cell_scores(1)
-        gain_columns()
-        xsg = keep.tile([P, S], U8, name="xsg", tag="hb3", align_bytes=64)
+        xsg = keep.tile([P, S], U8, name="xsg", tag="hb1", align_bytes=64)
         nc.vector.tensor_copy(xsg[:], xs[:].indirect(offs_t[:]))
+
+        zg = {}
+
+        def gather_z(i, tag):
+            zg[i] = keep.tile([P, S], F32, name="zg", tag=tag, align_bytes=64)
+            for d in range(2):
+                nc.vector.tensor_copy(zg[i][:, H * d : H * (d + 1)], z[i][:].indirect(cell_t[:, 16 * d : 16 * (d + 1)]))
+
+        gather_z(0, "zg0")
+        gather_z(1, "zg1")
         nc.vector.tensor_copy(xg[:], xw[:].bitcast(U32).indirect(offs_t[:]))
-        zg_all = keep.tile([P, 4, 2, H], F32, name="zg_all", tag="xw", align_bytes=64)
-        zg = {u: zg_all[:, n] for n, u in enumerate(units)}
-        y_side((0, 0))
-        y_side((0, 1))
-        gather_z((0, 0))
-        z_side((0, 0))
-        y_side((1, 0))
-        gather_z((0, 1))
-        finish((0, 0))
-        z_side((0, 1))
-        y_side((1, 1))
-        finish((0, 1))
-        gather_z((1, 0))
-        gather_z((1, 1))
-        z_side((1, 0))
-        finish((1, 0))
-        z_side((1, 1))
-        finish((1, 1))
+        yp = [psum.tile([P, S], F32, name=f"yp{i}", tag=f"yp{i}") for i in range(NT)]
+        for i in range(NT):
+            nc.tensor.matmul_mx(out=yp[i][:], lhsT=hq[i][:].bitcast(FP8X4), lhsT_scale=hs[i][:],
+                                rhs=xg[:].bitcast(FP8X4), rhs_scale=xsg[4:P, :], start=True, stop=True)
+
+        def add(i, cols):
+            nc.vector.tensor_tensor(u[i][:, cols], yp[i][:, cols], zg[i][:, cols], ALU.add)
+
+        def scale(i, cols):
+            if i in POOL_TILES:
+                nc.gpsimd.tensor_tensor(v[i][:, cols], u[i][:, cols], gall[:, cols], ALU.mult)
+            else:
+                nc.vector.tensor_tensor(v[i][:, cols], u[i][:, cols], gb[:, cols], ALU.mult)
+
+        def store(i, cols):
+            nc.scalar.activation(res[i][:, cols], v[i][:, cols], ACT.Tanh)
+            nc.sync.dma_start(out[P * i : P * (i + 1), cols], res[i][:, cols])
+
+        whole = slice(0, S)
+        halves = [slice(0, H), slice(H, S)]
+        gather_z(2, "xw")
+        for i in range(3):
+            add(i, whole)
+            scale(i, whole)
+            store(i, whole)
+        gather_z(3, "xw")
+        for cols in halves:
+            add(3, cols)
+        for cols in halves:
+            scale(3, cols)
+            store(3, cols)

@@ -19,7 +19,7 @@ P = 128
 NT = 4
 H = 256
 ZW = R + 16
-POOL_TILES = (0, 1, 2)
+POOL_TILES = ((1, 0), (2, 0))
 
 
 def tile_picked_yivf_cal_p_kernel(tc, x_words, x_scales, hT, e_words, e_scales, gain, offs, cent, cell, out):
@@ -36,7 +36,7 @@ def tile_picked_yivf_cal_p_kernel(tc, x_words, x_scales, hT, e_words, e_scales, 
         ew = keep.tile([P, W], I32, name="ew", align_bytes=64)
         es = keep.tile([P, W], U8, name="es", align_bytes=64)
         gwin = keep.tile([P, T], F32, name="gwin", align_bytes=64)
-        hraw = [keep.tile([P, 4, H], F32, name=f"hraw{a}", align_bytes=64) for a in range(2)]
+        hraw = [keep.tile([P, 4, H], F32, name=f"hraw{a}", tag=f"hraw{a}", align_bytes=64) for a in range(2)]
         hb = [keep.tile([P, P, 4], BF16, name=f"hb{i}", tag=f"hb{i}", align_bytes=64) for i in range(NT)]
         hq = [keep.tile([P, P], U32, name=f"hq{i}", align_bytes=64) for i in range(NT)]
         hs = [keep.tile([P, P], U8, name=f"hs{i}", align_bytes=64) for i in range(NT)]
@@ -44,7 +44,6 @@ def tile_picked_yivf_cal_p_kernel(tc, x_words, x_scales, hT, e_words, e_scales, 
         eg = keep.tile([P, R], U32, name="eg", align_bytes=64)
         esg = keep.tile([P, R], U8, name="esg", align_bytes=64)
         gg = keep.tile([P, S], F32, name="gg", align_bytes=64)
-        gcol = keep.tile([P, NT], F32, name="gcol", align_bytes=64)
         gall = keep.tile([P, S], F32, name="gall", align_bytes=64)
         ident = keep.tile([P, P], F32, name="ident", align_bytes=64)
         warm = keep.tile([P, 16], F32, name="warm", align_bytes=64)
@@ -53,25 +52,25 @@ def tile_picked_yivf_cal_p_kernel(tc, x_words, x_scales, hT, e_words, e_scales, 
         v = [keep.tile([P, S], F32, name=f"v{i}", align_bytes=64) for i in range(NT)]
         res = [keep.tile([P, S], F32, name=f"res{i}", align_bytes=64) for i in range(NT)]
 
-        nc.gpsimd.memset(es[:].bitcast(I32), 0)
+        nc.vector.memset(es[:].bitcast(I32), 0)
         nc.gpsimd.memset(warm[:, 0:1], 0.0)
-        nc.gpsimd.memset(xs[:].bitcast(I32), 0)
         nc.vector.memset(gwin[0 : P - 1, :], 0.0)
+        nc.gpsimd.memset(xs[:].bitcast(I32), 0)
 
         h_rows = hT.rearrange("(p j) t -> p j t", j=4)
         nc.sync.dma_start(offs_t[:], offs)
-        nc.scalar.dma_start(hraw[0][:], h_rows[:, :, 0:H])
         nc.sync.dma_start(gwin[P - 1 : P, :], gain[0:1, :])
-        nc.scalar.dma_start(ew[:], e_words[0].rearrange("p n t -> p (n t)").bitcast(I32))
         nc.sync.dma_start(cent_t[:], cent)
         for q in range(4):
             nc.sync.dma_start(es[32 * q : 32 * q + 4, :].bitcast(I32), e_scales[0, 4 * q : 4 * q + 4, :].bitcast(I32))
+        nc.sync.dma_start(hraw[0][:], h_rows[:, :, 0:H])
+        nc.sync.dma_start(ew[:], e_words[0].rearrange("p n t -> p (n t)").bitcast(I32))
         for q in range(4):
             nc.sync.dma_start(xs[32 * q + 4 : 32 * q + 4 + 4, :].bitcast(I32), x_scales[0, 4 * q : 4 * q + 4, :].bitcast(I32))
+        nc.sync.dma_start(hraw[1][:], h_rows[:, :, H : 2 * H])
         nc.sync.dma_start(cell_t[:], cell)
+        nc.sync.dma_start(xw[:], x_words[0].rearrange("p n t -> p (n t)").bitcast(I32))
         nc.scalar.activation(warm[:, 8:9], warm[:, 0:1], ACT.Tanh)
-        nc.scalar.dma_start(hraw[1][:], h_rows[:, :, H : 2 * H])
-        nc.scalar.dma_start(xw[:], x_words[0].rearrange("p n t -> p (n t)").bitcast(I32))
 
         make_identity(nc, ident[:])
         for i in range(NT):
@@ -87,64 +86,110 @@ def tile_picked_yivf_cal_p_kernel(tc, x_words, x_scales, hT, e_words, e_scales, 
             nc.vector.quantize_mx(out=hq[i][:].bitcast(FP8X4), scales=hs[i][:], in_=hb[i][:].rearrange("p t j -> p (t j)"))
 
         def cell_scores(i):
-            zp = psum.tile([P, R], F32, name="zp", tag=f"zp{i % 2}")
+            zp = psum.tile([P, R], F32, name="zp", tag=("zp0", "zp1", "zp2", "zp0")[i])
             nc.tensor.matmul_mx(out=zp[:], lhsT=hq[i][:].bitcast(FP8X4), lhsT_scale=hs[i][:],
                                 rhs=eg[:].bitcast(FP8X4), rhs_scale=esg[:], start=True, stop=True)
             nc.scalar.copy(z[i][:, 0:R], zp[:])
 
-        for i in range(NT):
-            cell_scores(i)
+        cell_scores(0)
+        cell_scores(1)
 
-        gT = psum.tile([P, NT, P], F32, name="gT", tag="zp0")
+        gT = psum.tile([P, NT, P], F32, name="gT", tag="zp1")
         for c in range(NT):
             nc.tensor.transpose(gT[:, c, :], gg[:, P * c : P * (c + 1)], ident[:])
+        gcol = keep.tile([P, NT], F32, name="gcol", tag="hraw1", align_bytes=64)
         nc.scalar.copy(gcol[:], gT[:, :, P - 1])
         gb = psum.tile([P, S], F32, name="gb", tag="gb")
         for c in range(NT):
             nc.tensor.transpose(gb[:, P * c : P * (c + 1)], gcol[:, c : c + 1].to_broadcast([P, P]), ident[:])
-        nc.scalar.copy(gall[:], gb[:])
 
+        cell_scores(2)
+        cell_scores(3)
+        nc.scalar.copy(gall[:], gb[:])
         xsg = keep.tile([P, S], U8, name="xsg", tag="hb1", align_bytes=64)
         nc.vector.tensor_copy(xsg[:], xs[:].indirect(offs_t[:]))
 
-        zg = {}
+        halves = [slice(0, H), slice(H, S)]
+        chunks = [slice(P * c, P * (c + 1)) for c in range(NT)]
 
-        def gather_z(i, tag):
-            zg[i] = keep.tile([P, S], F32, name="zg", tag=tag, align_bytes=64)
+        def gather_half(i, d, dst):
+            nc.vector.tensor_copy(dst[:, halves[d]], z[i][:].indirect(cell_t[:, 16 * d : 16 * (d + 1)]))
+
+        def gather_z(i, dst):
             for d in range(2):
-                nc.vector.tensor_copy(zg[i][:, H * d : H * (d + 1)], z[i][:].indirect(cell_t[:, 16 * d : 16 * (d + 1)]))
+                gather_half(i, d, dst)
 
-        gather_z(0, "zg0")
-        gather_z(1, "zg1")
+        zg0 = keep.tile([P, S], F32, name="zg0", align_bytes=64)
+        gather_z(0, zg0)
+        zT_ps = psum.tile([P, NT, P], F32, name="zT_ps", tag="zT")
+        for c in range(NT):
+            nc.tensor.transpose(zT_ps[:, c, :], zg0[:, chunks[c]], ident[:])
+        for c in range(NT):
+            nc.scalar.activation(u[0][:, chunks[c]], zT_ps[:, c, :], ACT.Copy, scale=gcol[:, c : c + 1])
+
         nc.vector.tensor_copy(xg[:], xw[:].bitcast(U32).indirect(offs_t[:]))
-        yp = [psum.tile([P, S], F32, name=f"yp{i}", tag=f"yp{i}") for i in range(NT)]
-        for i in range(NT):
+        yp = {i: psum.tile([P, S], F32, name=f"yp{i}", tag=f"yp{i}") for i in range(1, NT)}
+
+        def scores(i):
             nc.tensor.matmul_mx(out=yp[i][:], lhsT=hq[i][:].bitcast(FP8X4), lhsT_scale=hs[i][:],
                                 rhs=xg[:].bitcast(FP8X4), rhs_scale=xsg[4:P, :], start=True, stop=True)
 
-        def add(i, cols):
-            nc.vector.tensor_tensor(u[i][:, cols], yp[i][:, cols], zg[i][:, cols], ALU.add)
+        scores(1)
+        yT_ps = psum.tile([P, NT, P], F32, name="yT_ps", tag="zp2")
+        for c in range(NT):
+            nc.tensor.matmul_mx(out=yT_ps[:, c, :], lhsT=xg[:, chunks[c]].bitcast(FP8X4), lhsT_scale=xsg[4:P, chunks[c]],
+                                rhs=hq[0][:].bitcast(FP8X4), rhs_scale=hs[0][:], start=True, stop=True)
+        for i in range(2, NT):
+            scores(i)
+        for c in range(NT):
+            nc.scalar.activation(v[0][:, chunks[c]], yT_ps[:, c, :], ACT.Copy, scale=gcol[:, c : c + 1])
+        back = psum.tile([P, S], F32, name="back", tag="zp0")
+        for c in range(NT):
+            nc.tensor.matmul(back[:, chunks[c]], u[0][:, chunks[c]], ident[:], start=True, stop=False, is_transpose=True)
+            nc.tensor.matmul(back[:, chunks[c]], v[0][:, chunks[c]], ident[:], start=False, stop=True, is_transpose=True)
+        nc.scalar.activation(res[0][:], back[:], ACT.Tanh)
+        nc.sync.dma_start(out[0:P, :], res[0][:])
 
-        def scale(i, cols):
-            if i in POOL_TILES:
+        zg_pair = keep.tile([P, 2, S], F32, name="zg_pair", tag="xw", align_bytes=64)
+        zg = {1: zg_pair[:, 0, :], 2: zg_pair[:, 1, :], 3: zg_pair[:, 0, :]}
+        gather_z(1, zg[1])
+        gather_z(2, zg[2])
+
+        def add(i, d):
+            nc.vector.tensor_tensor(u[i][:, halves[d]], yp[i][:, halves[d]], zg[i][:, halves[d]], ALU.add)
+
+        def scale(i, d):
+            cols = halves[d]
+            if (i, d) in POOL_TILES:
                 nc.gpsimd.tensor_tensor(v[i][:, cols], u[i][:, cols], gall[:, cols], ALU.mult)
             else:
                 nc.vector.tensor_tensor(v[i][:, cols], u[i][:, cols], gb[:, cols], ALU.mult)
 
-        def store(i, cols):
+        def squash(i, d, store):
+            cols = halves[d]
             nc.scalar.activation(res[i][:, cols], v[i][:, cols], ACT.Tanh)
-            nc.sync.dma_start(out[P * i : P * (i + 1), cols], res[i][:, cols])
+            if store is not None:
+                nc.sync.dma_start(out[P * i : P * (i + 1), store], res[i][:, store])
 
         whole = slice(0, S)
-        halves = [slice(0, H), slice(H, S)]
-        gather_z(2, "xw")
-        for i in range(3):
-            add(i, whole)
-            scale(i, whole)
-            store(i, whole)
-        gather_z(3, "xw")
-        for cols in halves:
-            add(3, cols)
-        for cols in halves:
-            scale(3, cols)
-            store(3, cols)
+
+        add(1, 0)
+        scale(1, 0)
+        add(1, 1)
+        gather_half(3, 0, zg[3])
+        scale(1, 1)
+        squash(1, 1, halves[1])
+        squash(1, 0, halves[0])
+        gather_half(3, 1, zg[3])
+        add(2, 0)
+        scale(2, 0)
+        add(2, 1)
+        add(3, 0)
+        scale(2, 1)
+        squash(2, 1, halves[1])
+        squash(2, 0, halves[0])
+        add(3, 1)
+        scale(3, 0)
+        squash(3, 0, halves[0])
+        scale(3, 1)
+        squash(3, 1, halves[1])

@@ -19,7 +19,6 @@ P = 128
 NT = 4
 H = 256
 ZW = R + 16
-POOL_TILES = ((1, 0), (2, 0))
 
 
 def tile_picked_yivf_cal_p_kernel(tc, x_words, x_scales, hT, e_words, e_scales, gain, offs, cent, cell, out):
@@ -36,7 +35,10 @@ def tile_picked_yivf_cal_p_kernel(tc, x_words, x_scales, hT, e_words, e_scales, 
         ew = keep.tile([P, W], I32, name="ew", align_bytes=64)
         es = keep.tile([P, W], U8, name="es", align_bytes=64)
         gwin = keep.tile([P, T], F32, name="gwin", align_bytes=64)
-        hraw = [keep.tile([P, 4, H], F32, name=f"hraw{a}", tag=f"hraw{a}", align_bytes=64) for a in range(2)]
+        h01 = keep.tile([P, 4, H], F32, name="h01", align_bytes=64)
+        h2 = keep.tile([P, 4, P], F32, name="h2", tag="h2", align_bytes=64)
+        h3 = keep.tile([P, 4, P], F32, name="h3", align_bytes=64)
+        hraw = [h01[:, :, 0:P], h01[:, :, P:H], h2[:], h3[:]]
         hb = [keep.tile([P, P, 4], BF16, name=f"hb{i}", tag=f"hb{i}", align_bytes=64) for i in range(NT)]
         hq = [keep.tile([P, P], U32, name=f"hq{i}", align_bytes=64) for i in range(NT)]
         hs = [keep.tile([P, P], U8, name=f"hs{i}", align_bytes=64) for i in range(NT)]
@@ -44,12 +46,11 @@ def tile_picked_yivf_cal_p_kernel(tc, x_words, x_scales, hT, e_words, e_scales, 
         eg = keep.tile([P, R], U32, name="eg", align_bytes=64)
         esg = keep.tile([P, R], U8, name="esg", align_bytes=64)
         gg = keep.tile([P, S], F32, name="gg", align_bytes=64)
-        gall = keep.tile([P, S], F32, name="gall", align_bytes=64)
         ident = keep.tile([P, P], F32, name="ident", align_bytes=64)
         warm = keep.tile([P, 16], F32, name="warm", align_bytes=64)
         z = [keep.tile([P, ZW], F32, name=f"z{i}", align_bytes=64) for i in range(NT)]
-        u = [keep.tile([P, S], F32, name=f"u{i}", align_bytes=64) for i in range(NT)]
-        v = [keep.tile([P, S], F32, name=f"v{i}", align_bytes=64) for i in range(NT)]
+        u0 = keep.tile([P, S], F32, name="u0", align_bytes=64)
+        v0 = keep.tile([P, S], F32, name="v0", align_bytes=64)
         res = [keep.tile([P, S], F32, name=f"res{i}", align_bytes=64) for i in range(NT)]
 
         nc.vector.memset(es[:].bitcast(I32), 0)
@@ -63,133 +64,141 @@ def tile_picked_yivf_cal_p_kernel(tc, x_words, x_scales, hT, e_words, e_scales, 
         nc.sync.dma_start(cent_t[:], cent)
         for q in range(4):
             nc.sync.dma_start(es[32 * q : 32 * q + 4, :].bitcast(I32), e_scales[0, 4 * q : 4 * q + 4, :].bitcast(I32))
-        nc.sync.dma_start(hraw[0][:], h_rows[:, :, 0:H])
+        nc.sync.dma_start(h01[:], h_rows[:, :, 0:H])
         nc.sync.dma_start(ew[:], e_words[0].rearrange("p n t -> p (n t)").bitcast(I32))
         for q in range(4):
             nc.sync.dma_start(xs[32 * q + 4 : 32 * q + 4 + 4, :].bitcast(I32), x_scales[0, 4 * q : 4 * q + 4, :].bitcast(I32))
-        nc.sync.dma_start(hraw[1][:], h_rows[:, :, H : 2 * H])
+        nc.sync.dma_start(h2[:], h_rows[:, :, 2 * P : 3 * P])
         nc.sync.dma_start(cell_t[:], cell)
         nc.sync.dma_start(xw[:], x_words[0].rearrange("p n t -> p (n t)").bitcast(I32))
+        nc.sync.dma_start(h3[:], h_rows[:, :, 3 * P : 4 * P])
         nc.scalar.activation(warm[:, 8:9], warm[:, 0:1], ACT.Tanh)
 
         make_identity(nc, ident[:])
         for i in range(NT):
             nc.gpsimd.memset(z[i][:, R:], 0.0)
 
-        nc.vector.tensor_copy(gg[:], gwin[:].indirect(offs_t[:]))
-        nc.vector.tensor_copy(esg[:], es[:].indirect(cent_t[:]))
-        nc.vector.tensor_copy(eg[:], ew[:].bitcast(U32).indirect(cent_t[:]))
+        halves = [slice(0, H), slice(H, S)]
+        chunks = [slice(P * c, P * (c + 1)) for c in range(NT)]
+        lists = [slice(0, H // 16), slice(H // 16, S // 16)]
 
-        for i in range(NT):
-            a, b = divmod(i, 2)
-            nc.scalar.copy(hb[i][:], hraw[a][:, :, P * b : P * (b + 1)].rearrange("p j t -> p t j"))
+        def interleave(i):
+            turned = hraw[i].rearrange("p j t -> p t j")
+            if i == 3:
+                nc.gpsimd.tensor_scalar(hb[i][:], turned, 1.0, 0.0, ALU.mult, ALU.add)
+            else:
+                nc.scalar.copy(hb[i][:], turned)
+
+        def quantize(i):
             nc.vector.quantize_mx(out=hq[i][:].bitcast(FP8X4), scales=hs[i][:], in_=hb[i][:].rearrange("p t j -> p (t j)"))
 
-        def cell_scores(i):
-            zp = psum.tile([P, R], F32, name="zp", tag=("zp0", "zp1", "zp2", "zp0")[i])
+        def cell_scores(i, tag):
+            zp = psum.tile([P, R], F32, name="zp", tag=tag)
             nc.tensor.matmul_mx(out=zp[:], lhsT=hq[i][:].bitcast(FP8X4), lhsT_scale=hs[i][:],
                                 rhs=eg[:].bitcast(FP8X4), rhs_scale=esg[:], start=True, stop=True)
             nc.scalar.copy(z[i][:, 0:R], zp[:])
 
-        cell_scores(0)
-        cell_scores(1)
+        ysb = {}
 
-        gT = psum.tile([P, NT, P], F32, name="gT", tag="zp1")
-        for c in range(NT):
-            nc.tensor.transpose(gT[:, c, :], gg[:, P * c : P * (c + 1)], ident[:])
-        gcol = keep.tile([P, NT], F32, name="gcol", tag="hraw1", align_bytes=64)
-        nc.scalar.copy(gcol[:], gT[:, :, P - 1])
-        gb = psum.tile([P, S], F32, name="gb", tag="gb")
-        for c in range(NT):
-            nc.tensor.transpose(gb[:, P * c : P * (c + 1)], gcol[:, c : c + 1].to_broadcast([P, P]), ident[:])
+        def scores(units, tag):
+            yp = psum.tile([P, len(units), H], F32, name="yp", tag=tag)
+            for n, (i, d) in enumerate(units):
+                nc.tensor.matmul_mx(out=yp[:, n, :], lhsT=hq[i][:].bitcast(FP8X4), lhsT_scale=hs[i][:],
+                                    rhs=xg[:, halves[d]].bitcast(FP8X4), rhs_scale=xsg[4:P, halves[d]], start=True, stop=True)
+            yc = keep.tile([P, len(units), H], F32, name="yc%d%d" % units[0], align_bytes=64)
+            nc.scalar.copy(yc[:], yp[:])
+            for n, unit in enumerate(units):
+                ysb[unit] = yc[:, n, :]
 
-        cell_scores(2)
-        cell_scores(3)
-        nc.scalar.copy(gall[:], gb[:])
-        xsg = keep.tile([P, S], U8, name="xsg", tag="hb1", align_bytes=64)
-        nc.vector.tensor_copy(xsg[:], xs[:].indirect(offs_t[:]))
+        sums = {i: keep.tile([P, S], F32, name=f"sum{i}", align_bytes=64) for i in range(1, NT)}
+        scaled = {i: keep.tile([P, S], F32, name=f"scaled{i}", align_bytes=64) for i in range(1, NT)}
 
-        halves = [slice(0, H), slice(H, S)]
-        chunks = [slice(P * c, P * (c + 1)) for c in range(NT)]
+        def look_up(i, d):
+            nc.vector.tensor_tensor(sums[i][:, halves[d]], z[i][:].indirect(cell_t[:, lists[d]]), ysb[i, d], ALU.add)
 
-        def gather_half(i, d, dst):
-            nc.vector.tensor_copy(dst[:, halves[d]], z[i][:].indirect(cell_t[:, 16 * d : 16 * (d + 1)]))
+        def scale(i, cols):
+            nc.vector.tensor_tensor(scaled[i][:, cols], sums[i][:, cols], gb[:, cols], ALU.mult)
 
-        def gather_z(i, dst):
-            for d in range(2):
-                gather_half(i, d, dst)
-
-        zg0 = keep.tile([P, S], F32, name="zg0", align_bytes=64)
-        gather_z(0, zg0)
-        zT_ps = psum.tile([P, NT, P], F32, name="zT_ps", tag="zT")
-        for c in range(NT):
-            nc.tensor.transpose(zT_ps[:, c, :], zg0[:, chunks[c]], ident[:])
-        for c in range(NT):
-            nc.scalar.activation(u[0][:, chunks[c]], zT_ps[:, c, :], ACT.Copy, scale=gcol[:, c : c + 1])
-
-        nc.vector.tensor_copy(xg[:], xw[:].bitcast(U32).indirect(offs_t[:]))
-        yp = {i: psum.tile([P, S], F32, name=f"yp{i}", tag=f"yp{i}") for i in range(1, NT)}
-
-        def scores(i):
-            nc.tensor.matmul_mx(out=yp[i][:], lhsT=hq[i][:].bitcast(FP8X4), lhsT_scale=hs[i][:],
-                                rhs=xg[:].bitcast(FP8X4), rhs_scale=xsg[4:P, :], start=True, stop=True)
-
-        scores(1)
-        yT_ps = psum.tile([P, NT, P], F32, name="yT_ps", tag="zp2")
-        for c in range(NT):
-            nc.tensor.matmul_mx(out=yT_ps[:, c, :], lhsT=xg[:, chunks[c]].bitcast(FP8X4), lhsT_scale=xsg[4:P, chunks[c]],
-                                rhs=hq[0][:].bitcast(FP8X4), rhs_scale=hs[0][:], start=True, stop=True)
-        for i in range(2, NT):
-            scores(i)
-        for c in range(NT):
-            nc.scalar.activation(v[0][:, chunks[c]], yT_ps[:, c, :], ACT.Copy, scale=gcol[:, c : c + 1])
-        back = psum.tile([P, S], F32, name="back", tag="zp0")
-        for c in range(NT):
-            nc.tensor.matmul(back[:, chunks[c]], u[0][:, chunks[c]], ident[:], start=True, stop=False, is_transpose=True)
-            nc.tensor.matmul(back[:, chunks[c]], v[0][:, chunks[c]], ident[:], start=False, stop=True, is_transpose=True)
-        nc.scalar.activation(res[0][:], back[:], ACT.Tanh)
-        nc.sync.dma_start(out[0:P, :], res[0][:])
-
-        zg_pair = keep.tile([P, 2, S], F32, name="zg_pair", tag="xw", align_bytes=64)
-        zg = {1: zg_pair[:, 0, :], 2: zg_pair[:, 1, :], 3: zg_pair[:, 0, :]}
-        gather_z(1, zg[1])
-        gather_z(2, zg[2])
-
-        def add(i, d):
-            nc.vector.tensor_tensor(u[i][:, halves[d]], yp[i][:, halves[d]], zg[i][:, halves[d]], ALU.add)
-
-        def scale(i, d):
-            cols = halves[d]
-            if (i, d) in POOL_TILES:
-                nc.gpsimd.tensor_tensor(v[i][:, cols], u[i][:, cols], gall[:, cols], ALU.mult)
-            else:
-                nc.vector.tensor_tensor(v[i][:, cols], u[i][:, cols], gb[:, cols], ALU.mult)
-
-        def squash(i, d, store):
-            cols = halves[d]
-            nc.scalar.activation(res[i][:, cols], v[i][:, cols], ACT.Tanh)
-            if store is not None:
-                nc.sync.dma_start(out[P * i : P * (i + 1), store], res[i][:, store])
+        def squash(i, cols):
+            nc.scalar.activation(res[i][:, cols], scaled[i][:, cols], ACT.Tanh)
+            nc.sync.dma_start(out[P * i : P * (i + 1), cols], res[i][:, cols])
 
         whole = slice(0, S)
 
-        add(1, 0)
-        scale(1, 0)
-        add(1, 1)
-        gather_half(3, 0, zg[3])
-        scale(1, 1)
-        squash(1, 1, halves[1])
-        squash(1, 0, halves[0])
-        gather_half(3, 1, zg[3])
-        add(2, 0)
-        scale(2, 0)
-        add(2, 1)
-        add(3, 0)
-        scale(2, 1)
-        squash(2, 1, halves[1])
-        squash(2, 0, halves[0])
-        add(3, 1)
-        scale(3, 0)
-        squash(3, 0, halves[0])
-        scale(3, 1)
-        squash(3, 1, halves[1])
+        nc.vector.tensor_copy(gg[:], gwin[:].indirect(offs_t[:]))
+        nc.vector.tensor_copy(esg[:], es[:].indirect(cent_t[:]))
+        nc.vector.tensor_copy(eg[:], ew[:].bitcast(U32).indirect(cent_t[:]))
+        for i in range(2):
+            interleave(i)
+            quantize(i)
+        cell_scores(0, "b0")
+        cell_scores(1, "b1")
+
+        xsg = keep.tile([P, S], U8, name="xsg", tag="hb1", align_bytes=64)
+        nc.vector.tensor_copy(xsg[:], xs[:].indirect(offs_t[:]))
+        interleave(2)
+        quantize(2)
+
+        gT = psum.tile([P, NT, P], F32, name="gT", tag="b1")
+        for c in range(NT):
+            nc.tensor.transpose(gT[:, c, :], gg[:, chunks[c]], ident[:])
+        gcol = keep.tile([P, NT], F32, name="gcol", tag="h2", align_bytes=64)
+        nc.scalar.copy(gcol[:], gT[:, :, P - 1])
+        cell_scores(2, "b0")
+
+        zg0a = keep.tile([P, H], F32, name="zg0a", align_bytes=64)
+        nc.vector.tensor_copy(zg0a[:], z[0][:].indirect(cell_t[:, lists[0]]))
+        zTa = psum.tile([P, 2, P], F32, name="zTa", tag="b2")
+        for c in range(2):
+            nc.tensor.transpose(zTa[:, c, :], zg0a[:, chunks[c]], ident[:])
+        for c in range(2):
+            nc.scalar.activation(u0[:, chunks[c]], zTa[:, c, :], ACT.Copy, scale=gcol[:, c : c + 1])
+
+        for d in range(2):
+            nc.vector.tensor_copy(xg[:, halves[d]], xw[:].bitcast(U32).indirect(offs_t[:, lists[d]]))
+        zg0b = keep.tile([P, H], F32, name="zg0b", tag="xw", align_bytes=64)
+        nc.vector.tensor_copy(zg0b[:], z[0][:].indirect(cell_t[:, lists[1]]))
+
+        scores([(1, 0)], "b3")
+        scores([(1, 1)], "b4")
+        scores([(2, 0), (2, 1)], "b5")
+        interleave(3)
+        look_up(1, 0)
+        quantize(3)
+        look_up(1, 1)
+
+        yT_ps = psum.tile([P, NT, P], F32, name="yT_ps", tag="b6")
+        for c in range(NT):
+            nc.tensor.matmul_mx(out=yT_ps[:, c, :], lhsT=xg[:, chunks[c]].bitcast(FP8X4), lhsT_scale=xsg[4:P, chunks[c]],
+                                rhs=hq[0][:].bitcast(FP8X4), rhs_scale=hs[0][:], start=True, stop=True)
+        zTb = psum.tile([P, 2, P], F32, name="zTb", tag="b2")
+        for c in range(2):
+            nc.tensor.transpose(zTb[:, c, :], zg0b[:, chunks[c]], ident[:])
+        gb = psum.tile([P, S], F32, name="gb", tag="b5")
+        for c in range(NT):
+            nc.tensor.transpose(gb[:, chunks[c]], gcol[:, c : c + 1].to_broadcast([P, P]), ident[:])
+        cell_scores(3, "b1")
+        scores([(3, 0), (3, 1)], "b7")
+        for c in range(2):
+            nc.scalar.activation(u0[:, chunks[2 + c]], zTb[:, c, :], ACT.Copy, scale=gcol[:, 2 + c : 3 + c])
+        for c in range(NT):
+            nc.scalar.activation(v0[:, chunks[c]], yT_ps[:, c, :], ACT.Copy, scale=gcol[:, c : c + 1])
+        back = psum.tile([P, S], F32, name="back", tag="b4")
+        for c in range(NT):
+            nc.tensor.matmul(back[:, chunks[c]], u0[:, chunks[c]], ident[:], start=True, stop=False, is_transpose=True)
+            nc.tensor.matmul(back[:, chunks[c]], v0[:, chunks[c]], ident[:], start=False, stop=True, is_transpose=True)
+
+        look_up(2, 0)
+        scale(1, whole)
+        look_up(2, 1)
+        squash(1, whole)
+        look_up(3, 0)
+        nc.scalar.activation(res[0][:], back[:], ACT.Tanh)
+        nc.sync.dma_start(out[0:P, :], res[0][:])
+        scale(2, whole)
+        look_up(3, 1)
+        squash(2, whole)
+        for d in range(2):
+            scale(3, halves[d])
+        for d in range(2):
+            squash(3, halves[d])

@@ -35,10 +35,10 @@ def tile_picked_yivf_cal_p_kernel(tc, x_words, x_scales, hT, e_words, e_scales, 
         ew = keep.tile([P, W], I32, name="ew", align_bytes=64)
         es = keep.tile([P, W], U8, name="es", align_bytes=64)
         gwin = keep.tile([P, T], F32, name="gwin", align_bytes=64)
-        h01 = keep.tile([P, 4, H], F32, name="h01", align_bytes=64)
-        h2 = keep.tile([P, 4, P], F32, name="h2", tag="h2", align_bytes=64)
+        h0 = keep.tile([P, 4, P], F32, name="h0", tag="h0", align_bytes=64)
+        h12 = keep.tile([P, 4, H], F32, name="h12", tag="h12", align_bytes=64)
         h3 = keep.tile([P, 4, P], F32, name="h3", align_bytes=64)
-        hraw = [h01[:, :, 0:P], h01[:, :, P:H], h2[:], h3[:]]
+        hraw = [h0[:], h12[:, :, 0:P], h12[:, :, P:H], h3[:]]
         hb = [keep.tile([P, P, 4], BF16, name=f"hb{i}", tag=f"hb{i}", align_bytes=64) for i in range(NT)]
         hq = [keep.tile([P, P], U32, name=f"hq{i}", align_bytes=64) for i in range(NT)]
         hs = [keep.tile([P, P], U8, name=f"hs{i}", align_bytes=64) for i in range(NT)]
@@ -49,7 +49,6 @@ def tile_picked_yivf_cal_p_kernel(tc, x_words, x_scales, hT, e_words, e_scales, 
         ident = keep.tile([P, P], F32, name="ident", align_bytes=64)
         warm = keep.tile([P, 16], F32, name="warm", align_bytes=64)
         z = [keep.tile([P, ZW], F32, name=f"z{i}", align_bytes=64) for i in range(NT)]
-        u0 = keep.tile([P, S], F32, name="u0", align_bytes=64)
         v0 = keep.tile([P, S], F32, name="v0", align_bytes=64)
         res = [keep.tile([P, S], F32, name=f"res{i}", align_bytes=64) for i in range(NT)]
 
@@ -64,12 +63,12 @@ def tile_picked_yivf_cal_p_kernel(tc, x_words, x_scales, hT, e_words, e_scales, 
         nc.sync.dma_start(cent_t[:], cent)
         for q in range(4):
             nc.sync.dma_start(es[32 * q : 32 * q + 4, :].bitcast(I32), e_scales[0, 4 * q : 4 * q + 4, :].bitcast(I32))
-        nc.sync.dma_start(h01[:], h_rows[:, :, 0:H])
         nc.sync.dma_start(ew[:], e_words[0].rearrange("p n t -> p (n t)").bitcast(I32))
+        nc.sync.dma_start(h0[:], h_rows[:, :, 0:P])
         for q in range(4):
             nc.sync.dma_start(xs[32 * q + 4 : 32 * q + 4 + 4, :].bitcast(I32), x_scales[0, 4 * q : 4 * q + 4, :].bitcast(I32))
-        nc.sync.dma_start(h2[:], h_rows[:, :, 2 * P : 3 * P])
         nc.sync.dma_start(cell_t[:], cell)
+        nc.sync.dma_start(h12[:], h_rows[:, :, P : 3 * P])
         nc.sync.dma_start(xw[:], x_words[0].rearrange("p n t -> p (n t)").bitcast(I32))
         nc.sync.dma_start(h3[:], h_rows[:, :, 3 * P : 4 * P])
         nc.scalar.activation(warm[:, 8:9], warm[:, 0:1], ACT.Tanh)
@@ -84,7 +83,7 @@ def tile_picked_yivf_cal_p_kernel(tc, x_words, x_scales, hT, e_words, e_scales, 
 
         def interleave(i):
             turned = hraw[i].rearrange("p j t -> p t j")
-            if i == 3:
+            if i % 2:
                 nc.gpsimd.tensor_scalar(hb[i][:], turned, 1.0, 0.0, ALU.mult, ALU.add)
             else:
                 nc.scalar.copy(hb[i][:], turned)
@@ -128,31 +127,32 @@ def tile_picked_yivf_cal_p_kernel(tc, x_words, x_scales, hT, e_words, e_scales, 
         nc.vector.tensor_copy(gg[:], gwin[:].indirect(offs_t[:]))
         nc.vector.tensor_copy(esg[:], es[:].indirect(cent_t[:]))
         nc.vector.tensor_copy(eg[:], ew[:].bitcast(U32).indirect(cent_t[:]))
-        for i in range(2):
-            interleave(i)
-            quantize(i)
+        interleave(0)
+        quantize(0)
         cell_scores(0, "b0")
-        cell_scores(1, "b1")
-
-        xsg = keep.tile([P, S], U8, name="xsg", tag="hb1", align_bytes=64)
+        xsg = keep.tile([P, S], U8, name="xsg", tag="hb0", align_bytes=64)
         nc.vector.tensor_copy(xsg[:], xs[:].indirect(offs_t[:]))
-        interleave(2)
-        quantize(2)
 
         gT = psum.tile([P, NT, P], F32, name="gT", tag="b1")
         for c in range(NT):
             nc.tensor.transpose(gT[:, c, :], gg[:, chunks[c]], ident[:])
-        gcol = keep.tile([P, NT], F32, name="gcol", tag="h2", align_bytes=64)
+        gcol = keep.tile([P, NT], F32, name="gcol", tag="h0", align_bytes=64)
         nc.scalar.copy(gcol[:], gT[:, :, P - 1])
-        cell_scores(2, "b0")
 
+        interleave(1)
+        interleave(2)
         zg0a = keep.tile([P, H], F32, name="zg0a", align_bytes=64)
         nc.vector.tensor_copy(zg0a[:], z[0][:].indirect(cell_t[:, lists[0]]))
+        quantize(1)
+        cell_scores(1, "b1")
+        quantize(2)
+        u0 = keep.tile([P, S], F32, name="u0", tag="h12", align_bytes=64)
         zTa = psum.tile([P, 2, P], F32, name="zTa", tag="b2")
         for c in range(2):
             nc.tensor.transpose(zTa[:, c, :], zg0a[:, chunks[c]], ident[:])
         for c in range(2):
             nc.scalar.activation(u0[:, chunks[c]], zTa[:, c, :], ACT.Copy, scale=gcol[:, c : c + 1])
+        cell_scores(2, "b0")
 
         for d in range(2):
             nc.vector.tensor_copy(xg[:, halves[d]], xw[:].bitcast(U32).indirect(offs_t[:, lists[d]]))
@@ -163,15 +163,15 @@ def tile_picked_yivf_cal_p_kernel(tc, x_words, x_scales, hT, e_words, e_scales, 
         scores([(1, 1)], "b4")
         scores([(2, 0), (2, 1)], "b5")
         interleave(3)
-        look_up(1, 0)
         quantize(3)
+        look_up(1, 0)
         look_up(1, 1)
 
         yT_ps = psum.tile([P, NT, P], F32, name="yT_ps", tag="b6")
         for c in range(NT):
             nc.tensor.matmul_mx(out=yT_ps[:, c, :], lhsT=xg[:, chunks[c]].bitcast(FP8X4), lhsT_scale=xsg[4:P, chunks[c]],
                                 rhs=hq[0][:].bitcast(FP8X4), rhs_scale=hs[0][:], start=True, stop=True)
-        zTb = psum.tile([P, 2, P], F32, name="zTb", tag="b2")
+        zTb = psum.tile([P, 2, P], F32, name="zTb", tag="b3")
         for c in range(2):
             nc.tensor.transpose(zTb[:, c, :], zg0b[:, chunks[c]], ident[:])
         gb = psum.tile([P, S], F32, name="gb", tag="b5")

@@ -40,20 +40,18 @@ def tile_picked_yivf_cal_p_kernel(tc, x_words, x_scales, hT, e_words, e_scales, 
         h3 = keep.tile([P, 4, P], F32, name="h3", align_bytes=64)
         hraw = [h0[:], h12[:, :, 0:P], h12[:, :, P:H], h3[:]]
         hb = [keep.tile([P, P, 4], BF16, name=f"hb{i}", tag=f"hb{i}", align_bytes=64) for i in range(NT)]
-        hq = [keep.tile([P, P], U32, name=f"hq{i}", align_bytes=64) for i in range(NT)]
+        hq = [keep.tile([P, P], U32, name=f"hq{i}", tag=f"hq{i}", align_bytes=64) for i in range(NT)]
         hs = [keep.tile([P, P], U8, name=f"hs{i}", align_bytes=64) for i in range(NT)]
         xg = keep.tile([P, S], U32, name="xg", align_bytes=64)
         eg = keep.tile([P, R], U32, name="eg", align_bytes=64)
         esg = keep.tile([P, R], U8, name="esg", align_bytes=64)
         gg = keep.tile([P, S], F32, name="gg", align_bytes=64)
         ident = keep.tile([P, P], F32, name="ident", align_bytes=64)
-        warm = keep.tile([P, 16], F32, name="warm", align_bytes=64)
         z = [keep.tile([P, ZW], F32, name=f"z{i}", align_bytes=64) for i in range(NT)]
         v0 = keep.tile([P, S], F32, name="v0", align_bytes=64)
         res = [keep.tile([P, S], F32, name=f"res{i}", align_bytes=64) for i in range(NT)]
 
         nc.vector.memset(es[:].bitcast(I32), 0)
-        nc.gpsimd.memset(warm[:, 0:1], 0.0)
         nc.vector.memset(gwin[0 : P - 1, :], 0.0)
         nc.gpsimd.memset(xs[:].bitcast(I32), 0)
 
@@ -71,7 +69,6 @@ def tile_picked_yivf_cal_p_kernel(tc, x_words, x_scales, hT, e_words, e_scales, 
         nc.sync.dma_start(h12[:], h_rows[:, :, P : 3 * P])
         nc.sync.dma_start(xw[:], x_words[0].rearrange("p n t -> p (n t)").bitcast(I32))
         nc.sync.dma_start(h3[:], h_rows[:, :, 3 * P : 4 * P])
-        nc.scalar.activation(warm[:, 8:9], warm[:, 0:1], ACT.Tanh)
 
         make_identity(nc, ident[:])
         for i in range(NT):
@@ -110,10 +107,12 @@ def tile_picked_yivf_cal_p_kernel(tc, x_words, x_scales, hT, e_words, e_scales, 
                 ysb[unit] = yc[:, n, :]
 
         sums = {i: keep.tile([P, S], F32, name=f"sum{i}", align_bytes=64) for i in range(1, NT)}
-        scaled = {i: keep.tile([P, S], F32, name=f"scaled{i}", align_bytes=64) for i in range(1, NT)}
+        scaled = {i: keep.tile([P, S], F32, name=f"scaled{i}", align_bytes=64) for i in range(2, NT)}
 
-        def look_up(i, d):
-            nc.vector.tensor_tensor(sums[i][:, halves[d]], z[i][:].indirect(cell_t[:, lists[d]]), ysb[i, d], ALU.add)
+        def look_up(i, d, part=slice(0, H)):
+            cols = slice(H * d + part.start, H * d + part.stop)
+            entries = cell_t[:, cols.start // 16 : cols.stop // 16]
+            nc.vector.tensor_tensor(sums[i][:, cols], z[i][:].indirect(entries), ysb[i, d][:, part], ALU.add)
 
         def scale(i, cols):
             nc.vector.tensor_tensor(scaled[i][:, cols], sums[i][:, cols], gb[:, cols], ALU.mult)
@@ -167,6 +166,9 @@ def tile_picked_yivf_cal_p_kernel(tc, x_words, x_scales, hT, e_words, e_scales, 
         look_up(1, 0)
         look_up(1, 1)
 
+        gb = psum.tile([P, S], F32, name="gb", tag="b4")
+        for c in range(NT):
+            nc.tensor.transpose(gb[:, chunks[c]], gcol[:, c : c + 1].to_broadcast([P, P]), ident[:])
         yT_ps = psum.tile([P, NT, P], F32, name="yT_ps", tag="b6")
         for c in range(NT):
             nc.tensor.matmul_mx(out=yT_ps[:, c, :], lhsT=xg[:, chunks[c]].bitcast(FP8X4), lhsT_scale=xsg[4:P, chunks[c]],
@@ -174,31 +176,34 @@ def tile_picked_yivf_cal_p_kernel(tc, x_words, x_scales, hT, e_words, e_scales, 
         zTb = psum.tile([P, 2, P], F32, name="zTb", tag="b3")
         for c in range(2):
             nc.tensor.transpose(zTb[:, c, :], zg0b[:, chunks[c]], ident[:])
-        gb = psum.tile([P, S], F32, name="gb", tag="b5")
-        for c in range(NT):
-            nc.tensor.transpose(gb[:, chunks[c]], gcol[:, c : c + 1].to_broadcast([P, P]), ident[:])
         cell_scores(3, "b1")
         scores([(3, 0), (3, 1)], "b7")
         for c in range(2):
             nc.scalar.activation(u0[:, chunks[2 + c]], zTb[:, c, :], ACT.Copy, scale=gcol[:, 2 + c : 3 + c])
         for c in range(NT):
             nc.scalar.activation(v0[:, chunks[c]], yT_ps[:, c, :], ACT.Copy, scale=gcol[:, c : c + 1])
-        back = psum.tile([P, S], F32, name="back", tag="b4")
+        back = psum.tile([P, S], F32, name="back", tag="b5")
         for c in range(NT):
             nc.tensor.matmul(back[:, chunks[c]], u0[:, chunks[c]], ident[:], start=True, stop=False, is_transpose=True)
             nc.tensor.matmul(back[:, chunks[c]], v0[:, chunks[c]], ident[:], start=False, stop=True, is_transpose=True)
 
+        scaled[1] = keep.tile([P, S], F32, name="scaled1", align_bytes=64)
         look_up(2, 0)
-        scale(1, whole)
+        scale(1, halves[0])
         look_up(2, 1)
+        scale(1, halves[1])
         squash(1, whole)
+        scale(2, halves[0])
         look_up(3, 0)
         nc.scalar.activation(res[0][:], back[:], ACT.Tanh)
         nc.sync.dma_start(out[0:P, :], res[0][:])
-        scale(2, whole)
-        look_up(3, 1)
+        scale(2, halves[1])
+        look_up(3, 1, chunks[0])
         squash(2, whole)
-        for d in range(2):
-            scale(3, halves[d])
-        for d in range(2):
-            squash(3, halves[d])
+        scale(3, halves[0])
+        look_up(3, 1, chunks[1])
+        squash(3, halves[0])
+        for c in range(2, NT):
+            scale(3, chunks[c])
+        for c in range(2, NT):
+            squash(3, chunks[c])

@@ -25,22 +25,25 @@ def tile_picked_yivf_cal_p_kernel(tc, x_words, x_scales, hT, e_words, e_scales, 
     nc = tc.nc
     with ExitStack() as ctx:
         keep = ctx.enter_context(tc.tile_pool(name="keep", bufs=1))
+        lay = ctx.enter_context(tc.tile_pool(name="lay", bufs=1))
         psum = ctx.enter_context(tc.psum_pool(name="psum", bufs=1))
 
         offs_t = keep.tile([P, S // 16], U16, name="offs_t")
         cent_t = keep.tile([P, R // 16], U16, name="cent_t")
         cell_t = keep.tile([P, S // 16], U16, name="cell_t")
         xw = keep.tile([P, T], I32, name="xw", tag="xw", align_bytes=64)
-        xs = keep.tile([P, T], U8, name="xs", align_bytes=64)
+        xs = keep.tile([P, T], U8, name="xs", tag="xs", align_bytes=64)
         ew = keep.tile([P, W], I32, name="ew", align_bytes=64)
         es = keep.tile([P, W], U8, name="es", align_bytes=64)
         gwin = keep.tile([P, T], F32, name="gwin", align_bytes=64)
         h0 = keep.tile([P, 4, P], F32, name="h0", tag="h0", align_bytes=64)
-        h12 = keep.tile([P, 4, H], F32, name="h12", tag="h12", align_bytes=64)
+        h1 = keep.tile([P, 4, P], F32, name="h1", align_bytes=64)
+        h2 = lay.tile([P, 4, P], F32, name="h2", align_bytes=64, offset=1024)
         h3 = keep.tile([P, 4, P], F32, name="h3", align_bytes=64)
-        hraw = [h0[:], h12[:, :, 0:P], h12[:, :, P:H], h3[:]]
-        hb = [keep.tile([P, P, 4], BF16, name=f"hb{i}", tag=f"hb{i}", align_bytes=64) for i in range(NT)]
-        hq = [keep.tile([P, P], U32, name=f"hq{i}", tag=f"hq{i}", align_bytes=64) for i in range(NT)]
+        hraw = [h0[:], h1[:], h2[:], h3[:]]
+        hb = [keep.tile([P, P, 4], BF16, name=f"hb{i}", tag=f"hb{i}", align_bytes=64) for i in range(2)]
+        hb.append(lay.tile([P, P, 4], BF16, name="hb2", align_bytes=64, offset=6144))
+        hq = {i: keep.tile([P, P], U32, name=f"hq{i}", align_bytes=64) for i in range(NT)}
         hs = [keep.tile([P, P], U8, name=f"hs{i}", align_bytes=64) for i in range(NT)]
         xg = keep.tile([P, S], U32, name="xg", align_bytes=64)
         eg = keep.tile([P, R], U32, name="eg", align_bytes=64)
@@ -61,13 +64,14 @@ def tile_picked_yivf_cal_p_kernel(tc, x_words, x_scales, hT, e_words, e_scales, 
         nc.sync.dma_start(cent_t[:], cent)
         for q in range(4):
             nc.sync.dma_start(es[32 * q : 32 * q + 4, :].bitcast(I32), e_scales[0, 4 * q : 4 * q + 4, :].bitcast(I32))
-        nc.sync.dma_start(ew[:], e_words[0].rearrange("p n t -> p (n t)").bitcast(I32))
         nc.sync.dma_start(h0[:], h_rows[:, :, 0:P])
+        nc.sync.dma_start(ew[:], e_words[0].rearrange("p n t -> p (n t)").bitcast(I32))
         for q in range(4):
             nc.sync.dma_start(xs[32 * q + 4 : 32 * q + 4 + 4, :].bitcast(I32), x_scales[0, 4 * q : 4 * q + 4, :].bitcast(I32))
         nc.sync.dma_start(cell_t[:], cell)
-        nc.sync.dma_start(h12[:], h_rows[:, :, P : 3 * P])
+        nc.sync.dma_start(h1[:], h_rows[:, :, P : 2 * P])
         nc.sync.dma_start(xw[:], x_words[0].rearrange("p n t -> p (n t)").bitcast(I32))
+        nc.sync.dma_start(h2[:], h_rows[:, :, 2 * P : 3 * P])
         nc.sync.dma_start(h3[:], h_rows[:, :, 3 * P : 4 * P])
 
         make_identity(nc, ident[:])
@@ -96,17 +100,21 @@ def tile_picked_yivf_cal_p_kernel(tc, x_words, x_scales, hT, e_words, e_scales, 
 
         ysb = {}
 
-        def scores(units, tag):
+        def scores(units, tag, reuse=None):
             yp = psum.tile([P, len(units), H], F32, name="yp", tag=tag)
             for n, (i, d) in enumerate(units):
                 nc.tensor.matmul_mx(out=yp[:, n, :], lhsT=hq[i][:].bitcast(FP8X4), lhsT_scale=hs[i][:],
                                     rhs=xg[:, halves[d]].bitcast(FP8X4), rhs_scale=xsg[4:P, halves[d]], start=True, stop=True)
-            yc = keep.tile([P, len(units), H], F32, name="yc%d%d" % units[0], align_bytes=64)
+            name = "yc%d%d" % units[0]
+            if reuse:
+                yc = lay.tile([P, len(units), H], F32, name=name, align_bytes=64, offset=1536)
+            else:
+                yc = keep.tile([P, len(units), H], F32, name=name, align_bytes=64)
             nc.scalar.copy(yc[:], yp[:])
             for n, unit in enumerate(units):
                 ysb[unit] = yc[:, n, :]
 
-        sums = {i: keep.tile([P, S], F32, name=f"sum{i}", align_bytes=64) for i in range(1, NT)}
+        sums = {}
         scaled = {i: keep.tile([P, S], F32, name=f"scaled{i}", align_bytes=64) for i in range(2, NT)}
 
         def look_up(i, d, part=slice(0, H)):
@@ -125,11 +133,11 @@ def tile_picked_yivf_cal_p_kernel(tc, x_words, x_scales, hT, e_words, e_scales, 
 
         nc.vector.tensor_copy(gg[:], gwin[:].indirect(offs_t[:]))
         nc.vector.tensor_copy(esg[:], es[:].indirect(cent_t[:]))
-        nc.vector.tensor_copy(eg[:], ew[:].bitcast(U32).indirect(cent_t[:]))
         interleave(0)
         quantize(0)
+        nc.vector.tensor_copy(eg[:], ew[:].bitcast(U32).indirect(cent_t[:]))
         cell_scores(0, "b0")
-        xsg = keep.tile([P, S], U8, name="xsg", tag="hb0", align_bytes=64)
+        xsg = keep.tile([P, S], U8, name="xsg", align_bytes=64)
         nc.vector.tensor_copy(xsg[:], xs[:].indirect(offs_t[:]))
 
         gT = psum.tile([P, NT, P], F32, name="gT", tag="b1")
@@ -139,37 +147,41 @@ def tile_picked_yivf_cal_p_kernel(tc, x_words, x_scales, hT, e_words, e_scales, 
         nc.scalar.copy(gcol[:], gT[:, :, P - 1])
 
         interleave(1)
-        interleave(2)
-        zg0a = keep.tile([P, H], F32, name="zg0a", align_bytes=64)
-        nc.vector.tensor_copy(zg0a[:], z[0][:].indirect(cell_t[:, lists[0]]))
         quantize(1)
+        zg0a = keep.tile([P, H], F32, name="zg0a", tag="hb1", align_bytes=64)
+        nc.vector.tensor_copy(zg0a[:], z[0][:].indirect(cell_t[:, lists[0]]))
         cell_scores(1, "b1")
-        quantize(2)
-        u0 = keep.tile([P, S], F32, name="u0", tag="h12", align_bytes=64)
         zTa = psum.tile([P, 2, P], F32, name="zTa", tag="b2")
         for c in range(2):
             nc.tensor.transpose(zTa[:, c, :], zg0a[:, chunks[c]], ident[:])
-        for c in range(2):
-            nc.scalar.activation(u0[:, chunks[c]], zTa[:, c, :], ACT.Copy, scale=gcol[:, c : c + 1])
-        cell_scores(2, "b0")
 
         for d in range(2):
             nc.vector.tensor_copy(xg[:, halves[d]], xw[:].bitcast(U32).indirect(offs_t[:, lists[d]]))
-        zg0b = keep.tile([P, H], F32, name="zg0b", tag="xw", align_bytes=64)
-        nc.vector.tensor_copy(zg0b[:], z[0][:].indirect(cell_t[:, lists[1]]))
 
-        scores([(1, 0)], "b3")
+        interleave(2)
+        scores([(1, 0)], "b3", "h2")
         scores([(1, 1)], "b4")
+        u0 = lay.tile([P, S], F32, name="u0", align_bytes=64, offset=2560)
+        for c in range(2):
+            nc.scalar.activation(u0[:, chunks[c]], zTa[:, c, :], ACT.Copy, scale=gcol[:, c : c + 1])
+        quantize(2)
+        zg0b = lay.tile([P, H], F32, name="zg0b", align_bytes=64, offset=5632)
+        nc.vector.tensor_copy(zg0b[:], z[0][:].indirect(cell_t[:, lists[1]]))
+        cell_scores(2, "b0")
         scores([(2, 0), (2, 1)], "b5")
+        hb.append(lay.tile([P, P, 4], BF16, name="hb3", align_bytes=64, offset=512))
         interleave(3)
-        quantize(3)
+        sums[1] = lay.tile([P, S], F32, name="sum1", align_bytes=64, offset=6656)
         look_up(1, 0)
+        quantize(3)
+        sums[2] = keep.tile([P, S], F32, name="sum2", align_bytes=64)
+        sums[3] = keep.tile([P, S], F32, name="sum3", align_bytes=64)
         look_up(1, 1)
 
-        gb = psum.tile([P, S], F32, name="gb", tag="b4")
+        gb = psum.tile([P, S], F32, name="gb", tag="b5")
         for c in range(NT):
             nc.tensor.transpose(gb[:, chunks[c]], gcol[:, c : c + 1].to_broadcast([P, P]), ident[:])
-        yT_ps = psum.tile([P, NT, P], F32, name="yT_ps", tag="b6")
+        yT_ps = psum.tile([P, NT, P], F32, name="yT_ps", tag="b0")
         for c in range(NT):
             nc.tensor.matmul_mx(out=yT_ps[:, c, :], lhsT=xg[:, chunks[c]].bitcast(FP8X4), lhsT_scale=xsg[4:P, chunks[c]],
                                 rhs=hq[0][:].bitcast(FP8X4), rhs_scale=hs[0][:], start=True, stop=True)
@@ -182,7 +194,7 @@ def tile_picked_yivf_cal_p_kernel(tc, x_words, x_scales, hT, e_words, e_scales, 
             nc.scalar.activation(u0[:, chunks[2 + c]], zTb[:, c, :], ACT.Copy, scale=gcol[:, 2 + c : 3 + c])
         for c in range(NT):
             nc.scalar.activation(v0[:, chunks[c]], yT_ps[:, c, :], ACT.Copy, scale=gcol[:, c : c + 1])
-        back = psum.tile([P, S], F32, name="back", tag="b5")
+        back = psum.tile([P, S], F32, name="back", tag="b4")
         for c in range(NT):
             nc.tensor.matmul(back[:, chunks[c]], u0[:, chunks[c]], ident[:], start=True, stop=False, is_transpose=True)
             nc.tensor.matmul(back[:, chunks[c]], v0[:, chunks[c]], ident[:], start=False, stop=True, is_transpose=True)

@@ -37,12 +37,12 @@ def tile_picked_yivf_cal_p_kernel(tc, x_words, x_scales, hT, e_words, e_scales, 
         es = keep.tile([P, W], U8, name="es", align_bytes=64)
         gwin = keep.tile([P, T], F32, name="gwin", align_bytes=64)
         h0 = keep.tile([P, 4, P], F32, name="h0", tag="h0", align_bytes=64)
-        h1 = keep.tile([P, 4, P], F32, name="h1", align_bytes=64)
-        h2 = lay.tile([P, 4, P], F32, name="h2", align_bytes=64, offset=1024)
+        h1 = keep.tile([P, 4, P], F32, name="h1", tag="h1", align_bytes=64)
+        h2 = lay.tile([P, 4, P], F32, name="h2", align_bytes=64, offset=3008)
         h3 = keep.tile([P, 4, P], F32, name="h3", align_bytes=64)
         hraw = [h0[:], h1[:], h2[:], h3[:]]
         hb = [keep.tile([P, P, 4], BF16, name=f"hb{i}", tag=f"hb{i}", align_bytes=64) for i in range(2)]
-        hb.append(lay.tile([P, P, 4], BF16, name="hb2", align_bytes=64, offset=6144))
+        hb.append(keep.tile([P, P, 4], BF16, name="hb2", tag="hb2", align_bytes=64))
         hq = {i: keep.tile([P, P], U32, name=f"hq{i}", align_bytes=64) for i in range(NT)}
         hs = [keep.tile([P, P], U8, name=f"hs{i}", align_bytes=64) for i in range(NT)]
         xg = keep.tile([P, S], U32, name="xg", align_bytes=64)
@@ -84,10 +84,11 @@ def tile_picked_yivf_cal_p_kernel(tc, x_words, x_scales, hT, e_words, e_scales, 
 
         def interleave(i):
             turned = hraw[i].rearrange("p j t -> p t j")
-            if i % 2:
-                nc.gpsimd.tensor_scalar(hb[i][:], turned, 1.0, 0.0, ALU.mult, ALU.add)
-            else:
-                nc.scalar.copy(hb[i][:], turned)
+            cut = (P, 0, 80, 0)[i]
+            if cut < P:
+                nc.gpsimd.tensor_scalar(hb[i][:, cut:, :], turned[:, cut:, :], 1.0, 0.0, ALU.mult, ALU.add)
+            if cut > 0:
+                nc.scalar.copy(hb[i][:, :cut, :], turned[:, :cut, :])
 
         def quantize(i):
             nc.vector.quantize_mx(out=hq[i][:].bitcast(FP8X4), scales=hs[i][:], in_=hb[i][:].rearrange("p t j -> p (t j)"))
@@ -106,11 +107,11 @@ def tile_picked_yivf_cal_p_kernel(tc, x_words, x_scales, hT, e_words, e_scales, 
                 nc.tensor.matmul_mx(out=yp[:, n, :], lhsT=hq[i][:].bitcast(FP8X4), lhsT_scale=hs[i][:],
                                     rhs=xg[:, halves[d]].bitcast(FP8X4), rhs_scale=xsg[4:P, halves[d]], start=True, stop=True)
             name = "yc%d%d" % units[0]
-            if reuse:
-                yc = lay.tile([P, len(units), H], F32, name=name, align_bytes=64, offset=1536)
+            if reuse is not None:
+                yc = reuse
             else:
                 yc = keep.tile([P, len(units), H], F32, name=name, align_bytes=64)
-            nc.scalar.copy(yc[:], yp[:])
+            nc.scalar.copy(yc[:, 0 : len(units), :], yp[:])
             for n, unit in enumerate(units):
                 ysb[unit] = yc[:, n, :]
 
@@ -145,73 +146,74 @@ def tile_picked_yivf_cal_p_kernel(tc, x_words, x_scales, hT, e_words, e_scales, 
             nc.tensor.transpose(gT[:, c, :], gg[:, chunks[c]], ident[:])
         gcol = keep.tile([P, NT], F32, name="gcol", tag="h0", align_bytes=64)
         nc.scalar.copy(gcol[:], gT[:, :, P - 1])
+        gb = psum.tile([P, S], F32, name="gb", tag="b6")
+        for c in range(NT):
+            nc.tensor.transpose(gb[:, chunks[c]], gcol[:, c : c + 1].to_broadcast([P, P]), ident[:])
 
         interleave(1)
         quantize(1)
-        zg0a = keep.tile([P, H], F32, name="zg0a", tag="hb1", align_bytes=64)
-        nc.vector.tensor_copy(zg0a[:], z[0][:].indirect(cell_t[:, lists[0]]))
+        zg0a = keep.tile([P, P], F32, name="zg0a", tag="h1", align_bytes=64)
+        nc.vector.tensor_copy(zg0a[:], z[0][:].indirect(cell_t[:, 0:8]))
         cell_scores(1, "b1")
-        zTa = psum.tile([P, 2, P], F32, name="zTa", tag="b2")
-        for c in range(2):
-            nc.tensor.transpose(zTa[:, c, :], zg0a[:, chunks[c]], ident[:])
+        zTa = psum.tile([P, P], F32, name="zTa", tag="b2")
+        nc.tensor.transpose(zTa[:], zg0a[:], ident[:])
 
         for d in range(2):
             nc.vector.tensor_copy(xg[:, halves[d]], xw[:].bitcast(U32).indirect(offs_t[:, lists[d]]))
 
         interleave(2)
-        scores([(1, 0)], "b3", "h2")
+        pair = lay.tile([P, 3, H], F32, name="pair", align_bytes=64, offset=0)
+        scores([(1, 0)], "b3", pair)
         scores([(1, 1)], "b4")
-        u0 = lay.tile([P, S], F32, name="u0", align_bytes=64, offset=2560)
-        for c in range(2):
-            nc.scalar.activation(u0[:, chunks[c]], zTa[:, c, :], ACT.Copy, scale=gcol[:, c : c + 1])
+        u0 = lay.tile([P, S], F32, name="u0", align_bytes=64, offset=4992)
+        nc.scalar.activation(u0[:, chunks[0]], zTa[:], ACT.Copy, scale=gcol[:, 0:1])
         quantize(2)
-        zg0b = lay.tile([P, H], F32, name="zg0b", align_bytes=64, offset=5632)
-        nc.vector.tensor_copy(zg0b[:], z[0][:].indirect(cell_t[:, lists[1]]))
+        zg0b = pair[:].rearrange("p a b -> p (a b)")[:, H:]
+        nc.vector.tensor_copy(zg0b[:, chunks[0]], z[0][:].indirect(cell_t[:, 8:16]))
+        nc.vector.tensor_copy(zg0b[:, P : P + H], z[0][:].indirect(cell_t[:, lists[1]]))
         cell_scores(2, "b0")
         scores([(2, 0), (2, 1)], "b5")
-        hb.append(lay.tile([P, P, 4], BF16, name="hb3", align_bytes=64, offset=512))
+        hb.append(lay.tile([P, P, 4], BF16, name="hb3", align_bytes=64, offset=3072))
         interleave(3)
-        sums[1] = lay.tile([P, S], F32, name="sum1", align_bytes=64, offset=6656)
+        sums[1] = keep.tile([P, S], F32, name="sum1", tag="hb2", align_bytes=64)
         look_up(1, 0)
         quantize(3)
         sums[2] = keep.tile([P, S], F32, name="sum2", align_bytes=64)
         sums[3] = keep.tile([P, S], F32, name="sum3", align_bytes=64)
         look_up(1, 1)
 
-        gb = psum.tile([P, S], F32, name="gb", tag="b5")
-        for c in range(NT):
-            nc.tensor.transpose(gb[:, chunks[c]], gcol[:, c : c + 1].to_broadcast([P, P]), ident[:])
         yT_ps = psum.tile([P, NT, P], F32, name="yT_ps", tag="b0")
         for c in range(NT):
             nc.tensor.matmul_mx(out=yT_ps[:, c, :], lhsT=xg[:, chunks[c]].bitcast(FP8X4), lhsT_scale=xsg[4:P, chunks[c]],
                                 rhs=hq[0][:].bitcast(FP8X4), rhs_scale=hs[0][:], start=True, stop=True)
-        zTb = psum.tile([P, 2, P], F32, name="zTb", tag="b3")
-        for c in range(2):
+        zTb = psum.tile([P, 3, P], F32, name="zTb", tag="b3")
+        for c in range(3):
             nc.tensor.transpose(zTb[:, c, :], zg0b[:, chunks[c]], ident[:])
-        cell_scores(3, "b1")
-        scores([(3, 0), (3, 1)], "b7")
-        for c in range(2):
-            nc.scalar.activation(u0[:, chunks[2 + c]], zTb[:, c, :], ACT.Copy, scale=gcol[:, 2 + c : 3 + c])
+        for c in range(3):
+            nc.scalar.activation(u0[:, chunks[1 + c]], zTb[:, c, :], ACT.Copy, scale=gcol[:, 1 + c : 2 + c])
         for c in range(NT):
             nc.scalar.activation(v0[:, chunks[c]], yT_ps[:, c, :], ACT.Copy, scale=gcol[:, c : c + 1])
+        cell_scores(3, "b1")
+        scores([(3, 0)], "b7")
+        scores([(3, 1)], "b2")
         back = psum.tile([P, S], F32, name="back", tag="b4")
         for c in range(NT):
             nc.tensor.matmul(back[:, chunks[c]], u0[:, chunks[c]], ident[:], start=True, stop=False, is_transpose=True)
             nc.tensor.matmul(back[:, chunks[c]], v0[:, chunks[c]], ident[:], start=False, stop=True, is_transpose=True)
 
         scaled[1] = keep.tile([P, S], F32, name="scaled1", align_bytes=64)
-        look_up(2, 0)
-        scale(1, halves[0])
-        look_up(2, 1)
-        scale(1, halves[1])
+        for d in range(2):
+            scale(1, halves[d])
         squash(1, whole)
-        scale(2, halves[0])
-        look_up(3, 0)
         nc.scalar.activation(res[0][:], back[:], ACT.Tanh)
         nc.sync.dma_start(out[0:P, :], res[0][:])
-        scale(2, halves[1])
-        look_up(3, 1, chunks[0])
+        for d in range(2):
+            look_up(2, d)
+        for d in range(2):
+            scale(2, halves[d])
         squash(2, whole)
+        look_up(3, 0)
+        look_up(3, 1, chunks[0])
         scale(3, halves[0])
         look_up(3, 1, chunks[1])
         squash(3, halves[0])

@@ -31,64 +31,63 @@ def tile_picked_yivf_cal_p_kernel(tc, x_words, x_scales, hT, e_words, e_scales, 
         offs_t = keep.tile([P, S // 16], U16, name="offs_t")
         cent_t = keep.tile([P, R // 16], U16, name="cent_t")
         cell_t = keep.tile([P, S // 16], U16, name="cell_t")
-        xw = keep.tile([P, T], I32, name="xw", tag="xw", align_bytes=64)
-        xs = keep.tile([P, T], U8, name="xs", tag="xs", align_bytes=64)
+        xw = keep.tile([P, T], I32, name="xw", align_bytes=64)
+        xs = lay.tile([P, T], U8, name="xs", align_bytes=64, offset=0)
         ew = keep.tile([P, W], I32, name="ew", align_bytes=64)
         es = keep.tile([P, W], U8, name="es", align_bytes=64)
         gwin = keep.tile([P, T], F32, name="gwin", align_bytes=64)
-        h0 = keep.tile([P, 4, P], F32, name="h0", tag="h0", align_bytes=64)
-        h1 = keep.tile([P, 4, P], F32, name="h1", tag="h1", align_bytes=64)
-        h2 = lay.tile([P, 4, P], F32, name="h2", align_bytes=64, offset=3008)
-        h3 = keep.tile([P, 4, P], F32, name="h3", align_bytes=64)
-        hraw = [h0[:], h1[:], h2[:], h3[:]]
-        hb = [keep.tile([P, P, 4], BF16, name=f"hb{i}", tag=f"hb{i}", align_bytes=64) for i in range(2)]
-        hb.append(keep.tile([P, P, 4], BF16, name="hb2", tag="hb2", align_bytes=64))
-        hq = {i: keep.tile([P, P], U32, name=f"hq{i}", align_bytes=64) for i in range(NT)}
+        hpair = [keep.tile([P, 4, 2 * P], F32, name=f"hpair{u}", tag=f"hpair{u}", align_bytes=64) for u in range(2)]
+        hsrc = [hpair[i // 2][:, :, P * (i % 2) : P * (i % 2 + 1)] for i in range(NT)]
+        hb = [keep.tile([P, P, 4], BF16, name=f"hb{i}", align_bytes=64) for i in range(NT)]
+        hq = [keep.tile([P, P], U32, name=f"hq{i}", align_bytes=64) for i in range(NT)]
         hs = [keep.tile([P, P], U8, name=f"hs{i}", align_bytes=64) for i in range(NT)]
-        xg = keep.tile([P, S], U32, name="xg", align_bytes=64)
+        xg = [keep.tile([P, H], U32, name=f"xg{d}", align_bytes=64) for d in range(2)]
+        xsg = [keep.tile([P, H], U8, name=f"xsg{d}", align_bytes=64) for d in range(2)]
         eg = keep.tile([P, R], U32, name="eg", align_bytes=64)
         esg = keep.tile([P, R], U8, name="esg", align_bytes=64)
         gg = keep.tile([P, S], F32, name="gg", align_bytes=64)
+        gcol = keep.tile([P, NT], F32, name="gcol", align_bytes=64)
         ident = keep.tile([P, P], F32, name="ident", align_bytes=64)
-        z = [keep.tile([P, ZW], F32, name=f"z{i}", align_bytes=64) for i in range(NT)]
-        v0 = keep.tile([P, S], F32, name="v0", align_bytes=64)
-        res = [keep.tile([P, S], F32, name=f"res{i}", align_bytes=64) for i in range(NT)]
+        zw = [ZW, ZW, S + 16, S + 16]
+        z = [keep.tile([P, zw[i]], F32, name=f"z{i}", align_bytes=64) for i in range(NT)]
+        zg = {i: keep.tile([P, S], F32, name=f"zg{i}", align_bytes=64) for i in range(1, NT)}
+        sums = [keep.tile([P, 2, H], F32, name=f"sum{u}", align_bytes=64) for u in range(NT)]
+        scaled = [keep.tile([P, 2, H], F32, name=f"scaled{u}", align_bytes=64) for u in range(NT)]
+        res = [keep.tile([P, 2, H], F32, name=f"res{u}", align_bytes=64) for u in range(NT)]
 
+        nc.gpsimd.memset(xs[:].bitcast(I32), 0)
+        nc.gpsimd.memset(z[3][:, R:], 0.0)
+        for i in range(NT - 1):
+            nc.scalar.copy(z[i][:, R:], z[3][:, R : zw[i]])
         nc.vector.memset(es[:].bitcast(I32), 0)
         nc.vector.memset(gwin[0 : P - 1, :], 0.0)
-        nc.gpsimd.memset(xs[:].bitcast(I32), 0)
 
         h_rows = hT.rearrange("(p j) t -> p j t", j=4)
-        nc.sync.dma_start(offs_t[:], offs)
-        nc.sync.dma_start(gwin[P - 1 : P, :], gain[0:1, :])
         nc.sync.dma_start(cent_t[:], cent)
+        nc.sync.dma_start(hpair[0][:], h_rows[:, :, 0 : 2 * P])
         for q in range(4):
             nc.sync.dma_start(es[32 * q : 32 * q + 4, :].bitcast(I32), e_scales[0, 4 * q : 4 * q + 4, :].bitcast(I32))
-        nc.sync.dma_start(h0[:], h_rows[:, :, 0:P])
+        nc.sync.dma_start(gwin[P - 1 : P, :], gain[0:1, :])
         nc.sync.dma_start(ew[:], e_words[0].rearrange("p n t -> p (n t)").bitcast(I32))
+        nc.sync.dma_start(offs_t[:], offs)
+        nc.sync.dma_start(cell_t[:], cell)
         for q in range(4):
             nc.sync.dma_start(xs[32 * q + 4 : 32 * q + 4 + 4, :].bitcast(I32), x_scales[0, 4 * q : 4 * q + 4, :].bitcast(I32))
-        nc.sync.dma_start(cell_t[:], cell)
-        nc.sync.dma_start(h1[:], h_rows[:, :, P : 2 * P])
+        nc.sync.dma_start(hpair[1][:], h_rows[:, :, 2 * P : 4 * P])
         nc.sync.dma_start(xw[:], x_words[0].rearrange("p n t -> p (n t)").bitcast(I32))
-        nc.sync.dma_start(h2[:], h_rows[:, :, 2 * P : 3 * P])
-        nc.sync.dma_start(h3[:], h_rows[:, :, 3 * P : 4 * P])
 
         make_identity(nc, ident[:])
-        for i in range(NT):
-            nc.gpsimd.memset(z[i][:, R:], 0.0)
 
         halves = [slice(0, H), slice(H, S)]
         chunks = [slice(P * c, P * (c + 1)) for c in range(NT)]
         lists = [slice(0, H // 16), slice(H // 16, S // 16)]
 
-        def interleave(i):
-            turned = hraw[i].rearrange("p j t -> p t j")
-            cut = (P, 0, 80, 0)[i]
-            if cut < P:
-                nc.gpsimd.tensor_scalar(hb[i][:, cut:, :], turned[:, cut:, :], 1.0, 0.0, ALU.mult, ALU.add)
+        def interleave(i, cut):
+            turned = hsrc[i].rearrange("p j t -> p t j")
             if cut > 0:
                 nc.scalar.copy(hb[i][:, :cut, :], turned[:, :cut, :])
+            if cut < P:
+                nc.gpsimd.tensor_scalar(hb[i][:, cut:, :], turned[:, cut:, :], 1.0, 0.0, ALU.mult, ALU.add)
 
         def quantize(i):
             nc.vector.quantize_mx(out=hq[i][:].bitcast(FP8X4), scales=hs[i][:], in_=hb[i][:].rearrange("p t j -> p (t j)"))
@@ -99,125 +98,83 @@ def tile_picked_yivf_cal_p_kernel(tc, x_words, x_scales, hT, e_words, e_scales, 
                                 rhs=eg[:].bitcast(FP8X4), rhs_scale=esg[:], start=True, stop=True)
             nc.scalar.copy(z[i][:, 0:R], zp[:])
 
-        ysb = {}
+        units = [[(0, 0), (1, 0)], [(0, 1), (1, 1)], [(2, 0), (2, 1)], [(3, 0), (3, 1)]]
 
-        def scores(units, tag, reuse=None):
-            yp = psum.tile([P, len(units), H], F32, name="yp", tag=tag)
-            for n, (i, d) in enumerate(units):
-                nc.tensor.matmul_mx(out=yp[:, n, :], lhsT=hq[i][:].bitcast(FP8X4), lhsT_scale=hs[i][:],
-                                    rhs=xg[:, halves[d]].bitcast(FP8X4), rhs_scale=xsg[4:P, halves[d]], start=True, stop=True)
-            name = "yc%d%d" % units[0]
-            if reuse is not None:
-                yc = reuse
+        def look_up(i, d, on_vector):
+            if on_vector:
+                nc.vector.tensor_copy(zg[i][:, halves[d]], z[i][:].indirect(cell_t[:, lists[d]]))
             else:
-                yc = keep.tile([P, len(units), H], F32, name=name, align_bytes=64)
-            nc.scalar.copy(yc[:, 0 : len(units), :], yp[:])
-            for n, unit in enumerate(units):
-                ysb[unit] = yc[:, n, :]
+                nc.scalar.activation(zg[i][:, halves[d]], z[i][:].indirect(cell_t[:, lists[d]]), ACT.Copy)
 
-        sums = {}
-        scaled = {i: keep.tile([P, S], F32, name=f"scaled{i}", align_bytes=64) for i in range(2, NT)}
+        yp = {}
 
-        def look_up(i, d, part=slice(0, H)):
-            cols = slice(H * d + part.start, H * d + part.stop)
-            entries = cell_t[:, cols.start // 16 : cols.stop // 16]
-            nc.vector.tensor_tensor(sums[i][:, cols], z[i][:].indirect(entries), ysb[i, d][:, part], ALU.add)
+        def scores(u, tag):
+            yp[u] = psum.tile([P, 2, H], F32, name="yp", tag=tag)
+            for n, (i, d) in enumerate(units[u]):
+                nc.tensor.matmul_mx(out=yp[u][:, n, :], lhsT=hq[i][:].bitcast(FP8X4), lhsT_scale=hs[i][:],
+                                    rhs=xg[d][:].bitcast(FP8X4), rhs_scale=xsg[d][4:P, :], start=True, stop=True)
 
-        def scale(i, cols):
-            nc.vector.tensor_tensor(scaled[i][:, cols], sums[i][:, cols], gb[:, cols], ALU.mult)
+        def add(u, n):
+            i, d = units[u][n]
+            nc.vector.tensor_tensor(sums[u][:, n, :], yp[u][:, n, :], zg[i][:, halves[d]], ALU.add)
 
-        def squash(i, cols):
-            nc.scalar.activation(res[i][:, cols], scaled[i][:, cols], ACT.Tanh)
-            nc.sync.dma_start(out[P * i : P * (i + 1), cols], res[i][:, cols])
-
-        whole = slice(0, S)
-
-        nc.vector.tensor_copy(gg[:], gwin[:].indirect(offs_t[:]))
         nc.vector.tensor_copy(esg[:], es[:].indirect(cent_t[:]))
-        interleave(0)
+        interleave(0, P)
+        interleave(1, 0)
         quantize(0)
+        quantize(1)
         nc.vector.tensor_copy(eg[:], ew[:].bitcast(U32).indirect(cent_t[:]))
-        cell_scores(0, "b0")
-        xsg = keep.tile([P, S], U8, name="xsg", align_bytes=64)
-        nc.vector.tensor_copy(xsg[:], xs[:].indirect(offs_t[:]))
-
-        gT = psum.tile([P, NT, P], F32, name="gT", tag="b1")
+        nc.scalar.activation(gg[:], gwin[:].indirect(offs_t[:]), ACT.Copy)
+        cell_scores(0, "b2")
+        cell_scores(1, "b3")
+        for d in range(2):
+            nc.vector.tensor_copy(xsg[d][:], xs[:].indirect(offs_t[:, lists[d]]))
+        zg[0] = lay.tile([P, S], F32, name="zg0", align_bytes=64, offset=0)
+        interleave(2, 0)
+        interleave(3, 0)
+        look_up(0, 0, True)
+        look_up(1, 0, False)
+        gT = psum.tile([P, NT, P], F32, name="gT", tag="b4")
         for c in range(NT):
             nc.tensor.transpose(gT[:, c, :], gg[:, chunks[c]], ident[:])
-        gcol = keep.tile([P, NT], F32, name="gcol", tag="h0", align_bytes=64)
         nc.scalar.copy(gcol[:], gT[:, :, P - 1])
-        gb = psum.tile([P, S], F32, name="gb", tag="b6")
+        gb = psum.tile([P, S], F32, name="gb", tag="b1")
         for c in range(NT):
             nc.tensor.transpose(gb[:, chunks[c]], gcol[:, c : c + 1].to_broadcast([P, P]), ident[:])
-
-        interleave(1)
-        quantize(1)
-        zg0a = keep.tile([P, P], F32, name="zg0a", tag="h1", align_bytes=64)
-        nc.vector.tensor_copy(zg0a[:], z[0][:].indirect(cell_t[:, 0:8]))
-        cell_scores(1, "b1")
-        zTa = psum.tile([P, P], F32, name="zTa", tag="b2")
-        nc.tensor.transpose(zTa[:], zg0a[:], ident[:])
-
-        for d in range(2):
-            nc.vector.tensor_copy(xg[:, halves[d]], xw[:].bitcast(U32).indirect(offs_t[:, lists[d]]))
-
-        interleave(2)
-        pair = lay.tile([P, 3, H], F32, name="pair", align_bytes=64, offset=0)
-        scores([(1, 0)], "b3", pair)
-        scores([(1, 1)], "b4")
-        u0 = lay.tile([P, S], F32, name="u0", align_bytes=64, offset=4992)
-        nc.scalar.activation(u0[:, chunks[0]], zTa[:], ACT.Copy, scale=gcol[:, 0:1])
         quantize(2)
-        zg0b = pair[:].rearrange("p a b -> p (a b)")[:, H:]
-        nc.vector.tensor_copy(zg0b[:, chunks[0]], z[0][:].indirect(cell_t[:, 8:16]))
-        nc.vector.tensor_copy(zg0b[:, P : P + H], z[0][:].indirect(cell_t[:, lists[1]]))
         cell_scores(2, "b0")
-        scores([(2, 0), (2, 1)], "b5")
-        hb.append(lay.tile([P, P, 4], BF16, name="hb3", align_bytes=64, offset=3072))
-        interleave(3)
-        sums[1] = keep.tile([P, S], F32, name="sum1", tag="hb2", align_bytes=64)
-        look_up(1, 0)
+        look_up(0, 1, True)
+        look_up(1, 1, False)
         quantize(3)
-        sums[2] = keep.tile([P, S], F32, name="sum2", align_bytes=64)
-        sums[3] = keep.tile([P, S], F32, name="sum3", align_bytes=64)
-        look_up(1, 1)
+        cell_scores(3, "b2")
+        gsb = keep.tile([P, H], F32, name="gsb", tag="hpair1", align_bytes=64)
+        nc.scalar.copy(gsb[:], gb[:, halves[0]])
+        for d in range(2):
+            nc.vector.tensor_copy(xg[d][:], xw[:].bitcast(U32).indirect(offs_t[:, lists[d]]))
+        for u in range(NT):
+            scores(u, f"b{4 + u}")
+        for i in range(2, NT):
+            nc.scalar.activation(zg[i][:], z[i][:].indirect(cell_t[:]), ACT.Copy)
 
-        yT_ps = psum.tile([P, NT, P], F32, name="yT_ps", tag="b0")
-        for c in range(NT):
-            nc.tensor.matmul_mx(out=yT_ps[:, c, :], lhsT=xg[:, chunks[c]].bitcast(FP8X4), lhsT_scale=xsg[4:P, chunks[c]],
-                                rhs=hq[0][:].bitcast(FP8X4), rhs_scale=hs[0][:], start=True, stop=True)
-        zTb = psum.tile([P, 3, P], F32, name="zTb", tag="b3")
-        for c in range(3):
-            nc.tensor.transpose(zTb[:, c, :], zg0b[:, chunks[c]], ident[:])
-        for c in range(3):
-            nc.scalar.activation(u0[:, chunks[1 + c]], zTb[:, c, :], ACT.Copy, scale=gcol[:, 1 + c : 2 + c])
-        for c in range(NT):
-            nc.scalar.activation(v0[:, chunks[c]], yT_ps[:, c, :], ACT.Copy, scale=gcol[:, c : c + 1])
-        cell_scores(3, "b1")
-        scores([(3, 0)], "b7")
-        scores([(3, 1)], "b2")
-        back = psum.tile([P, S], F32, name="back", tag="b4")
-        for c in range(NT):
-            nc.tensor.matmul(back[:, chunks[c]], u0[:, chunks[c]], ident[:], start=True, stop=False, is_transpose=True)
-            nc.tensor.matmul(back[:, chunks[c]], v0[:, chunks[c]], ident[:], start=False, stop=True, is_transpose=True)
-
-        scaled[1] = keep.tile([P, S], F32, name="scaled1", align_bytes=64)
+        out_rows = out.rearrange("(g p) s -> p g s", p=P)
+        for n in range(2):
+            add(0, n)
+            nc.gpsimd.tensor_tensor(scaled[0][:, n, :], sums[0][:, n, :], gsb[:], ALU.mult)
+        for n in range(2):
+            add(1, n)
+        nc.vector.tensor_tensor(sums[2][:].rearrange("p a b -> p (a b)"), yp[2][:].rearrange("p a b -> p (a b)"), zg[2][:], ALU.add)
+        nc.vector.tensor_tensor(scaled[1][:], sums[1][:], gb[:, halves[1]].unsqueeze(1).to_broadcast([P, 2, H]), ALU.mult)
+        nc.vector.tensor_tensor(scaled[2][:].rearrange("p a b -> p (a b)"), sums[2][:].rearrange("p a b -> p (a b)"), gb[:], ALU.mult)
+        for n in range(2):
+            add(3, n)
         for d in range(2):
-            scale(1, halves[d])
-        squash(1, whole)
-        nc.scalar.activation(res[0][:], back[:], ACT.Tanh)
-        nc.sync.dma_start(out[0:P, :], res[0][:])
+            nc.vector.tensor_tensor(scaled[3][:, d, :], sums[3][:, d, :], gb[:, halves[d]], ALU.mult)
+        for u in range(NT - 1):
+            nc.scalar.activation(res[u][:], scaled[u][:], ACT.Tanh)
+            if u < 2:
+                nc.sync.dma_start(out_rows[:, 0:2, halves[u]], res[u][:])
+            else:
+                nc.sync.dma_start(out_rows[:, u, :], res[u][:].rearrange("p a b -> p (a b)"))
         for d in range(2):
-            look_up(2, d)
-        for d in range(2):
-            scale(2, halves[d])
-        squash(2, whole)
-        look_up(3, 0)
-        look_up(3, 1, chunks[0])
-        scale(3, halves[0])
-        look_up(3, 1, chunks[1])
-        squash(3, halves[0])
-        for c in range(2, NT):
-            scale(3, chunks[c])
-        for c in range(2, NT):
-            squash(3, chunks[c])
+            nc.scalar.activation(res[3][:, d, :], scaled[3][:, d, :], ACT.Tanh)
+            nc.sync.dma_start(out_rows[:, 3, halves[d]], res[3][:, d, :])

@@ -34,12 +34,12 @@ def tile_picked_yivf_cal_p_kernel(tc, x_words, x_scales, hT, e_words, e_scales, 
         xw = keep.tile([P, T], I32, name="xw", align_bytes=64)
         xs = lay.tile([P, T], U8, name="xs", align_bytes=64, offset=0)
         ew = keep.tile([P, W], I32, name="ew", align_bytes=64)
-        es = keep.tile([P, W], U8, name="es", align_bytes=64)
+        es = lay.tile([P, W], U8, name="es", align_bytes=64, offset=2048)
         gwin = keep.tile([P, T], F32, name="gwin", align_bytes=64)
         hpair = [keep.tile([P, 4, 2 * P], F32, name=f"hpair{u}", tag=f"hpair{u}", align_bytes=64) for u in range(2)]
         hsrc = [hpair[i // 2][:, :, P * (i % 2) : P * (i % 2 + 1)] for i in range(NT)]
-        hb = [keep.tile([P, P, 4], BF16, name=f"hb{i}", align_bytes=64) for i in range(NT)]
-        hq = [keep.tile([P, P], U32, name=f"hq{i}", align_bytes=64) for i in range(NT)]
+        hb = [keep.tile([P, P, 4], BF16, name=f"hb{i}", tag=f"hb{i}", align_bytes=64) for i in range(NT)]
+        hq = {i: keep.tile([P, P], U32, name=f"hq{i}", align_bytes=64) for i in (2, 3)}
         hs = [keep.tile([P, P], U8, name=f"hs{i}", align_bytes=64) for i in range(NT)]
         xg = [keep.tile([P, H], U32, name=f"xg{d}", align_bytes=64) for d in range(2)]
         xsg = [keep.tile([P, H], U8, name=f"xsg{d}", align_bytes=64) for d in range(2)]
@@ -50,10 +50,14 @@ def tile_picked_yivf_cal_p_kernel(tc, x_words, x_scales, hT, e_words, e_scales, 
         ident = keep.tile([P, P], F32, name="ident", align_bytes=64)
         zw = [ZW, ZW, S + 16, S + 16]
         z = [keep.tile([P, zw[i]], F32, name=f"z{i}", align_bytes=64) for i in range(NT)]
-        zg = {i: keep.tile([P, S], F32, name=f"zg{i}", align_bytes=64) for i in range(1, NT)}
-        sums = [keep.tile([P, 2, H], F32, name=f"sum{u}", align_bytes=64) for u in range(NT)]
+        zg = {}
+        zrow = {i: keep.tile([P, S], F32, name=f"zg{i}", align_bytes=64) for i in range(1, NT)}
+        for i in range(1, NT):
+            for d in range(2):
+                zg[i, d] = zrow[i][:, H * d : H * (d + 1)]
+        sums = [keep.tile([P, 2, H], F32, name=f"sum{u}", tag=f"sum{u}", align_bytes=64) for u in range(NT)]
         scaled = [keep.tile([P, 2, H], F32, name=f"scaled{u}", align_bytes=64) for u in range(NT)]
-        res = [keep.tile([P, 2, H], F32, name=f"res{u}", align_bytes=64) for u in range(NT)]
+        res = {(u, n): keep.tile([P, H], F32, name=f"res{u}{n}", align_bytes=64) for u in range(NT) for n in range(2) if (u, n) != (3, 0)}
 
         nc.gpsimd.memset(xs[:].bitcast(I32), 0)
         nc.gpsimd.memset(z[3][:, R:], 0.0)
@@ -102,9 +106,9 @@ def tile_picked_yivf_cal_p_kernel(tc, x_words, x_scales, hT, e_words, e_scales, 
 
         def look_up(i, d, on_vector):
             if on_vector:
-                nc.vector.tensor_copy(zg[i][:, halves[d]], z[i][:].indirect(cell_t[:, lists[d]]))
+                nc.vector.tensor_copy(zg[i, d], z[i][:].indirect(cell_t[:, lists[d]]))
             else:
-                nc.scalar.activation(zg[i][:, halves[d]], z[i][:].indirect(cell_t[:, lists[d]]), ACT.Copy)
+                nc.scalar.activation(zg[i, d], z[i][:].indirect(cell_t[:, lists[d]]), ACT.Copy)
 
         yp = {}
 
@@ -116,9 +120,11 @@ def tile_picked_yivf_cal_p_kernel(tc, x_words, x_scales, hT, e_words, e_scales, 
 
         def add(u, n):
             i, d = units[u][n]
-            nc.vector.tensor_tensor(sums[u][:, n, :], yp[u][:, n, :], zg[i][:, halves[d]], ALU.add)
+            nc.vector.tensor_tensor(sums[u][:, n, :], yp[u][:, n, :], zg[i, d], ALU.add)
 
         nc.vector.tensor_copy(esg[:], es[:].indirect(cent_t[:]))
+        for i in range(2):
+            hq[i] = lay.tile([P, P], U32, name=f"hq{i}", align_bytes=64, offset=2048 + 512 * i)
         interleave(0, P)
         interleave(1, 0)
         quantize(0)
@@ -129,20 +135,22 @@ def tile_picked_yivf_cal_p_kernel(tc, x_words, x_scales, hT, e_words, e_scales, 
         cell_scores(1, "b3")
         for d in range(2):
             nc.vector.tensor_copy(xsg[d][:], xs[:].indirect(offs_t[:, lists[d]]))
-        zg[0] = lay.tile([P, S], F32, name="zg0", align_bytes=64, offset=0)
+        zg[0, 0] = lay.tile([P, H], F32, name="zg00", align_bytes=64, offset=0)[:]
         interleave(2, 0)
         interleave(3, 0)
         look_up(0, 0, True)
-        look_up(1, 0, False)
+        nc.scalar.activation(zrow[1][:, chunks[0]], z[1][:].indirect(cell_t[:, 0:8]), ACT.Copy)
         gT = psum.tile([P, NT, P], F32, name="gT", tag="b4")
         for c in range(NT):
             nc.tensor.transpose(gT[:, c, :], gg[:, chunks[c]], ident[:])
         nc.scalar.copy(gcol[:], gT[:, :, P - 1])
+        nc.scalar.activation(zrow[1][:, chunks[1]], z[1][:].indirect(cell_t[:, 8:16]), ACT.Copy)
         gb = psum.tile([P, S], F32, name="gb", tag="b1")
         for c in range(NT):
             nc.tensor.transpose(gb[:, chunks[c]], gcol[:, c : c + 1].to_broadcast([P, P]), ident[:])
         quantize(2)
         cell_scores(2, "b0")
+        zg[0, 1] = keep.tile([P, H], F32, name="zg01", tag="hb2", align_bytes=64)[:]
         look_up(0, 1, True)
         look_up(1, 1, False)
         quantize(3)
@@ -154,27 +162,34 @@ def tile_picked_yivf_cal_p_kernel(tc, x_words, x_scales, hT, e_words, e_scales, 
         for u in range(NT):
             scores(u, f"b{4 + u}")
         for i in range(2, NT):
-            nc.scalar.activation(zg[i][:], z[i][:].indirect(cell_t[:]), ACT.Copy)
+            nc.scalar.activation(zrow[i][:], z[i][:].indirect(cell_t[:]), ACT.Copy)
 
-        out_rows = out.rearrange("(g p) s -> p g s", p=P)
+        def scale(u, n):
+            nc.vector.tensor_tensor(scaled[u][:, n, :], sums[u][:, n, :], gb[:, halves[units[u][n][1]]], ALU.mult)
+
+        def squash(u, n):
+            i, d = units[u][n]
+            nc.scalar.activation(res[u, n][:], scaled[u][:, n, :], ACT.Tanh)
+            nc.sync.dma_start(out[P * i : P * (i + 1), halves[d]], res[u, n][:])
+
+        def scale_on_gpsimd(u, n):
+            nc.gpsimd.tensor_tensor(scaled[u][:, n, :], sums[u][:, n, :], gsb[:], ALU.mult)
+
         for n in range(2):
             add(0, n)
-            nc.gpsimd.tensor_tensor(scaled[0][:, n, :], sums[0][:, n, :], gsb[:], ALU.mult)
-        for n in range(2):
-            add(1, n)
-        nc.vector.tensor_tensor(sums[2][:].rearrange("p a b -> p (a b)"), yp[2][:].rearrange("p a b -> p (a b)"), zg[2][:], ALU.add)
-        nc.vector.tensor_tensor(scaled[1][:], sums[1][:], gb[:, halves[1]].unsqueeze(1).to_broadcast([P, 2, H]), ALU.mult)
-        nc.vector.tensor_tensor(scaled[2][:].rearrange("p a b -> p (a b)"), sums[2][:].rearrange("p a b -> p (a b)"), gb[:], ALU.mult)
-        for n in range(2):
-            add(3, n)
-        for d in range(2):
-            nc.vector.tensor_tensor(scaled[3][:, d, :], sums[3][:, d, :], gb[:, halves[d]], ALU.mult)
-        for u in range(NT - 1):
-            nc.scalar.activation(res[u][:], scaled[u][:], ACT.Tanh)
-            if u < 2:
-                nc.sync.dma_start(out_rows[:, 0:2, halves[u]], res[u][:])
-            else:
-                nc.sync.dma_start(out_rows[:, u, :], res[u][:].rearrange("p a b -> p (a b)"))
-        for d in range(2):
-            nc.scalar.activation(res[3][:, d, :], scaled[3][:, d, :], ACT.Tanh)
-            nc.sync.dma_start(out_rows[:, 3, halves[d]], res[3][:, d, :])
+            scale_on_gpsimd(0, n)
+        add(1, 0)
+        add(1, 1)
+        add(2, 0)
+        scale_on_gpsimd(2, 0)
+        scale(1, 0)
+        scale(1, 1)
+        add(2, 1)
+        add(3, 0)
+        scale_on_gpsimd(3, 0)
+        add(3, 1)
+        scale(2, 1)
+        scale(3, 1)
+        res[3, 0] = keep.tile([P, H], F32, name="res30", tag="sum3", align_bytes=64)
+        for u, n in ((0, 0), (0, 1), (1, 0), (1, 1), (2, 0), (2, 1), (3, 1), (3, 0)):
+            squash(u, n)

@@ -120,7 +120,7 @@ def tile_picked_yivf_cal_p_kernel(tc, x_words, x_scales, hT, e_words, e_scales, 
 
         def add(u, n):
             i, d = units[u][n]
-            nc.vector.tensor_tensor(sums[u][:, n, :], yp[u][:, n, :], zg[i, d], ALU.add)
+            nc.vector.tensor_tensor(sums[u][:, n, :], zg[i, d], yp[u][:, n, :], ALU.add)
 
         nc.vector.tensor_copy(esg[:], es[:].indirect(cent_t[:]))
         for i in range(2):

@@ -38,7 +38,7 @@ def tile_picked_yivf_cal_p_kernel(tc, x_words, x_scales, hT, e_words, e_scales, 
         gwin = keep.tile([P, T], F32, name="gwin", align_bytes=64)
         hpair = [keep.tile([P, 4, 2 * P], F32, name=f"hpair{u}", tag=f"hpair{u}", align_bytes=64) for u in range(2)]
         hsrc = [hpair[i // 2][:, :, P * (i % 2) : P * (i % 2 + 1)] for i in range(NT)]
-        hb = [keep.tile([P, P, 4], BF16, name=f"hb{i}", tag=f"hb{i}", align_bytes=64) for i in range(NT)]
+        hb = [keep.tile([P, P, 4], BF16, name=f"hb{i}", align_bytes=64) for i in range(NT)]
         hq = {i: keep.tile([P, P], U32, name=f"hq{i}", align_bytes=64) for i in (2, 3)}
         hs = [keep.tile([P, P], U8, name=f"hs{i}", align_bytes=64) for i in range(NT)]
         xg = [keep.tile([P, H], U32, name=f"xg{d}", align_bytes=64) for d in range(2)]
@@ -57,7 +57,7 @@ def tile_picked_yivf_cal_p_kernel(tc, x_words, x_scales, hT, e_words, e_scales, 
                 zg[i, d] = zrow[i][:, H * d : H * (d + 1)]
         sums = [keep.tile([P, 2, H], F32, name=f"sum{u}", tag=f"sum{u}", align_bytes=64) for u in range(NT)]
         scaled = [keep.tile([P, 2, H], F32, name=f"scaled{u}", align_bytes=64) for u in range(NT)]
-        res = {(u, n): keep.tile([P, H], F32, name=f"res{u}{n}", align_bytes=64) for u in range(NT) for n in range(2) if (u, n) != (3, 0)}
+        res = {(u, n): keep.tile([P, H], F32, name=f"res{u}{n}", align_bytes=64) for u in range(NT) for n in range(2) if (u, n) != (2, 0)}
 
         nc.gpsimd.memset(xs[:].bitcast(I32), 0)
         nc.gpsimd.memset(z[3][:, R:], 0.0)
@@ -150,9 +150,9 @@ def tile_picked_yivf_cal_p_kernel(tc, x_words, x_scales, hT, e_words, e_scales, 
             nc.tensor.transpose(gb[:, chunks[c]], gcol[:, c : c + 1].to_broadcast([P, P]), ident[:])
         quantize(2)
         cell_scores(2, "b0")
-        zg[0, 1] = keep.tile([P, H], F32, name="zg01", tag="hb2", align_bytes=64)[:]
-        look_up(0, 1, True)
+        zg[0, 1] = keep.tile([P, H], F32, name="zg01", align_bytes=64)[:]
         look_up(1, 1, False)
+        look_up(0, 1, False)
         quantize(3)
         cell_scores(3, "b2")
         gsb = keep.tile([P, H], F32, name="gsb", tag="hpair1", align_bytes=64)
@@ -164,13 +164,14 @@ def tile_picked_yivf_cal_p_kernel(tc, x_words, x_scales, hT, e_words, e_scales, 
         for i in range(2, NT):
             nc.scalar.activation(zrow[i][:], z[i][:].indirect(cell_t[:]), ACT.Copy)
 
-        def scale(u, n):
-            nc.vector.tensor_tensor(scaled[u][:, n, :], sums[u][:, n, :], gb[:, halves[units[u][n][1]]], ALU.mult)
+        def scale(u, n, part=slice(0, H)):
+            start = H * units[u][n][1]
+            nc.vector.tensor_tensor(scaled[u][:, n, part], sums[u][:, n, part], gb[:, start + part.start : start + part.stop], ALU.mult)
 
-        def squash(u, n):
+        def squash(u, n, part=slice(0, H)):
             i, d = units[u][n]
-            nc.scalar.activation(res[u, n][:], scaled[u][:, n, :], ACT.Tanh)
-            nc.sync.dma_start(out[P * i : P * (i + 1), halves[d]], res[u, n][:])
+            nc.scalar.activation(res[u, n][:, part], scaled[u][:, n, part], ACT.Tanh)
+            nc.sync.dma_start(out[P * i : P * (i + 1), H * d + part.start : H * d + part.stop], res[u, n][:, part])
 
         def scale_on_gpsimd(u, n):
             nc.gpsimd.tensor_tensor(scaled[u][:, n, :], sums[u][:, n, :], gsb[:], ALU.mult)
@@ -186,10 +187,13 @@ def tile_picked_yivf_cal_p_kernel(tc, x_words, x_scales, hT, e_words, e_scales, 
         scale(1, 1)
         add(2, 1)
         add(3, 0)
-        scale_on_gpsimd(3, 0)
-        add(3, 1)
         scale(2, 1)
-        scale(3, 1)
-        res[3, 0] = keep.tile([P, H], F32, name="res30", tag="sum3", align_bytes=64)
-        for u, n in ((0, 0), (0, 1), (1, 0), (1, 1), (2, 0), (2, 1), (3, 1), (3, 0)):
+        add(3, 1)
+        scale(3, 0)
+        for c in range(2):
+            scale(3, 1, chunks[c])
+        res[2, 0] = keep.tile([P, H], F32, name="res20", tag="sum1", align_bytes=64)
+        for u, n in ((0, 0), (0, 1), (1, 0), (1, 1), (2, 0), (2, 1), (3, 0)):
             squash(u, n)
+        for c in range(2):
+            squash(3, 1, chunks[c])

@@ -112,15 +112,17 @@ def tile_picked_yivf_cal_p_kernel(tc, x_words, x_scales, hT, e_words, e_scales, 
 
         yp = {}
 
-        def scores(u, tag):
-            yp[u] = psum.tile([P, 2, H], F32, name="yp", tag=tag)
-            for n, (i, d) in enumerate(units[u]):
-                nc.tensor.matmul_mx(out=yp[u][:, n, :], lhsT=hq[i][:].bitcast(FP8X4), lhsT_scale=hs[i][:],
+        def scores(pieces, tag):
+            bank = psum.tile([P, len(pieces), H], F32, name="yp", tag=tag)
+            for k, (u, n) in enumerate(pieces):
+                i, d = units[u][n]
+                nc.tensor.matmul_mx(out=bank[:, k, :], lhsT=hq[i][:].bitcast(FP8X4), lhsT_scale=hs[i][:],
                                     rhs=xg[d][:].bitcast(FP8X4), rhs_scale=xsg[d][4:P, :], start=True, stop=True)
+                yp[u, n] = bank[:, k, :]
 
         def add(u, n):
             i, d = units[u][n]
-            nc.vector.tensor_tensor(sums[u][:, n, :], zg[i, d], yp[u][:, n, :], ALU.add)
+            nc.vector.tensor_tensor(sums[u][:, n, :], zg[i, d], yp[u, n], ALU.add)
 
         nc.vector.tensor_copy(esg[:], es[:].indirect(cent_t[:]))
         for i in range(2):
@@ -159,8 +161,12 @@ def tile_picked_yivf_cal_p_kernel(tc, x_words, x_scales, hT, e_words, e_scales, 
         nc.scalar.copy(gsb[:], gb[:, halves[0]])
         for d in range(2):
             nc.vector.tensor_copy(xg[d][:], xw[:].bitcast(U32).indirect(offs_t[:, lists[d]]))
-        for u in range(NT):
-            scores(u, f"b{4 + u}")
+        scores([(0, 0)], "b4")
+        scores([(0, 1)], "b5")
+        scores([(1, 0)], "b6")
+        scores([(1, 1)], "b3")
+        scores([(2, 0), (2, 1)], "b7")
+        scores([(3, 0), (3, 1)], "b0")
         for i in range(2, NT):
             nc.scalar.activation(zrow[i][:], z[i][:].indirect(cell_t[:]), ACT.Copy)
 
@@ -181,9 +187,9 @@ def tile_picked_yivf_cal_p_kernel(tc, x_words, x_scales, hT, e_words, e_scales, 
             scale_on_gpsimd(0, n)
         add(1, 0)
         add(1, 1)
+        scale(1, 0)
         add(2, 0)
         scale_on_gpsimd(2, 0)
-        scale(1, 0)
         scale(1, 1)
         add(2, 1)
         add(3, 0)
@@ -192,8 +198,8 @@ def tile_picked_yivf_cal_p_kernel(tc, x_words, x_scales, hT, e_words, e_scales, 
         scale(3, 0)
         for c in range(2):
             scale(3, 1, chunks[c])
-        res[2, 0] = keep.tile([P, H], F32, name="res20", tag="sum1", align_bytes=64)
-        for u, n in ((0, 0), (0, 1), (1, 0), (1, 1), (2, 0), (2, 1), (3, 0)):
+        res[2, 0] = keep.tile([P, H], F32, name="res20", tag="sum2", align_bytes=64)
+        for u, n in ((0, 0), (0, 1), (1, 0), (1, 1), (2, 1), (2, 0), (3, 0)):
             squash(u, n)
         for c in range(2):
             squash(3, 1, chunks[c])

@@ -32,24 +32,24 @@ def tile_picked_yivf_cal_p_kernel(tc, x_words, x_scales, hT, e_words, e_scales, 
         cent_t = keep.tile([P, R // 16], U16, name="cent_t")
         cell_t = keep.tile([P, S // 16], U16, name="cell_t")
         xw = keep.tile([P, T], I32, name="xw", align_bytes=64)
-        xs = lay.tile([P, T], U8, name="xs", align_bytes=64, offset=0)
+        xs = keep.tile([P, T], U8, name="xs", align_bytes=64)
         ew = keep.tile([P, W], I32, name="ew", align_bytes=64)
         es = lay.tile([P, W], U8, name="es", align_bytes=64, offset=2048)
-        gwin = keep.tile([P, T], F32, name="gwin", align_bytes=64)
+        gwin = lay.tile([P, T], F32, name="gwin", align_bytes=64, offset=4096)
         hpair = [keep.tile([P, 4, 2 * P], F32, name=f"hpair{u}", tag=f"hpair{u}", align_bytes=64) for u in range(2)]
         hsrc = [hpair[i // 2][:, :, P * (i % 2) : P * (i % 2 + 1)] for i in range(NT)]
-        hb = [keep.tile([P, P, 4], BF16, name=f"hb{i}", align_bytes=64) for i in range(NT)]
+        hb = {i: keep.tile([P, P, 4], BF16, name=f"hb{i}", align_bytes=64) for i in (1, 2, 3)}
         hq = {i: keep.tile([P, P], U32, name=f"hq{i}", align_bytes=64) for i in (2, 3)}
         hs = [keep.tile([P, P], U8, name=f"hs{i}", align_bytes=64) for i in range(NT)]
         xg = [keep.tile([P, H], U32, name=f"xg{d}", align_bytes=64) for d in range(2)]
-        xsg = [keep.tile([P, H], U8, name=f"xsg{d}", align_bytes=64) for d in range(2)]
+        xsg = keep.tile([P, S], U8, name="xsg", align_bytes=64)
+        xplane = keep.tile([P, S], U8, name="xplane", align_bytes=64)
         eg = keep.tile([P, R], U32, name="eg", align_bytes=64)
         esg = keep.tile([P, R], U8, name="esg", align_bytes=64)
         gg = keep.tile([P, S], F32, name="gg", align_bytes=64)
         gcol = keep.tile([P, NT], F32, name="gcol", align_bytes=64)
         ident = keep.tile([P, P], F32, name="ident", align_bytes=64)
-        zw = [ZW, ZW, S + 16, S + 16]
-        z = [keep.tile([P, zw[i]], F32, name=f"z{i}", align_bytes=64) for i in range(NT)]
+        z = [keep.tile([P, ZW], F32, name=f"z{i}", align_bytes=64) for i in range(NT)]
         zg = {}
         zrow = {i: keep.tile([P, S], F32, name=f"zg{i}", align_bytes=64) for i in range(1, NT)}
         for i in range(1, NT):
@@ -59,28 +59,32 @@ def tile_picked_yivf_cal_p_kernel(tc, x_words, x_scales, hT, e_words, e_scales, 
         scaled = [keep.tile([P, 2, H], F32, name=f"scaled{u}", align_bytes=64) for u in range(NT)]
         res = {(u, n): keep.tile([P, H], F32, name=f"res{u}{n}", align_bytes=64) for u in range(NT) for n in range(2) if (u, n) != (2, 0)}
 
-        nc.gpsimd.memset(xs[:].bitcast(I32), 0)
-        nc.gpsimd.memset(z[3][:, R:], 0.0)
-        for i in range(NT - 1):
-            nc.scalar.copy(z[i][:, R:], z[3][:, R : zw[i]])
+        make_identity(nc, ident[:])
         nc.vector.memset(es[:].bitcast(I32), 0)
+        nc.vector.memset(z[0][:, R:], 0.0)
         nc.vector.memset(gwin[0 : P - 1, :], 0.0)
+        nc.vector.memset(xs[0 : P - 16, :].bitcast(I32), 0)
+
+        def load_centroid_scales(queue, q):
+            queue.dma_start(es[32 * q : 32 * q + 4, :].bitcast(I32), e_scales[0, 4 * q : 4 * q + 4, :].bitcast(I32))
 
         h_rows = hT.rearrange("(p j) t -> p j t", j=4)
+        nc.sync.dma_start(offs_t[:], offs)
+        nc.scalar.dma_start(xs[P - 16 : P, :].bitcast(I32), x_scales[0].bitcast(I32))
         nc.sync.dma_start(cent_t[:], cent)
+        nc.scalar.dma_start(gwin[P - 1 : P, :], gain[0:1, :])
         nc.sync.dma_start(hpair[0][:], h_rows[:, :, 0 : 2 * P])
         for q in range(4):
-            nc.sync.dma_start(es[32 * q : 32 * q + 4, :].bitcast(I32), e_scales[0, 4 * q : 4 * q + 4, :].bitcast(I32))
-        nc.sync.dma_start(gwin[P - 1 : P, :], gain[0:1, :])
+            load_centroid_scales(nc.sync, q)
         nc.sync.dma_start(ew[:], e_words[0].rearrange("p n t -> p (n t)").bitcast(I32))
-        nc.sync.dma_start(offs_t[:], offs)
-        nc.sync.dma_start(cell_t[:], cell)
-        for q in range(4):
-            nc.sync.dma_start(xs[32 * q + 4 : 32 * q + 4 + 4, :].bitcast(I32), x_scales[0, 4 * q : 4 * q + 4, :].bitcast(I32))
         nc.sync.dma_start(hpair[1][:], h_rows[:, :, 2 * P : 4 * P])
+        nc.sync.dma_start(cell_t[:], cell)
         nc.sync.dma_start(xw[:], x_words[0].rearrange("p n t -> p (n t)").bitcast(I32))
 
-        make_identity(nc, ident[:])
+        nc.scalar.copy(z[1][:, R:], z[0][:, R:])
+        nc.gpsimd.memset(xplane[:].bitcast(I32), 0)
+        for i in range(2, NT):
+            nc.gpsimd.memset(z[i][:, R:], 0.0)
 
         halves = [slice(0, H), slice(H, S)]
         chunks = [slice(P * c, P * (c + 1)) for c in range(NT)]
@@ -117,62 +121,65 @@ def tile_picked_yivf_cal_p_kernel(tc, x_words, x_scales, hT, e_words, e_scales, 
             for k, (u, n) in enumerate(pieces):
                 i, d = units[u][n]
                 nc.tensor.matmul_mx(out=bank[:, k, :], lhsT=hq[i][:].bitcast(FP8X4), lhsT_scale=hs[i][:],
-                                    rhs=xg[d][:].bitcast(FP8X4), rhs_scale=xsg[d][4:P, :], start=True, stop=True)
+                                    rhs=xg[d][:].bitcast(FP8X4), rhs_scale=xplane[:, halves[d]], start=True, stop=True)
                 yp[u, n] = bank[:, k, :]
 
         def add(u, n):
             i, d = units[u][n]
             nc.vector.tensor_tensor(sums[u][:, n, :], zg[i, d], yp[u, n], ALU.add)
 
+        nc.vector.tensor_copy(xsg[:], xs[:].indirect(offs_t[:]))
+        for q in range(4):
+            rows = P - 16 + 4 * q
+            nc.sync.dma_start(xplane[32 * q : 32 * q + 4, :].bitcast(I32), xsg[rows : rows + 4, :].bitcast(I32))
+        for d in range(2):
+            nc.scalar.activation(gg[:, halves[d]], gwin[:].indirect(offs_t[:, lists[d]]), ACT.Copy)
+        hb[0] = lay.tile([P, P, 4], BF16, name="hb0", align_bytes=64, offset=4096)
         nc.vector.tensor_copy(esg[:], es[:].indirect(cent_t[:]))
         for i in range(2):
             hq[i] = lay.tile([P, P], U32, name=f"hq{i}", align_bytes=64, offset=2048 + 512 * i)
         interleave(0, P)
         interleave(1, 0)
-        quantize(0)
-        quantize(1)
-        nc.vector.tensor_copy(eg[:], ew[:].bitcast(U32).indirect(cent_t[:]))
-        nc.scalar.activation(gg[:], gwin[:].indirect(offs_t[:]), ACT.Copy)
-        cell_scores(0, "b2")
-        cell_scores(1, "b3")
-        for d in range(2):
-            nc.vector.tensor_copy(xsg[d][:], xs[:].indirect(offs_t[:, lists[d]]))
-        zg[0, 0] = lay.tile([P, H], F32, name="zg00", align_bytes=64, offset=0)[:]
-        interleave(2, 0)
-        interleave(3, 0)
-        look_up(0, 0, True)
-        nc.scalar.activation(zrow[1][:, chunks[0]], z[1][:].indirect(cell_t[:, 0:8]), ACT.Copy)
-        gT = psum.tile([P, NT, P], F32, name="gT", tag="b4")
+        gT = psum.tile([P, NT, P], F32, name="gT", tag="b0")
         for c in range(NT):
             nc.tensor.transpose(gT[:, c, :], gg[:, chunks[c]], ident[:])
         nc.scalar.copy(gcol[:], gT[:, :, P - 1])
-        nc.scalar.activation(zrow[1][:, chunks[1]], z[1][:].indirect(cell_t[:, 8:16]), ACT.Copy)
-        gb = psum.tile([P, S], F32, name="gb", tag="b1")
+        gb = [psum.tile([P, H], F32, name=f"gb{d}", tag=f"b{1 + d}") for d in range(2)]
         for c in range(NT):
-            nc.tensor.transpose(gb[:, chunks[c]], gcol[:, c : c + 1].to_broadcast([P, P]), ident[:])
+            nc.tensor.transpose(gb[c // 2][:, chunks[c % 2]], gcol[:, c : c + 1].to_broadcast([P, P]), ident[:])
+        gsb = keep.tile([P, H], F32, name="gsb", align_bytes=64)
+        nc.scalar.copy(gsb[:], gb[0][:])
+        gains = [gsb, gb[1]]
+        quantize(0)
+        quantize(1)
+        nc.vector.tensor_copy(eg[:], ew[:].bitcast(U32).indirect(cent_t[:]))
+        cell_scores(0, "b0")
+        cell_scores(1, "b1")
+        for i in range(2, NT):
+            nc.vector.tensor_copy(hb[i][:], hsrc[i].rearrange("p j t -> p t j"))
+        for d in range(2):
+            look_up(1, d, False)
         quantize(2)
-        cell_scores(2, "b0")
-        zg[0, 1] = keep.tile([P, H], F32, name="zg01", align_bytes=64)[:]
-        look_up(1, 1, False)
-        look_up(0, 1, False)
+        cell_scores(2, "b3")
         quantize(3)
-        cell_scores(3, "b2")
-        gsb = keep.tile([P, H], F32, name="gsb", tag="hpair1", align_bytes=64)
-        nc.scalar.copy(gsb[:], gb[:, halves[0]])
+        cell_scores(3, "b4")
+        for d in range(2):
+            zg[0, d] = keep.tile([P, H], F32, name=f"zg0{d}", align_bytes=64)[:]
+            look_up(0, d, True)
         for d in range(2):
             nc.vector.tensor_copy(xg[d][:], xw[:].bitcast(U32).indirect(offs_t[:, lists[d]]))
-        scores([(0, 0)], "b4")
-        scores([(0, 1)], "b5")
-        scores([(1, 0)], "b6")
-        scores([(1, 1)], "b3")
-        scores([(2, 0), (2, 1)], "b7")
-        scores([(3, 0), (3, 1)], "b0")
+        scores([(0, 0)], "b5")
+        scores([(0, 1)], "b6")
+        scores([(1, 0)], "b7")
+        scores([(1, 1)], "b1")
+        scores([(2, 0), (2, 1)], "b0")
+        scores([(3, 0), (3, 1)], "b3")
         for i in range(2, NT):
-            nc.scalar.activation(zrow[i][:], z[i][:].indirect(cell_t[:]), ACT.Copy)
+            for d in range(2):
+                look_up(i, d, False)
 
         def scale(u, n, part=slice(0, H)):
-            start = H * units[u][n][1]
-            nc.vector.tensor_tensor(scaled[u][:, n, part], sums[u][:, n, part], gb[:, start + part.start : start + part.stop], ALU.mult)
+            nc.vector.tensor_tensor(scaled[u][:, n, part], sums[u][:, n, part], gains[units[u][n][1]][:, part], ALU.mult)
 
         def squash(u, n, part=slice(0, H)):
             i, d = units[u][n]

@@ -33,21 +33,21 @@ def tile_picked_yivf_cal_p_kernel(tc, x_words, x_scales, hT, e_words, e_scales, 
         cell_t = keep.tile([P, S // 16], U16, name="cell_t")
         xw = keep.tile([P, T], I32, name="xw", align_bytes=64)
         xs = keep.tile([P, T], U8, name="xs", align_bytes=64)
-        ew = keep.tile([P, W], I32, name="ew", align_bytes=64)
+        ew = lay.tile([P, W], I32, name="ew", align_bytes=64, offset=12288)
         es = lay.tile([P, W], U8, name="es", align_bytes=64, offset=2048)
-        gwin = lay.tile([P, T], F32, name="gwin", align_bytes=64, offset=4096)
-        hpair = [keep.tile([P, 4, 2 * P], F32, name=f"hpair{u}", tag=f"hpair{u}", align_bytes=64) for u in range(2)]
-        hsrc = [hpair[i // 2][:, :, P * (i % 2) : P * (i % 2 + 1)] for i in range(NT)]
-        hb = {i: keep.tile([P, P, 4], BF16, name=f"hb{i}", align_bytes=64) for i in (1, 2, 3)}
-        hq = {i: keep.tile([P, P], U32, name=f"hq{i}", align_bytes=64) for i in (2, 3)}
+        gwin = keep.tile([P, T], F32, name="gwin", align_bytes=64)
+        hraw = keep.tile([P, 4, V], F32, name="hraw", align_bytes=64)
+        hsrc = [hraw[:, :, P * i : P * (i + 1)] for i in range(NT)]
+        hb = {0: keep.tile([P, P, 4], BF16, name="hb0", align_bytes=64)}
+        hq = {}
         hs = [keep.tile([P, P], U8, name=f"hs{i}", align_bytes=64) for i in range(NT)]
         xg = [keep.tile([P, H], U32, name=f"xg{d}", align_bytes=64) for d in range(2)]
         xsg = keep.tile([P, S], U8, name="xsg", align_bytes=64)
         xplane = keep.tile([P, S], U8, name="xplane", align_bytes=64)
         eg = keep.tile([P, R], U32, name="eg", align_bytes=64)
         esg = keep.tile([P, R], U8, name="esg", align_bytes=64)
-        gg = keep.tile([P, S], F32, name="gg", align_bytes=64)
-        gcol = keep.tile([P, NT], F32, name="gcol", align_bytes=64)
+        gg = lay.tile([P, S], F32, name="gg", align_bytes=64, offset=16384)
+        gcol = lay.tile([P, NT], F32, name="gcol", align_bytes=64, offset=18432)
         ident = keep.tile([P, P], F32, name="ident", align_bytes=64)
         z = [keep.tile([P, ZW], F32, name=f"z{i}", align_bytes=64) for i in range(NT)]
         zg = {}
@@ -73,11 +73,10 @@ def tile_picked_yivf_cal_p_kernel(tc, x_words, x_scales, hT, e_words, e_scales, 
         nc.scalar.dma_start(xs[P - 16 : P, :].bitcast(I32), x_scales[0].bitcast(I32))
         nc.sync.dma_start(cent_t[:], cent)
         nc.scalar.dma_start(gwin[P - 1 : P, :], gain[0:1, :])
-        nc.sync.dma_start(hpair[0][:], h_rows[:, :, 0 : 2 * P])
+        nc.sync.dma_start(hraw[:], h_rows)
         for q in range(4):
             load_centroid_scales(nc.sync, q)
         nc.sync.dma_start(ew[:], e_words[0].rearrange("p n t -> p (n t)").bitcast(I32))
-        nc.sync.dma_start(hpair[1][:], h_rows[:, :, 2 * P : 4 * P])
         nc.sync.dma_start(cell_t[:], cell)
         nc.sync.dma_start(xw[:], x_words[0].rearrange("p n t -> p (n t)").bitcast(I32))
 
@@ -89,13 +88,6 @@ def tile_picked_yivf_cal_p_kernel(tc, x_words, x_scales, hT, e_words, e_scales, 
         halves = [slice(0, H), slice(H, S)]
         chunks = [slice(P * c, P * (c + 1)) for c in range(NT)]
         lists = [slice(0, H // 16), slice(H // 16, S // 16)]
-
-        def interleave(i, cut):
-            turned = hsrc[i].rearrange("p j t -> p t j")
-            if cut > 0:
-                nc.scalar.copy(hb[i][:, :cut, :], turned[:, :cut, :])
-            if cut < P:
-                nc.gpsimd.tensor_scalar(hb[i][:, cut:, :], turned[:, cut:, :], 1.0, 0.0, ALU.mult, ALU.add)
 
         def quantize(i):
             nc.vector.quantize_mx(out=hq[i][:].bitcast(FP8X4), scales=hs[i][:], in_=hb[i][:].rearrange("p t j -> p (t j)"))
@@ -134,12 +126,9 @@ def tile_picked_yivf_cal_p_kernel(tc, x_words, x_scales, hT, e_words, e_scales, 
             nc.sync.dma_start(xplane[32 * q : 32 * q + 4, :].bitcast(I32), xsg[rows : rows + 4, :].bitcast(I32))
         for d in range(2):
             nc.scalar.activation(gg[:, halves[d]], gwin[:].indirect(offs_t[:, lists[d]]), ACT.Copy)
-        hb[0] = lay.tile([P, P, 4], BF16, name="hb0", align_bytes=64, offset=4096)
         nc.vector.tensor_copy(esg[:], es[:].indirect(cent_t[:]))
-        for i in range(2):
-            hq[i] = lay.tile([P, P], U32, name=f"hq{i}", align_bytes=64, offset=2048 + 512 * i)
-        interleave(0, P)
-        interleave(1, 0)
+        hq[0] = lay.tile([P, P], U32, name="hq0", align_bytes=64, offset=2048)
+        nc.vector.tensor_copy(hb[0][:], hsrc[0].rearrange("p j t -> p t j"))
         gT = psum.tile([P, NT, P], F32, name="gT", tag="b0")
         for c in range(NT):
             nc.tensor.transpose(gT[:, c, :], gg[:, chunks[c]], ident[:])
@@ -150,22 +139,21 @@ def tile_picked_yivf_cal_p_kernel(tc, x_words, x_scales, hT, e_words, e_scales, 
         gsb = keep.tile([P, H], F32, name="gsb", align_bytes=64)
         nc.scalar.copy(gsb[:], gb[0][:])
         gains = [gsb, gb[1]]
+        for i in range(1, NT):
+            hb[i] = lay.tile([P, P, 4], BF16, name=f"hb{i}", align_bytes=64, offset=16384 + 1024 * (i - 1))
+            nc.scalar.copy(hb[i][:], hsrc[i].rearrange("p j t -> p t j"))
         quantize(0)
-        quantize(1)
         nc.vector.tensor_copy(eg[:], ew[:].bitcast(U32).indirect(cent_t[:]))
         cell_scores(0, "b0")
-        cell_scores(1, "b1")
-        for i in range(2, NT):
-            nc.vector.tensor_copy(hb[i][:], hsrc[i].rearrange("p j t -> p t j"))
-        for d in range(2):
-            look_up(1, d, False)
-        quantize(2)
-        cell_scores(2, "b3")
-        quantize(3)
-        cell_scores(3, "b4")
+        for i, tag in ((1, "b1"), (2, "b3"), (3, "b4")):
+            hq[i] = lay.tile([P, P], U32, name=f"hq{i}", align_bytes=64, offset=12288 + 512 * i)
+            quantize(i)
+            cell_scores(i, tag)
         for d in range(2):
             zg[0, d] = keep.tile([P, H], F32, name=f"zg0{d}", align_bytes=64)[:]
             look_up(0, d, True)
+        for d in range(2):
+            look_up(1, d, False)
         for d in range(2):
             nc.vector.tensor_copy(xg[d][:], xw[:].bitcast(U32).indirect(offs_t[:, lists[d]]))
         scores([(0, 0)], "b5")

@@ -50,14 +50,11 @@ def tile_picked_yivf_cal_p_kernel(tc, x_words, x_scales, hT, e_words, e_scales, 
         gcol = lay.tile([P, NT], F32, name="gcol", align_bytes=64, offset=18432)
         ident = keep.tile([P, P], F32, name="ident", align_bytes=64)
         z = [keep.tile([P, ZW], F32, name=f"z{i}", align_bytes=64) for i in range(NT)]
-        zg = {}
-        zrow = {i: keep.tile([P, S], F32, name=f"zg{i}", align_bytes=64) for i in range(1, NT)}
-        for i in range(1, NT):
-            for d in range(2):
-                zg[i, d] = zrow[i][:, H * d : H * (d + 1)]
-        sums = [keep.tile([P, 2, H], F32, name=f"sum{u}", tag=f"sum{u}", align_bytes=64) for u in range(NT)]
-        scaled = [keep.tile([P, 2, H], F32, name=f"scaled{u}", align_bytes=64) for u in range(NT)]
-        res = {(u, n): keep.tile([P, H], F32, name=f"res{u}{n}", align_bytes=64) for u in range(NT) for n in range(2) if (u, n) != (2, 0)}
+        pieces = [(i, d) for d in range(2) for i in range(NT)]
+        zg = {key: keep.tile([P, H], F32, name=f"zg{key[0]}{key[1]}", align_bytes=64) for key in pieces }
+        sums = {key: keep.tile([P, H], F32, name=f"sum{key[0]}{key[1]}", align_bytes=64) for key in pieces}
+        scaled = [keep.tile([P, S], F32, name=f"scaled{i}", align_bytes=64) for i in range(NT)]
+        res = [keep.tile([P, S], F32, name=f"res{i}", align_bytes=64) for i in range(NT)]
 
         make_identity(nc, ident[:])
         nc.vector.memset(es[:].bitcast(I32), 0)
@@ -98,27 +95,21 @@ def tile_picked_yivf_cal_p_kernel(tc, x_words, x_scales, hT, e_words, e_scales, 
                                 rhs=eg[:].bitcast(FP8X4), rhs_scale=esg[:], start=True, stop=True)
             nc.scalar.copy(z[i][:, 0:R], zp[:])
 
-        units = [[(0, 0), (1, 0)], [(0, 1), (1, 1)], [(2, 0), (2, 1)], [(3, 0), (3, 1)]]
-
         def look_up(i, d, on_vector):
             if on_vector:
-                nc.vector.tensor_copy(zg[i, d], z[i][:].indirect(cell_t[:, lists[d]]))
+                nc.vector.tensor_copy(zg[i, d][:], z[i][:].indirect(cell_t[:, lists[d]]))
             else:
-                nc.scalar.activation(zg[i, d], z[i][:].indirect(cell_t[:, lists[d]]), ACT.Copy)
+                nc.scalar.activation(zg[i, d][:], z[i][:].indirect(cell_t[:, lists[d]]), ACT.Copy)
 
         yp = {}
 
-        def scores(pieces, tag):
-            bank = psum.tile([P, len(pieces), H], F32, name="yp", tag=tag)
-            for k, (u, n) in enumerate(pieces):
-                i, d = units[u][n]
-                nc.tensor.matmul_mx(out=bank[:, k, :], lhsT=hq[i][:].bitcast(FP8X4), lhsT_scale=hs[i][:],
-                                    rhs=xg[d][:].bitcast(FP8X4), rhs_scale=xplane[:, halves[d]], start=True, stop=True)
-                yp[u, n] = bank[:, k, :]
+        def scores(i, d, tag):
+            yp[i, d] = psum.tile([P, H], F32, name="yp", tag=tag)
+            nc.tensor.matmul_mx(out=yp[i, d][:], lhsT=hq[i][:].bitcast(FP8X4), lhsT_scale=hs[i][:],
+                                rhs=xg[d][:].bitcast(FP8X4), rhs_scale=xplane[:, halves[d]], start=True, stop=True)
 
-        def add(u, n):
-            i, d = units[u][n]
-            nc.vector.tensor_tensor(sums[u][:, n, :], zg[i, d], yp[u, n], ALU.add)
+        def add(i, d):
+            nc.vector.tensor_tensor(sums[i, d][:], zg[i, d][:], yp[i, d][:], ALU.add)
 
         nc.vector.tensor_copy(xsg[:], xs[:].indirect(offs_t[:]))
         for q in range(4):
@@ -133,12 +124,11 @@ def tile_picked_yivf_cal_p_kernel(tc, x_words, x_scales, hT, e_words, e_scales, 
         for c in range(NT):
             nc.tensor.transpose(gT[:, c, :], gg[:, chunks[c]], ident[:])
         nc.scalar.copy(gcol[:], gT[:, :, P - 1])
-        gb = [psum.tile([P, H], F32, name=f"gb{d}", tag=f"b{1 + d}") for d in range(2)]
+        gb = psum.tile([P, S], F32, name="gb", tag="b2")
         for c in range(NT):
-            nc.tensor.transpose(gb[c // 2][:, chunks[c % 2]], gcol[:, c : c + 1].to_broadcast([P, P]), ident[:])
+            nc.tensor.transpose(gb[:, chunks[c]], gcol[:, c : c + 1].to_broadcast([P, P]), ident[:])
         gsb = keep.tile([P, H], F32, name="gsb", align_bytes=64)
-        nc.scalar.copy(gsb[:], gb[0][:])
-        gains = [gsb, gb[1]]
+        nc.scalar.copy(gsb[:], gb[:, halves[0]])
         for i in range(1, NT):
             hb[i] = lay.tile([P, P, 4], BF16, name=f"hb{i}", align_bytes=64, offset=16384 + 1024 * (i - 1))
             nc.scalar.copy(hb[i][:], hsrc[i].rearrange("p j t -> p t j"))
@@ -149,52 +139,44 @@ def tile_picked_yivf_cal_p_kernel(tc, x_words, x_scales, hT, e_words, e_scales, 
             hq[i] = lay.tile([P, P], U32, name=f"hq{i}", align_bytes=64, offset=12288 + 512 * i)
             quantize(i)
             cell_scores(i, tag)
-        for d in range(2):
-            zg[0, d] = keep.tile([P, H], F32, name=f"zg0{d}", align_bytes=64)[:]
-            look_up(0, d, True)
-        for d in range(2):
-            look_up(1, d, False)
+        for i in range(NT):
+            for d in range(2):
+                look_up(i, d, i == 0)
         for d in range(2):
             nc.vector.tensor_copy(xg[d][:], xw[:].bitcast(U32).indirect(offs_t[:, lists[d]]))
-        scores([(0, 0)], "b5")
-        scores([(0, 1)], "b6")
-        scores([(1, 0)], "b7")
-        scores([(1, 1)], "b1")
-        scores([(2, 0), (2, 1)], "b0")
-        scores([(3, 0), (3, 1)], "b3")
-        for i in range(2, NT):
-            for d in range(2):
-                look_up(i, d, False)
+        for i, d, tag in ((0, 0, "b5"), (1, 0, "b6"), (0, 1, "b7"), (1, 1, "b0"), (2, 0, "b1"), (2, 1, "b3"), (3, 0, "b4")):
+            scores(i, d, tag)
 
-        def scale(u, n, part=slice(0, H)):
-            nc.vector.tensor_tensor(scaled[u][:, n, part], sums[u][:, n, part], gains[units[u][n][1]][:, part], ALU.mult)
+        def scale(i, part):
+            d = part.start // H
+            nc.vector.tensor_tensor(scaled[i][:, part], sums[i, d][:, part.start - H * d : part.stop - H * d], gb[:, part], ALU.mult)
 
-        def squash(u, n, part=slice(0, H)):
-            i, d = units[u][n]
-            nc.scalar.activation(res[u, n][:, part], scaled[u][:, n, part], ACT.Tanh)
-            nc.sync.dma_start(out[P * i : P * (i + 1), H * d + part.start : H * d + part.stop], res[u, n][:, part])
+        def squash(i, part):
+            nc.scalar.activation(res[i][:, part], scaled[i][:, part], ACT.Tanh)
+            nc.sync.dma_start(out[P * i : P * (i + 1), part], res[i][:, part])
 
-        def scale_on_gpsimd(u, n):
-            nc.gpsimd.tensor_tensor(scaled[u][:, n, :], sums[u][:, n, :], gsb[:], ALU.mult)
+        def scale_on_gpsimd(i):
+            nc.gpsimd.tensor_tensor(scaled[i][:, halves[0]], sums[i, 0][:], gsb[:], ALU.mult)
 
-        for n in range(2):
-            add(0, n)
-            scale_on_gpsimd(0, n)
+        add(0, 0)
+        scale_on_gpsimd(0)
+        scores(3, 1, "b5")
         add(1, 0)
+        scale_on_gpsimd(1)
+        add(0, 1)
         add(1, 1)
-        scale(1, 0)
+        scale(0, halves[1])
         add(2, 0)
-        scale_on_gpsimd(2, 0)
-        scale(1, 1)
+        scale_on_gpsimd(2)
+        scale(1, halves[1])
         add(2, 1)
         add(3, 0)
-        scale(2, 1)
+        scale(2, halves[1])
         add(3, 1)
-        scale(3, 0)
-        for c in range(2):
-            scale(3, 1, chunks[c])
-        res[2, 0] = keep.tile([P, H], F32, name="res20", tag="sum2", align_bytes=64)
-        for u, n in ((0, 0), (0, 1), (1, 0), (1, 1), (2, 1), (2, 0), (3, 0)):
-            squash(u, n)
-        for c in range(2):
-            squash(3, 1, chunks[c])
+        scale(3, halves[0])
+        for c in (2, 3):
+            scale(3, chunks[c])
+        for i in range(NT - 1):
+            squash(i, slice(0, S))
+        squash(3, slice(0, 3 * P))
+        squash(3, chunks[3])

@@ -34,18 +34,19 @@ def tile_picked_yivf_cal_p_kernel(tc, x_words, x_scales, hT, e_words, e_scales, 
         xw = keep.tile([P, T], I32, name="xw", align_bytes=64)
         xs = keep.tile([P, T], U8, name="xs", align_bytes=64)
         ew = lay.tile([P, W], I32, name="ew", align_bytes=64, offset=12288)
-        es = lay.tile([P, W], U8, name="es", align_bytes=64, offset=2048)
+        es = keep.tile([P, W], U8, name="es", align_bytes=64)
         gwin = keep.tile([P, T], F32, name="gwin", align_bytes=64)
         hraw = keep.tile([P, 4, V], F32, name="hraw", align_bytes=64)
         hsrc = [hraw[:, :, P * i : P * (i + 1)] for i in range(NT)]
-        hb = {0: keep.tile([P, P, 4], BF16, name="hb0", align_bytes=64)}
-        hq = {}
+        hb = {i: keep.tile([P, P, 4], BF16, name=f"hb{i}", align_bytes=64) for i in range(2)}
+        hq = {i: keep.tile([P, P], U32, name=f"hq{i}", align_bytes=64) for i in range(2)}
         hs = [keep.tile([P, P], U8, name=f"hs{i}", align_bytes=64) for i in range(NT)]
         xg = [keep.tile([P, H], U32, name=f"xg{d}", align_bytes=64) for d in range(2)]
         xsg = keep.tile([P, S], U8, name="xsg", align_bytes=64)
         xplane = keep.tile([P, S], U8, name="xplane", align_bytes=64)
         eg = keep.tile([P, R], U32, name="eg", align_bytes=64)
         esg = keep.tile([P, R], U8, name="esg", align_bytes=64)
+        eplane = keep.tile([P, R], U8, name="eplane", align_bytes=64)
         gg = lay.tile([P, S], F32, name="gg", align_bytes=64, offset=16384)
         gcol = lay.tile([P, NT], F32, name="gcol", align_bytes=64, offset=18432)
         ident = keep.tile([P, P], F32, name="ident", align_bytes=64)
@@ -56,31 +57,27 @@ def tile_picked_yivf_cal_p_kernel(tc, x_words, x_scales, hT, e_words, e_scales, 
         scaled = [keep.tile([P, S], F32, name=f"scaled{i}", align_bytes=64) for i in range(NT)]
         res = [keep.tile([P, S], F32, name=f"res{i}", align_bytes=64) for i in range(NT)]
 
-        make_identity(nc, ident[:])
-        nc.vector.memset(es[:].bitcast(I32), 0)
+        nc.vector.memset(es[0 : P - 16, :].bitcast(I32), 0)
         nc.vector.memset(z[0][:, R:], 0.0)
         nc.vector.memset(gwin[0 : P - 1, :], 0.0)
-        nc.vector.memset(xs[0 : P - 16, :].bitcast(I32), 0)
+        nc.vector.memset(xs[0:48, :].bitcast(I32), 0)
+        nc.gpsimd.memset(xs[64:P, :].bitcast(I32), 0)
 
-        def load_centroid_scales(queue, q):
-            queue.dma_start(es[32 * q : 32 * q + 4, :].bitcast(I32), e_scales[0, 4 * q : 4 * q + 4, :].bitcast(I32))
-
-        h_rows = hT.rearrange("(p j) t -> p j t", j=4)
         nc.sync.dma_start(offs_t[:], offs)
-        nc.scalar.dma_start(xs[P - 16 : P, :].bitcast(I32), x_scales[0].bitcast(I32))
+        nc.scalar.dma_start(es[P - 16 : P, :].bitcast(I32), e_scales[0].bitcast(I32))
         nc.sync.dma_start(cent_t[:], cent)
         nc.scalar.dma_start(gwin[P - 1 : P, :], gain[0:1, :])
-        nc.sync.dma_start(hraw[:], h_rows)
-        for q in range(4):
-            load_centroid_scales(nc.sync, q)
+        nc.sync.dma_start(xs[48:64, :].bitcast(I32), x_scales[0].bitcast(I32))
+        nc.sync.dma_start(hraw[:], hT.rearrange("(p j) t -> p j t", j=4))
         nc.sync.dma_start(ew[:], e_words[0].rearrange("p n t -> p (n t)").bitcast(I32))
         nc.sync.dma_start(cell_t[:], cell)
-        nc.sync.dma_start(xw[:], x_words[0].rearrange("p n t -> p (n t)").bitcast(I32))
 
         nc.scalar.copy(z[1][:, R:], z[0][:, R:])
+        nc.gpsimd.memset(eplane[:].bitcast(I32), 0)
         nc.gpsimd.memset(xplane[:].bitcast(I32), 0)
         for i in range(2, NT):
             nc.gpsimd.memset(z[i][:, R:], 0.0)
+        make_identity(nc, ident[:])
 
         halves = [slice(0, H), slice(H, S)]
         chunks = [slice(P * c, P * (c + 1)) for c in range(NT)]
@@ -92,7 +89,7 @@ def tile_picked_yivf_cal_p_kernel(tc, x_words, x_scales, hT, e_words, e_scales, 
         def cell_scores(i, tag):
             zp = psum.tile([P, R], F32, name="zp", tag=tag)
             nc.tensor.matmul_mx(out=zp[:], lhsT=hq[i][:].bitcast(FP8X4), lhsT_scale=hs[i][:],
-                                rhs=eg[:].bitcast(FP8X4), rhs_scale=esg[:], start=True, stop=True)
+                                rhs=eg[:].bitcast(FP8X4), rhs_scale=eplane[:], start=True, stop=True)
             nc.scalar.copy(z[i][:, 0:R], zp[:])
 
         def look_up(i, d, on_vector):
@@ -111,31 +108,39 @@ def tile_picked_yivf_cal_p_kernel(tc, x_words, x_scales, hT, e_words, e_scales, 
         def add(i, d):
             nc.vector.tensor_tensor(sums[i, d][:], zg[i, d][:], yp[i, d][:], ALU.add)
 
+        def deal_rows(plane, picked, first):
+            for q in range(4):
+                rows = first + 4 * q
+                nc.sync.dma_start(plane[32 * q : 32 * q + 4, :].bitcast(I32), picked[rows : rows + 4, :].bitcast(I32))
+
+        nc.vector.tensor_copy(esg[:], es[:].indirect(cent_t[:]))
+        deal_rows(eplane, esg, P - 16)
+        nc.sync.dma_start(xw[:], x_words[0].rearrange("p n t -> p (n t)").bitcast(I32))
         nc.vector.tensor_copy(xsg[:], xs[:].indirect(offs_t[:]))
-        for q in range(4):
-            rows = P - 16 + 4 * q
-            nc.sync.dma_start(xplane[32 * q : 32 * q + 4, :].bitcast(I32), xsg[rows : rows + 4, :].bitcast(I32))
+        deal_rows(xplane, xsg, 48)
         for d in range(2):
             nc.scalar.activation(gg[:, halves[d]], gwin[:].indirect(offs_t[:, lists[d]]), ACT.Copy)
-        nc.vector.tensor_copy(esg[:], es[:].indirect(cent_t[:]))
-        hq[0] = lay.tile([P, P], U32, name="hq0", align_bytes=64, offset=2048)
-        nc.vector.tensor_copy(hb[0][:], hsrc[0].rearrange("p j t -> p t j"))
+        for i in range(2):
+            nc.vector.tensor_copy(hb[i][:], hsrc[i].rearrange("p j t -> p t j"))
         gT = psum.tile([P, NT, P], F32, name="gT", tag="b0")
         for c in range(NT):
             nc.tensor.transpose(gT[:, c, :], gg[:, chunks[c]], ident[:])
         nc.scalar.copy(gcol[:], gT[:, :, P - 1])
-        gb = psum.tile([P, S], F32, name="gb", tag="b2")
+        gb = [psum.tile([P, H], F32, name=f"gb{d}", tag=f"b{1 + d}") for d in range(2)]
         for c in range(NT):
-            nc.tensor.transpose(gb[:, chunks[c]], gcol[:, c : c + 1].to_broadcast([P, P]), ident[:])
+            nc.tensor.transpose(gb[c // 2][:, chunks[c % 2]], gcol[:, c : c + 1].to_broadcast([P, P]), ident[:])
         gsb = keep.tile([P, H], F32, name="gsb", align_bytes=64)
-        nc.scalar.copy(gsb[:], gb[:, halves[0]])
-        for i in range(1, NT):
+        nc.scalar.copy(gsb[:], gb[0][:])
+        gains = [gsb, gb[1]]
+        for i in range(2, NT):
             hb[i] = lay.tile([P, P, 4], BF16, name=f"hb{i}", align_bytes=64, offset=16384 + 1024 * (i - 1))
             nc.scalar.copy(hb[i][:], hsrc[i].rearrange("p j t -> p t j"))
         quantize(0)
+        quantize(1)
         nc.vector.tensor_copy(eg[:], ew[:].bitcast(U32).indirect(cent_t[:]))
         cell_scores(0, "b0")
-        for i, tag in ((1, "b1"), (2, "b3"), (3, "b4")):
+        cell_scores(1, "b1")
+        for i, tag in ((2, "b3"), (3, "b4")):
             hq[i] = lay.tile([P, P], U32, name=f"hq{i}", align_bytes=64, offset=12288 + 512 * i)
             quantize(i)
             cell_scores(i, tag)
@@ -149,7 +154,8 @@ def tile_picked_yivf_cal_p_kernel(tc, x_words, x_scales, hT, e_words, e_scales, 
 
         def scale(i, part):
             d = part.start // H
-            nc.vector.tensor_tensor(scaled[i][:, part], sums[i, d][:, part.start - H * d : part.stop - H * d], gb[:, part], ALU.mult)
+            within = slice(part.start - H * d, part.stop - H * d)
+            nc.vector.tensor_tensor(scaled[i][:, part], sums[i, d][:, within], gains[d][:, within], ALU.mult)
 
         def squash(i, part):
             nc.scalar.activation(res[i][:, part], scaled[i][:, part], ACT.Tanh)

@@ -19,6 +19,7 @@ P = 128
 NT = 4
 H = 256
 ZW = R + 16
+GAIN_CUT = 1280
 
 
 def tile_picked_yivf_cal_p_kernel(tc, x_words, x_scales, hT, e_words, e_scales, gain, offs, cent, cell, out):
@@ -39,7 +40,7 @@ def tile_picked_yivf_cal_p_kernel(tc, x_words, x_scales, hT, e_words, e_scales, 
         hraw = keep.tile([P, 4, V], F32, name="hraw", align_bytes=64)
         hsrc = [hraw[:, :, P * i : P * (i + 1)] for i in range(NT)]
         hb = {i: keep.tile([P, P, 4], BF16, name=f"hb{i}", align_bytes=64) for i in range(2)}
-        hq = {i: keep.tile([P, P], U32, name=f"hq{i}", align_bytes=64) for i in range(2)}
+        hq = {0: keep.tile([P, P], U32, name="hq0", align_bytes=64)}
         hs = [keep.tile([P, P], U8, name=f"hs{i}", align_bytes=64) for i in range(NT)]
         xg = [keep.tile([P, H], U32, name=f"xg{d}", align_bytes=64) for d in range(2)]
         xsg = keep.tile([P, S], U8, name="xsg", align_bytes=64)
@@ -48,7 +49,7 @@ def tile_picked_yivf_cal_p_kernel(tc, x_words, x_scales, hT, e_words, e_scales, 
         esg = keep.tile([P, R], U8, name="esg", align_bytes=64)
         eplane = keep.tile([P, R], U8, name="eplane", align_bytes=64)
         gg = lay.tile([P, S], F32, name="gg", align_bytes=64, offset=16384)
-        gcol = lay.tile([P, NT], F32, name="gcol", align_bytes=64, offset=18432)
+        gcol = keep.tile([P, NT], F32, name="gcol", align_bytes=64)
         ident = keep.tile([P, P], F32, name="ident", align_bytes=64)
         z = [keep.tile([P, ZW], F32, name=f"z{i}", align_bytes=64) for i in range(NT)]
         pieces = [(i, d) for d in range(2) for i in range(NT)]
@@ -59,25 +60,25 @@ def tile_picked_yivf_cal_p_kernel(tc, x_words, x_scales, hT, e_words, e_scales, 
 
         nc.vector.memset(es[0 : P - 16, :].bitcast(I32), 0)
         nc.vector.memset(z[0][:, R:], 0.0)
-        nc.vector.memset(gwin[0 : P - 1, :], 0.0)
-        nc.vector.memset(xs[0:48, :].bitcast(I32), 0)
-        nc.gpsimd.memset(xs[64:P, :].bitcast(I32), 0)
+        nc.vector.memset(eplane[:].bitcast(I32), 0)
+        nc.vector.memset(gwin[0 : P - 1, 0:GAIN_CUT], 0.0)
+        nc.gpsimd.memset(gwin[0 : P - 1, GAIN_CUT:T], 0.0)
+        nc.gpsimd.memset(xs[0 : P - 16, :].bitcast(I32), 0)
 
         nc.sync.dma_start(offs_t[:], offs)
         nc.scalar.dma_start(es[P - 16 : P, :].bitcast(I32), e_scales[0].bitcast(I32))
         nc.sync.dma_start(cent_t[:], cent)
         nc.scalar.dma_start(gwin[P - 1 : P, :], gain[0:1, :])
-        nc.sync.dma_start(xs[48:64, :].bitcast(I32), x_scales[0].bitcast(I32))
+        nc.sync.dma_start(xs[P - 16 : P, :].bitcast(I32), x_scales[0].bitcast(I32))
         nc.sync.dma_start(hraw[:], hT.rearrange("(p j) t -> p j t", j=4))
         nc.sync.dma_start(ew[:], e_words[0].rearrange("p n t -> p (n t)").bitcast(I32))
         nc.sync.dma_start(cell_t[:], cell)
 
         nc.scalar.copy(z[1][:, R:], z[0][:, R:])
-        nc.gpsimd.memset(eplane[:].bitcast(I32), 0)
+        make_identity(nc, ident[:])
         nc.gpsimd.memset(xplane[:].bitcast(I32), 0)
         for i in range(2, NT):
             nc.gpsimd.memset(z[i][:, R:], 0.0)
-        make_identity(nc, ident[:])
 
         halves = [slice(0, H), slice(H, S)]
         chunks = [slice(P * c, P * (c + 1)) for c in range(NT)]
@@ -117,7 +118,7 @@ def tile_picked_yivf_cal_p_kernel(tc, x_words, x_scales, hT, e_words, e_scales, 
         deal_rows(eplane, esg, P - 16)
         nc.sync.dma_start(xw[:], x_words[0].rearrange("p n t -> p (n t)").bitcast(I32))
         nc.vector.tensor_copy(xsg[:], xs[:].indirect(offs_t[:]))
-        deal_rows(xplane, xsg, 48)
+        deal_rows(xplane, xsg, P - 16)
         for d in range(2):
             nc.scalar.activation(gg[:, halves[d]], gwin[:].indirect(offs_t[:, lists[d]]), ACT.Copy)
         for i in range(2):
@@ -129,18 +130,16 @@ def tile_picked_yivf_cal_p_kernel(tc, x_words, x_scales, hT, e_words, e_scales, 
         gb = [psum.tile([P, H], F32, name=f"gb{d}", tag=f"b{1 + d}") for d in range(2)]
         for c in range(NT):
             nc.tensor.transpose(gb[c // 2][:, chunks[c % 2]], gcol[:, c : c + 1].to_broadcast([P, P]), ident[:])
+        for i in range(2, NT):
+            hb[i] = lay.tile([P, P, 4], BF16, name=f"hb{i}", align_bytes=64, offset=16384 + 1024 * (i - 2))
+            nc.scalar.copy(hb[i][:], hsrc[i].rearrange("p j t -> p t j"))
         gsb = keep.tile([P, H], F32, name="gsb", align_bytes=64)
         nc.scalar.copy(gsb[:], gb[0][:])
         gains = [gsb, gb[1]]
-        for i in range(2, NT):
-            hb[i] = lay.tile([P, P, 4], BF16, name=f"hb{i}", align_bytes=64, offset=16384 + 1024 * (i - 1))
-            nc.scalar.copy(hb[i][:], hsrc[i].rearrange("p j t -> p t j"))
         quantize(0)
-        quantize(1)
         nc.vector.tensor_copy(eg[:], ew[:].bitcast(U32).indirect(cent_t[:]))
         cell_scores(0, "b0")
-        cell_scores(1, "b1")
-        for i, tag in ((2, "b3"), (3, "b4")):
+        for i, tag in ((1, "b1"), (2, "b3"), (3, "b4")):
             hq[i] = lay.tile([P, P], U32, name=f"hq{i}", align_bytes=64, offset=12288 + 512 * i)
             quantize(i)
             cell_scores(i, tag)

@@ -32,7 +32,7 @@ def tile_picked_yivf_cal_p_kernel(tc, x_words, x_scales, hT, e_words, e_scales, 
         offs_t = keep.tile([P, S // 16], U16, name="offs_t")
         cent_t = keep.tile([P, R // 16], U16, name="cent_t")
         cell_t = keep.tile([P, S // 16], U16, name="cell_t")
-        xw = keep.tile([P, T], I32, name="xw", align_bytes=64)
+        xw = lay.tile([P, T], I32, name="xw", align_bytes=64, offset=0)
         xs = keep.tile([P, T], U8, name="xs", align_bytes=64)
         ew = lay.tile([P, W], I32, name="ew", align_bytes=64, offset=12288)
         es = keep.tile([P, W], U8, name="es", align_bytes=64)
@@ -53,7 +53,7 @@ def tile_picked_yivf_cal_p_kernel(tc, x_words, x_scales, hT, e_words, e_scales, 
         ident = keep.tile([P, P], F32, name="ident", align_bytes=64)
         z = [keep.tile([P, ZW], F32, name=f"z{i}", align_bytes=64) for i in range(NT)]
         pieces = [(i, d) for d in range(2) for i in range(NT)]
-        zg = {key: keep.tile([P, H], F32, name=f"zg{key[0]}{key[1]}", align_bytes=64) for key in pieces }
+        zg = {key: keep.tile([P, H], F32, name=f"zg{key[0]}{key[1]}", align_bytes=64) for key in pieces if key != (0, 1)}
         sums = {key: keep.tile([P, H], F32, name=f"sum{key[0]}{key[1]}", align_bytes=64) for key in pieces}
         scaled = [keep.tile([P, S], F32, name=f"scaled{i}", align_bytes=64) for i in range(NT)]
         res = [keep.tile([P, S], F32, name=f"res{i}", align_bytes=64) for i in range(NT)]
@@ -135,7 +135,6 @@ def tile_picked_yivf_cal_p_kernel(tc, x_words, x_scales, hT, e_words, e_scales, 
             nc.scalar.copy(hb[i][:], hsrc[i].rearrange("p j t -> p t j"))
         gsb = keep.tile([P, H], F32, name="gsb", align_bytes=64)
         nc.scalar.copy(gsb[:], gb[0][:])
-        gains = [gsb, gb[1]]
         quantize(0)
         nc.vector.tensor_copy(eg[:], ew[:].bitcast(U32).indirect(cent_t[:]))
         cell_scores(0, "b0")
@@ -143,18 +142,15 @@ def tile_picked_yivf_cal_p_kernel(tc, x_words, x_scales, hT, e_words, e_scales, 
             hq[i] = lay.tile([P, P], U32, name=f"hq{i}", align_bytes=64, offset=12288 + 512 * i)
             quantize(i)
             cell_scores(i, tag)
-        for i in range(NT):
-            for d in range(2):
-                look_up(i, d, i == 0)
+        for i, d in sorted(zg):
+            look_up(i, d, i == 0)
         for d in range(2):
             nc.vector.tensor_copy(xg[d][:], xw[:].bitcast(U32).indirect(offs_t[:, lists[d]]))
-        for i, d, tag in ((0, 0, "b5"), (1, 0, "b6"), (0, 1, "b7"), (1, 1, "b0"), (2, 0, "b1"), (2, 1, "b3"), (3, 0, "b4")):
+        for i, d, tag in ((0, 0, "b5"), (1, 0, "b6"), (1, 1, "b7"), (0, 1, "b0"), (2, 0, "b1"), (2, 1, "b3"), (3, 0, "b4")):
             scores(i, d, tag)
 
-        def scale(i, part):
-            d = part.start // H
-            within = slice(part.start - H * d, part.stop - H * d)
-            nc.vector.tensor_tensor(scaled[i][:, part], sums[i, d][:, within], gains[d][:, within], ALU.mult)
+        def scale(i):
+            nc.vector.tensor_tensor(scaled[i][:, halves[1]], sums[i, 1][:], gb[1][:], ALU.mult)
 
         def squash(i, part):
             nc.scalar.activation(res[i][:, part], scaled[i][:, part], ACT.Tanh)
@@ -168,20 +164,19 @@ def tile_picked_yivf_cal_p_kernel(tc, x_words, x_scales, hT, e_words, e_scales, 
         scores(3, 1, "b5")
         add(1, 0)
         scale_on_gpsimd(1)
-        add(0, 1)
+        zg[0, 1] = lay.tile([P, H], F32, name="zg01", align_bytes=64, offset=0)
+        look_up(0, 1, True)
         add(1, 1)
-        scale(0, halves[1])
+        add(0, 1)
         add(2, 0)
         scale_on_gpsimd(2)
-        scale(1, halves[1])
+        scale(1)
         add(2, 1)
+        scale(0)
         add(3, 0)
-        scale(2, halves[1])
+        scale_on_gpsimd(3)
+        scale(2)
         add(3, 1)
-        scale(3, halves[0])
-        for c in (2, 3):
-            scale(3, chunks[c])
-        for i in range(NT - 1):
+        scale(3)
+        for i in (1, 0, 2, 3):
             squash(i, slice(0, S))
-        squash(3, slice(0, 3 * P))
-        squash(3, chunks[3])

@@ -89,8 +89,9 @@ def tile_picked_yivf_cal_p_kernel(tc, x_words, x_scales, hT, e_words, e_scales, 
 
         def cell_scores(i, tag):
             zp = psum.tile([P, R], F32, name="zp", tag=tag)
-            nc.tensor.matmul_mx(out=zp[:], lhsT=hq[i][:].bitcast(FP8X4), lhsT_scale=hs[i][:],
-                                rhs=eg[:].bitcast(FP8X4), rhs_scale=eplane[:], start=True, stop=True)
+            for part in chunks[:2] if i == 0 else [slice(0, R)]:
+                nc.tensor.matmul_mx(out=zp[:, part], lhsT=hq[i][:].bitcast(FP8X4), lhsT_scale=hs[i][:],
+                                    rhs=eg[:, part].bitcast(FP8X4), rhs_scale=eplane[:, part], start=True, stop=True)
             nc.scalar.copy(z[i][:, 0:R], zp[:])
 
         def look_up(i, d, on_vector):
@@ -136,7 +137,8 @@ def tile_picked_yivf_cal_p_kernel(tc, x_words, x_scales, hT, e_words, e_scales, 
         gsb = keep.tile([P, H], F32, name="gsb", align_bytes=64)
         nc.scalar.copy(gsb[:], gb[0][:])
         quantize(0)
-        nc.vector.tensor_copy(eg[:], ew[:].bitcast(U32).indirect(cent_t[:]))
+        for c in range(2):
+            nc.vector.tensor_copy(eg[:, chunks[c]], ew[:].bitcast(U32).indirect(cent_t[:, 8 * c : 8 * (c + 1)]))
         cell_scores(0, "b0")
         for i, tag in ((1, "b1"), (2, "b3"), (3, "b4")):
             hq[i] = lay.tile([P, P], U32, name=f"hq{i}", align_bytes=64, offset=12288 + 512 * i)
@@ -146,7 +148,7 @@ def tile_picked_yivf_cal_p_kernel(tc, x_words, x_scales, hT, e_words, e_scales, 
             look_up(i, d, i == 0)
         for d in range(2):
             nc.vector.tensor_copy(xg[d][:], xw[:].bitcast(U32).indirect(offs_t[:, lists[d]]))
-        for i, d, tag in ((0, 0, "b5"), (1, 0, "b6"), (1, 1, "b7"), (0, 1, "b0"), (2, 0, "b1"), (2, 1, "b3"), (3, 0, "b4")):
+        for i, d, tag in ((1, 0, "b5"), (0, 0, "b6"), (1, 1, "b7"), (0, 1, "b0"), (2, 0, "b1"), (2, 1, "b3"), (3, 0, "b4")):
             scores(i, d, tag)
 
         def scale(i):
@@ -159,11 +161,11 @@ def tile_picked_yivf_cal_p_kernel(tc, x_words, x_scales, hT, e_words, e_scales, 
         def scale_on_gpsimd(i):
             nc.gpsimd.tensor_tensor(scaled[i][:, halves[0]], sums[i, 0][:], gsb[:], ALU.mult)
 
-        add(0, 0)
-        scale_on_gpsimd(0)
-        scores(3, 1, "b5")
         add(1, 0)
         scale_on_gpsimd(1)
+        scores(3, 1, "b5")
+        add(0, 0)
+        scale_on_gpsimd(0)
         zg[0, 1] = lay.tile([P, H], F32, name="zg01", align_bytes=64, offset=0)
         look_up(0, 1, True)
         add(1, 1)

@@ -36,7 +36,7 @@ def tile_picked_yivf_cal_p_kernel(tc, x_words, x_scales, hT, e_words, e_scales, 
         xs = keep.tile([P, T], U8, name="xs", align_bytes=64)
         ew = lay.tile([P, W], I32, name="ew", align_bytes=64, offset=12288)
         es = keep.tile([P, W], U8, name="es", align_bytes=64)
-        gwin = keep.tile([P, T], F32, name="gwin", align_bytes=64)
+        gwin = lay.tile([P, T], F32, name="gwin", align_bytes=64, offset=20480)
         hraw = keep.tile([P, 4, V], F32, name="hraw", align_bytes=64)
         hsrc = [hraw[:, :, P * i : P * (i + 1)] for i in range(NT)]
         hb = {i: keep.tile([P, P, 4], BF16, name=f"hb{i}", align_bytes=64) for i in range(2)}
@@ -51,9 +51,10 @@ def tile_picked_yivf_cal_p_kernel(tc, x_words, x_scales, hT, e_words, e_scales, 
         gg = lay.tile([P, S], F32, name="gg", align_bytes=64, offset=16384)
         gcol = keep.tile([P, NT], F32, name="gcol", align_bytes=64)
         ident = keep.tile([P, P], F32, name="ident", align_bytes=64)
-        z = [keep.tile([P, ZW], F32, name=f"z{i}", align_bytes=64) for i in range(NT)]
+        z = {i: keep.tile([P, ZW], F32, name=f"z{i}", align_bytes=64) for i in range(2)}
         pieces = [(i, d) for d in range(2) for i in range(NT)]
-        zg = {key: keep.tile([P, H], F32, name=f"zg{key[0]}{key[1]}", align_bytes=64) for key in pieces if key != (0, 1)}
+        zg = {key: keep.tile([P, H], F32, name=f"zg{key[0]}{key[1]}", align_bytes=64)[:] for key in ((0, 0), (1, 0), (1, 1))}
+        zrow = {i: keep.tile([P, S], F32, name=f"zrow{i}", align_bytes=64) for i in range(2, NT)}
         sums = {key: keep.tile([P, H], F32, name=f"sum{key[0]}{key[1]}", align_bytes=64) for key in pieces}
         scaled = [keep.tile([P, S], F32, name=f"scaled{i}", align_bytes=64) for i in range(NT)]
         res = [keep.tile([P, S], F32, name=f"res{i}", align_bytes=64) for i in range(NT)]
@@ -77,8 +78,6 @@ def tile_picked_yivf_cal_p_kernel(tc, x_words, x_scales, hT, e_words, e_scales, 
         nc.scalar.copy(z[1][:, R:], z[0][:, R:])
         make_identity(nc, ident[:])
         nc.gpsimd.memset(xplane[:].bitcast(I32), 0)
-        for i in range(2, NT):
-            nc.gpsimd.memset(z[i][:, R:], 0.0)
 
         halves = [slice(0, H), slice(H, S)]
         chunks = [slice(P * c, P * (c + 1)) for c in range(NT)]
@@ -96,9 +95,9 @@ def tile_picked_yivf_cal_p_kernel(tc, x_words, x_scales, hT, e_words, e_scales, 
 
         def look_up(i, d, on_vector):
             if on_vector:
-                nc.vector.tensor_copy(zg[i, d][:], z[i][:].indirect(cell_t[:, lists[d]]))
+                nc.vector.tensor_copy(zg[i, d], z[i][:].indirect(cell_t[:, lists[d]]))
             else:
-                nc.scalar.activation(zg[i, d][:], z[i][:].indirect(cell_t[:, lists[d]]), ACT.Copy)
+                nc.scalar.activation(zg[i, d], z[i][:].indirect(cell_t[:, lists[d]]), ACT.Copy)
 
         yp = {}
 
@@ -108,7 +107,7 @@ def tile_picked_yivf_cal_p_kernel(tc, x_words, x_scales, hT, e_words, e_scales, 
                                 rhs=xg[d][:].bitcast(FP8X4), rhs_scale=xplane[:, halves[d]], start=True, stop=True)
 
         def add(i, d):
-            nc.vector.tensor_tensor(sums[i, d][:], zg[i, d][:], yp[i, d][:], ALU.add)
+            nc.vector.tensor_tensor(sums[i, d][:], zg[i, d], yp[i, d][:], ALU.add)
 
         def deal_rows(plane, picked, first):
             for q in range(4):
@@ -122,6 +121,9 @@ def tile_picked_yivf_cal_p_kernel(tc, x_words, x_scales, hT, e_words, e_scales, 
         deal_rows(xplane, xsg, P - 16)
         for d in range(2):
             nc.scalar.activation(gg[:, halves[d]], gwin[:].indirect(offs_t[:, lists[d]]), ACT.Copy)
+        for i in range(2, NT):
+            z[i] = lay.tile([P, S + 16], F32, name=f"z{i}", align_bytes=64, offset=20480 + 4096 * (i - 2))
+            nc.scalar.copy(z[i][:, R:], z[0][:, R : R + 1].to_broadcast([P, S + 16 - R]))
         for i in range(2):
             nc.vector.tensor_copy(hb[i][:], hsrc[i].rearrange("p j t -> p t j"))
         gT = psum.tile([P, NT, P], F32, name="gT", tag="b0")
@@ -146,13 +148,17 @@ def tile_picked_yivf_cal_p_kernel(tc, x_words, x_scales, hT, e_words, e_scales, 
             cell_scores(i, tag)
         for i, d in sorted(zg):
             look_up(i, d, i == 0)
+        for i in range(2, NT):
+            nc.scalar.activation(zrow[i][:], z[i][:].indirect(cell_t[:]), ACT.Copy)
+            for d in range(2):
+                zg[i, d] = zrow[i][:, halves[d]]
         for d in range(2):
             nc.vector.tensor_copy(xg[d][:], xw[:].bitcast(U32).indirect(offs_t[:, lists[d]]))
         for i, d, tag in ((1, 0, "b5"), (0, 0, "b6"), (1, 1, "b7"), (0, 1, "b0"), (2, 0, "b1"), (2, 1, "b3"), (3, 0, "b4")):
             scores(i, d, tag)
 
-        def scale(i):
-            nc.vector.tensor_tensor(scaled[i][:, halves[1]], sums[i, 1][:], gb[1][:], ALU.mult)
+        def scale(i, part=slice(0, H)):
+            nc.vector.tensor_tensor(scaled[i][:, H + part.start : H + part.stop], sums[i, 1][:, part], gb[1][:, part], ALU.mult)
 
         def squash(i, part):
             nc.scalar.activation(res[i][:, part], scaled[i][:, part], ACT.Tanh)
@@ -166,7 +172,7 @@ def tile_picked_yivf_cal_p_kernel(tc, x_words, x_scales, hT, e_words, e_scales, 
         scores(3, 1, "b5")
         add(0, 0)
         scale_on_gpsimd(0)
-        zg[0, 1] = lay.tile([P, H], F32, name="zg01", align_bytes=64, offset=0)
+        zg[0, 1] = lay.tile([P, H], F32, name="zg01", align_bytes=64, offset=0)[:]
         look_up(0, 1, True)
         add(1, 1)
         add(0, 1)
@@ -179,6 +185,9 @@ def tile_picked_yivf_cal_p_kernel(tc, x_words, x_scales, hT, e_words, e_scales, 
         scale_on_gpsimd(3)
         scale(2)
         add(3, 1)
-        scale(3)
-        for i in (1, 0, 2, 3):
+        for c in range(2):
+            scale(3, chunks[c])
+        for i in (1, 0, 2):
             squash(i, slice(0, S))
+        squash(3, slice(0, 3 * P))
+        squash(3, chunks[3])

@@ -18,8 +18,8 @@ ALU = mybir.AluOpType
 P = 128
 NT = 4
 H = 256
-ZW = R + 16
-GAIN_CUT = 1280
+ZW = R + 17
+GAIN_CUT = 896
 
 
 def tile_picked_yivf_cal_p_kernel(tc, x_words, x_scales, hT, e_words, e_scales, gain, offs, cent, cell, out):
@@ -35,8 +35,8 @@ def tile_picked_yivf_cal_p_kernel(tc, x_words, x_scales, hT, e_words, e_scales, 
         xw = lay.tile([P, T], I32, name="xw", align_bytes=64, offset=0)
         xs = keep.tile([P, T], U8, name="xs", align_bytes=64)
         ew = lay.tile([P, W], I32, name="ew", align_bytes=64, offset=12288)
-        es = keep.tile([P, W], U8, name="es", align_bytes=64)
-        gwin = lay.tile([P, T], F32, name="gwin", align_bytes=64, offset=20480)
+        es = keep.tile([P, W + 4], U8, name="es", align_bytes=64)
+        gwin = lay.tile([P, T + 1], F32, name="gwin", align_bytes=64, offset=20480)
         hraw = keep.tile([P, 4, V], F32, name="hraw", align_bytes=64)
         hsrc = [hraw[:, :, P * i : P * (i + 1)] for i in range(NT)]
         hb = {i: keep.tile([P, P, 4], BF16, name=f"hb{i}", align_bytes=64) for i in range(2)}
@@ -47,7 +47,7 @@ def tile_picked_yivf_cal_p_kernel(tc, x_words, x_scales, hT, e_words, e_scales, 
         xplane = keep.tile([P, S], U8, name="xplane", align_bytes=64)
         eg = keep.tile([P, R], U32, name="eg", align_bytes=64)
         esg = keep.tile([P, R], U8, name="esg", align_bytes=64)
-        eplane = keep.tile([P, R], U8, name="eplane", align_bytes=64)
+        eplane = keep.tile([P, R + 4], U8, name="eplane", align_bytes=64)
         gg = lay.tile([P, S], F32, name="gg", align_bytes=64, offset=16384)
         gcol = keep.tile([P, NT], F32, name="gcol", align_bytes=64)
         ident = keep.tile([P, P], F32, name="ident", align_bytes=64)
@@ -59,17 +59,17 @@ def tile_picked_yivf_cal_p_kernel(tc, x_words, x_scales, hT, e_words, e_scales, 
         scaled = [keep.tile([P, S], F32, name=f"scaled{i}", align_bytes=64) for i in range(NT)]
         res = [keep.tile([P, S], F32, name=f"res{i}", align_bytes=64) for i in range(NT)]
 
-        nc.vector.memset(es[0 : P - 16, :].bitcast(I32), 0)
         nc.vector.memset(z[0][:, R:], 0.0)
+        nc.vector.memset(es[0 : P - 16, :].bitcast(I32), 0)
         nc.vector.memset(eplane[:].bitcast(I32), 0)
-        nc.vector.memset(gwin[0 : P - 1, 0:GAIN_CUT], 0.0)
-        nc.gpsimd.memset(gwin[0 : P - 1, GAIN_CUT:T], 0.0)
+        nc.vector.memset(gwin[0 : P - 1, GAIN_CUT:], 0.0)
+        nc.gpsimd.memset(gwin[0 : P - 1, 0:GAIN_CUT], 0.0)
         nc.gpsimd.memset(xs[0 : P - 16, :].bitcast(I32), 0)
 
         nc.sync.dma_start(offs_t[:], offs)
-        nc.scalar.dma_start(es[P - 16 : P, :].bitcast(I32), e_scales[0].bitcast(I32))
+        nc.scalar.dma_start(es[P - 16 : P, 0:W].bitcast(I32), e_scales[0].bitcast(I32))
         nc.sync.dma_start(cent_t[:], cent)
-        nc.scalar.dma_start(gwin[P - 1 : P, :], gain[0:1, :])
+        nc.scalar.dma_start(gwin[P - 1 : P, 0:T], gain[0:1, :])
         nc.sync.dma_start(xs[P - 16 : P, :].bitcast(I32), x_scales[0].bitcast(I32))
         nc.sync.dma_start(hraw[:], hT.rearrange("(p j) t -> p j t", j=4))
         nc.sync.dma_start(ew[:], e_words[0].rearrange("p n t -> p (n t)").bitcast(I32))
@@ -112,20 +112,20 @@ def tile_picked_yivf_cal_p_kernel(tc, x_words, x_scales, hT, e_words, e_scales, 
         def deal_rows(plane, picked, first):
             for q in range(4):
                 rows = first + 4 * q
-                nc.sync.dma_start(plane[32 * q : 32 * q + 4, :].bitcast(I32), picked[rows : rows + 4, :].bitcast(I32))
+                nc.sync.dma_start(plane[32 * q : 32 * q + 4, 0 : picked.shape[1]].bitcast(I32), picked[rows : rows + 4, :].bitcast(I32))
 
-        nc.vector.tensor_copy(esg[:], es[:].indirect(cent_t[:]))
+        nc.vector.tensor_copy(esg[:], es[:, 0:W].indirect(cent_t[:]))
         deal_rows(eplane, esg, P - 16)
         nc.sync.dma_start(xw[:], x_words[0].rearrange("p n t -> p (n t)").bitcast(I32))
         nc.vector.tensor_copy(xsg[:], xs[:].indirect(offs_t[:]))
         deal_rows(xplane, xsg, P - 16)
         for d in range(2):
-            nc.scalar.activation(gg[:, halves[d]], gwin[:].indirect(offs_t[:, lists[d]]), ACT.Copy)
+            nc.scalar.activation(gg[:, halves[d]], gwin[:, 0:T].indirect(offs_t[:, lists[d]]), ACT.Copy)
         for i in range(2, NT):
             z[i] = lay.tile([P, S + 16], F32, name=f"z{i}", align_bytes=64, offset=20480 + 4096 * (i - 2))
             nc.scalar.copy(z[i][:, R:], z[0][:, R : R + 1].to_broadcast([P, S + 16 - R]))
-        for i in range(2):
-            nc.vector.tensor_copy(hb[i][:], hsrc[i].rearrange("p j t -> p t j"))
+        nc.vector.tensor_copy(hb[0][:], hsrc[0].rearrange("p j t -> p t j"))
+        nc.vector.tensor_copy(hb[1][:], hsrc[1].rearrange("p j t -> p t j"))
         gT = psum.tile([P, NT, P], F32, name="gT", tag="b0")
         for c in range(NT):
             nc.tensor.transpose(gT[:, c, :], gg[:, chunks[c]], ident[:])

@@ -53,7 +53,7 @@ def tile_picked_yivf_cal_p_kernel(tc, x_words, x_scales, hT, e_words, e_scales, 
         ident = keep.tile([P, P], F32, name="ident", align_bytes=64)
         z = {i: keep.tile([P, ZW], F32, name=f"z{i}", align_bytes=64) for i in range(2)}
         pieces = [(i, d) for d in range(2) for i in range(NT)]
-        zg = {key: keep.tile([P, H], F32, name=f"zg{key[0]}{key[1]}", align_bytes=64)[:] for key in ((0, 0), (1, 0), (1, 1))}
+        zg = {key: keep.tile([P, H], F32, name=f"zg{key[0]}{key[1]}", align_bytes=64)[:] for key in pieces if key[0] < 2}
         zrow = {i: keep.tile([P, S], F32, name=f"zrow{i}", align_bytes=64) for i in range(2, NT)}
         sums = {key: keep.tile([P, H], F32, name=f"sum{key[0]}{key[1]}", align_bytes=64) for key in pieces}
         scaled = [keep.tile([P, S], F32, name=f"scaled{i}", align_bytes=64) for i in range(NT)]
@@ -86,12 +86,18 @@ def tile_picked_yivf_cal_p_kernel(tc, x_words, x_scales, hT, e_words, e_scales, 
         def quantize(i):
             nc.vector.quantize_mx(out=hq[i][:].bitcast(FP8X4), scales=hs[i][:], in_=hb[i][:].rearrange("p t j -> p (t j)"))
 
+        zps = {}
+
         def cell_scores(i, tag):
             zp = psum.tile([P, R], F32, name="zp", tag=tag)
             for part in chunks[:2] if i == 0 else [slice(0, R)]:
                 nc.tensor.matmul_mx(out=zp[:, part], lhsT=hq[i][:].bitcast(FP8X4), lhsT_scale=hs[i][:],
                                     rhs=eg[:, part].bitcast(FP8X4), rhs_scale=eplane[:, part], start=True, stop=True)
-            nc.scalar.copy(z[i][:, 0:R], zp[:])
+            zps[i] = zp
+            if i in (0, 2):
+                nc.scalar.copy(z[i][:, 0:R], zp[:])
+            elif i == 1:
+                nc.vector.tensor_copy(z[i][:, 0:R], zp[:])
 
         def look_up(i, d, on_vector):
             if on_vector:
@@ -121,9 +127,8 @@ def tile_picked_yivf_cal_p_kernel(tc, x_words, x_scales, hT, e_words, e_scales, 
         deal_rows(xplane, xsg, P - 16)
         for d in range(2):
             nc.scalar.activation(gg[:, halves[d]], gwin[:, 0:T].indirect(offs_t[:, lists[d]]), ACT.Copy)
-        for i in range(2, NT):
-            z[i] = lay.tile([P, S + 16], F32, name=f"z{i}", align_bytes=64, offset=20480 + 4096 * (i - 2))
-            nc.scalar.copy(z[i][:, R:], z[0][:, R : R + 1].to_broadcast([P, S + 16 - R]))
+        z[2] = lay.tile([P, S + 16], F32, name="z2", align_bytes=64, offset=20480)
+        nc.scalar.copy(z[2][:, R:], z[0][:, R : R + 1].to_broadcast([P, S + 16 - R]))
         nc.vector.tensor_copy(hb[0][:], hsrc[0].rearrange("p j t -> p t j"))
         nc.vector.tensor_copy(hb[1][:], hsrc[1].rearrange("p j t -> p t j"))
         gT = psum.tile([P, NT, P], F32, name="gT", tag="b0")
@@ -147,14 +152,19 @@ def tile_picked_yivf_cal_p_kernel(tc, x_words, x_scales, hT, e_words, e_scales, 
             quantize(i)
             cell_scores(i, tag)
         for i, d in sorted(zg):
-            look_up(i, d, i == 0)
-        for i in range(2, NT):
-            nc.scalar.activation(zrow[i][:], z[i][:].indirect(cell_t[:]), ACT.Copy)
-            for d in range(2):
-                zg[i, d] = zrow[i][:, halves[d]]
+            look_up(i, d, (i, d) == (0, 0))
         for d in range(2):
             nc.vector.tensor_copy(xg[d][:], xw[:].bitcast(U32).indirect(offs_t[:, lists[d]]))
-        for i, d, tag in ((1, 0, "b5"), (0, 0, "b6"), (1, 1, "b7"), (0, 1, "b0"), (2, 0, "b1"), (2, 1, "b3"), (3, 0, "b4")):
+        z[3] = lay.tile([P, ZW], F32, name="z3", align_bytes=64, offset=0)
+        nc.vector.tensor_copy(z[3][:, 0:R], zps[3][:])
+        nc.gpsimd.memset(z[3][:, R:], 0.0)
+        for i in range(2, NT):
+            for d in range(2):
+                zg[i, d] = zrow[i][:, halves[d]]
+        nc.scalar.activation(zrow[2][:], z[2][:].indirect(cell_t[:]), ACT.Copy)
+        for d in range(2):
+            look_up(3, d, False)
+        for i, d, tag in ((0, 0, "b5"), (1, 0, "b6"), (0, 1, "b7"), (1, 1, "b0"), (2, 0, "b1"), (2, 1, "b3"), (3, 0, "b4")):
             scores(i, d, tag)
 
         def scale(i, part=slice(0, H)):
@@ -167,27 +177,25 @@ def tile_picked_yivf_cal_p_kernel(tc, x_words, x_scales, hT, e_words, e_scales, 
         def scale_on_gpsimd(i):
             nc.gpsimd.tensor_tensor(scaled[i][:, halves[0]], sums[i, 0][:], gsb[:], ALU.mult)
 
-        add(1, 0)
-        scale_on_gpsimd(1)
-        scores(3, 1, "b5")
         add(0, 0)
         scale_on_gpsimd(0)
-        zg[0, 1] = lay.tile([P, H], F32, name="zg01", align_bytes=64, offset=0)[:]
-        look_up(0, 1, True)
-        add(1, 1)
+        scores(3, 1, "b5")
+        add(1, 0)
+        scale_on_gpsimd(1)
         add(0, 1)
+        add(1, 1)
+        scale(0)
         add(2, 0)
         scale_on_gpsimd(2)
         scale(1)
         add(2, 1)
-        scale(0)
         add(3, 0)
         scale_on_gpsimd(3)
         scale(2)
         add(3, 1)
         for c in range(2):
             scale(3, chunks[c])
-        for i in (1, 0, 2):
+        for i in range(3):
             squash(i, slice(0, S))
         squash(3, slice(0, 3 * P))
         squash(3, chunks[3])

@@ -19,7 +19,7 @@ P = 128
 NT = 4
 H = 256
 ZW = R + 17
-GAIN_CUT = 896
+GAIN_CUT = 1088
 
 
 def tile_picked_yivf_cal_p_kernel(tc, x_words, x_scales, hT, e_words, e_scales, gain, offs, cent, cell, out):
@@ -33,23 +33,22 @@ def tile_picked_yivf_cal_p_kernel(tc, x_words, x_scales, hT, e_words, e_scales, 
         cent_t = keep.tile([P, R // 16], U16, name="cent_t")
         cell_t = keep.tile([P, S // 16], U16, name="cell_t")
         xw = lay.tile([P, T], I32, name="xw", align_bytes=64, offset=0)
-        xs = keep.tile([P, T], U8, name="xs", align_bytes=64)
+        xs = keep.tile([P, T + 4], U8, name="xs", align_bytes=64)
         ew = lay.tile([P, W], I32, name="ew", align_bytes=64, offset=12288)
         es = keep.tile([P, W + 4], U8, name="es", align_bytes=64)
         gwin = lay.tile([P, T + 1], F32, name="gwin", align_bytes=64, offset=20480)
         hraw = keep.tile([P, 4, V], F32, name="hraw", align_bytes=64)
         hsrc = [hraw[:, :, P * i : P * (i + 1)] for i in range(NT)]
         hb = {i: keep.tile([P, P, 4], BF16, name=f"hb{i}", align_bytes=64) for i in range(2)}
-        hq = {0: keep.tile([P, P], U32, name="hq0", align_bytes=64)}
+        hq = {i: keep.tile([P, P], U32, name=f"hq{i}", align_bytes=64) for i in range(2)}
         hs = [keep.tile([P, P], U8, name=f"hs{i}", align_bytes=64) for i in range(NT)]
-        xg = [keep.tile([P, H], U32, name=f"xg{d}", align_bytes=64) for d in range(2)]
+        xg = {1: keep.tile([P, H], U32, name="xg1", align_bytes=64)}
         xsg = keep.tile([P, S], U8, name="xsg", align_bytes=64)
         xplane = keep.tile([P, S], U8, name="xplane", align_bytes=64)
-        eg = keep.tile([P, R], U32, name="eg", align_bytes=64)
         esg = keep.tile([P, R], U8, name="esg", align_bytes=64)
         eplane = keep.tile([P, R + 4], U8, name="eplane", align_bytes=64)
         gg = lay.tile([P, S], F32, name="gg", align_bytes=64, offset=16384)
-        gcol = keep.tile([P, NT], F32, name="gcol", align_bytes=64)
+        gcol = lay.tile([P, NT], F32, name="gcol", align_bytes=64, offset=8192)
         ident = keep.tile([P, P], F32, name="ident", align_bytes=64)
         z = {i: keep.tile([P, ZW], F32, name=f"z{i}", align_bytes=64) for i in range(2)}
         pieces = [(i, d) for d in range(2) for i in range(NT)]
@@ -63,21 +62,22 @@ def tile_picked_yivf_cal_p_kernel(tc, x_words, x_scales, hT, e_words, e_scales, 
         nc.vector.memset(es[0 : P - 16, :].bitcast(I32), 0)
         nc.vector.memset(eplane[:].bitcast(I32), 0)
         nc.vector.memset(gwin[0 : P - 1, GAIN_CUT:], 0.0)
+        nc.vector.memset(xs[0 : P - 16, :].bitcast(I32), 0)
+        nc.gpsimd.memset(ident[:], 0.0)
+        nc.gpsimd.memset(xplane[:].bitcast(I32), 0)
+        make_identity(nc, ident[:], nomemset=True)
         nc.gpsimd.memset(gwin[0 : P - 1, 0:GAIN_CUT], 0.0)
-        nc.gpsimd.memset(xs[0 : P - 16, :].bitcast(I32), 0)
 
         nc.sync.dma_start(offs_t[:], offs)
         nc.scalar.dma_start(es[P - 16 : P, 0:W].bitcast(I32), e_scales[0].bitcast(I32))
         nc.sync.dma_start(cent_t[:], cent)
         nc.scalar.dma_start(gwin[P - 1 : P, 0:T], gain[0:1, :])
-        nc.sync.dma_start(xs[P - 16 : P, :].bitcast(I32), x_scales[0].bitcast(I32))
+        nc.sync.dma_start(xs[P - 16 : P, 0:T].bitcast(I32), x_scales[0].bitcast(I32))
         nc.sync.dma_start(hraw[:], hT.rearrange("(p j) t -> p j t", j=4))
         nc.sync.dma_start(ew[:], e_words[0].rearrange("p n t -> p (n t)").bitcast(I32))
         nc.sync.dma_start(cell_t[:], cell)
 
         nc.scalar.copy(z[1][:, R:], z[0][:, R:])
-        make_identity(nc, ident[:])
-        nc.gpsimd.memset(xplane[:].bitcast(I32), 0)
 
         halves = [slice(0, H), slice(H, S)]
         chunks = [slice(P * c, P * (c + 1)) for c in range(NT)]
@@ -89,15 +89,15 @@ def tile_picked_yivf_cal_p_kernel(tc, x_words, x_scales, hT, e_words, e_scales, 
         zps = {}
 
         def cell_scores(i, tag):
-            zp = psum.tile([P, R], F32, name="zp", tag=tag)
-            for part in chunks[:2] if i == 0 else [slice(0, R)]:
-                nc.tensor.matmul_mx(out=zp[:, part], lhsT=hq[i][:].bitcast(FP8X4), lhsT_scale=hs[i][:],
+            for part, bank in ((chunks[0], tag), (chunks[1], "b5")) if i == 0 else [(slice(0, R), tag)]:
+                zp = psum.tile([P, part.stop - part.start], F32, name="zp", tag=bank)
+                nc.tensor.matmul_mx(out=zp[:], lhsT=hq[i][:].bitcast(FP8X4), lhsT_scale=hs[i][:],
                                     rhs=eg[:, part].bitcast(FP8X4), rhs_scale=eplane[:, part], start=True, stop=True)
-            zps[i] = zp
-            if i in (0, 2):
-                nc.scalar.copy(z[i][:, 0:R], zp[:])
-            elif i == 1:
-                nc.vector.tensor_copy(z[i][:, 0:R], zp[:])
+                zps[i] = zp
+                if i in (0, 2):
+                    nc.scalar.copy(z[i][:, part], zp[:])
+                elif i == 1:
+                    nc.vector.tensor_copy(z[i][:, part], zp[:])
 
         def look_up(i, d, on_vector):
             if on_vector:
@@ -123,7 +123,7 @@ def tile_picked_yivf_cal_p_kernel(tc, x_words, x_scales, hT, e_words, e_scales, 
         nc.vector.tensor_copy(esg[:], es[:, 0:W].indirect(cent_t[:]))
         deal_rows(eplane, esg, P - 16)
         nc.sync.dma_start(xw[:], x_words[0].rearrange("p n t -> p (n t)").bitcast(I32))
-        nc.vector.tensor_copy(xsg[:], xs[:].indirect(offs_t[:]))
+        nc.vector.tensor_copy(xsg[:], xs[:, 0:T].indirect(offs_t[:]))
         deal_rows(xplane, xsg, P - 16)
         for d in range(2):
             nc.scalar.activation(gg[:, halves[d]], gwin[:, 0:T].indirect(offs_t[:, lists[d]]), ACT.Copy)
@@ -143,16 +143,23 @@ def tile_picked_yivf_cal_p_kernel(tc, x_words, x_scales, hT, e_words, e_scales, 
             nc.scalar.copy(hb[i][:], hsrc[i].rearrange("p j t -> p t j"))
         gsb = keep.tile([P, H], F32, name="gsb", align_bytes=64)
         nc.scalar.copy(gsb[:], gb[0][:])
-        quantize(0)
+        for i in range(2):
+            quantize(i)
+        eg = lay.tile([P, R], U32, name="eg", align_bytes=64, offset=8192)
         for c in range(2):
             nc.vector.tensor_copy(eg[:, chunks[c]], ew[:].bitcast(U32).indirect(cent_t[:, 8 * c : 8 * (c + 1)]))
         cell_scores(0, "b0")
         for i, tag in ((1, "b1"), (2, "b3"), (3, "b4")):
-            hq[i] = lay.tile([P, P], U32, name=f"hq{i}", align_bytes=64, offset=12288 + 512 * i)
-            quantize(i)
+            if i > 1:
+                hq[i] = lay.tile([P, P], U32, name=f"hq{i}", align_bytes=64, offset=12288 + 512 * i)
+                quantize(i)
             cell_scores(i, tag)
-        for i, d in sorted(zg):
-            look_up(i, d, (i, d) == (0, 0))
+            if i == 1:
+                for d in range(2):
+                    look_up(0, d, d == 0)
+        for d in range(2):
+            look_up(1, d, False)
+        xg[0] = lay.tile([P, H], U32, name="xg0", align_bytes=64, offset=17408)
         for d in range(2):
             nc.vector.tensor_copy(xg[d][:], xw[:].bitcast(U32).indirect(offs_t[:, lists[d]]))
         z[3] = lay.tile([P, ZW], F32, name="z3", align_bytes=64, offset=0)

@@ -83,6 +83,9 @@ def tile_picked_yivf_cal_p_kernel(tc, x_words, x_scales, hT, e_words, e_scales, 
         chunks = [slice(P * c, P * (c + 1)) for c in range(NT)]
         lists = [slice(0, H // 16), slice(H // 16, S // 16)]
 
+        def interleaved(i):
+            return hb[i][:].rearrange("p (c n) j -> p c j n", n=4), hsrc[i].rearrange("p j (c n) -> p c j n", n=4)
+
         def quantize(i):
             nc.vector.quantize_mx(out=hq[i][:].bitcast(FP8X4), scales=hs[i][:], in_=hb[i][:].rearrange("p t j -> p (t j)"))
 
@@ -129,8 +132,8 @@ def tile_picked_yivf_cal_p_kernel(tc, x_words, x_scales, hT, e_words, e_scales, 
             nc.scalar.activation(gg[:, halves[d]], gwin[:, 0:T].indirect(offs_t[:, lists[d]]), ACT.Copy)
         z[2] = lay.tile([P, S + 16], F32, name="z2", align_bytes=64, offset=20480)
         nc.scalar.copy(z[2][:, R:], z[0][:, R : R + 1].to_broadcast([P, S + 16 - R]))
-        nc.vector.tensor_copy(hb[0][:], hsrc[0].rearrange("p j t -> p t j"))
-        nc.vector.tensor_copy(hb[1][:], hsrc[1].rearrange("p j t -> p t j"))
+        for i in range(2):
+            nc.vector.tensor_copy(*interleaved(i))
         gT = psum.tile([P, NT, P], F32, name="gT", tag="b0")
         for c in range(NT):
             nc.tensor.transpose(gT[:, c, :], gg[:, chunks[c]], ident[:])
@@ -140,7 +143,7 @@ def tile_picked_yivf_cal_p_kernel(tc, x_words, x_scales, hT, e_words, e_scales, 
             nc.tensor.transpose(gb[c // 2][:, chunks[c % 2]], gcol[:, c : c + 1].to_broadcast([P, P]), ident[:])
         for i in range(2, NT):
             hb[i] = lay.tile([P, P, 4], BF16, name=f"hb{i}", align_bytes=64, offset=16384 + 1024 * (i - 2))
-            nc.scalar.copy(hb[i][:], hsrc[i].rearrange("p j t -> p t j"))
+            nc.scalar.copy(*interleaved(i))
         gsb = keep.tile([P, H], F32, name="gsb", align_bytes=64)
         nc.scalar.copy(gsb[:], gb[0][:])
         for i in range(2):

from contextlib import ExitStack

import concourse.mybir as mybir
from concourse.masks import make_identity

K, T, S, V, R, W = 512, 2048, 512, 512, 256, 1024
FLOPS = 2 * K * V * (S + R)

F32 = mybir.dt.float32
BF16 = mybir.dt.bfloat16
I32 = mybir.dt.int32
U32 = mybir.dt.uint32
U16 = mybir.dt.uint16
U8 = mybir.dt.uint8
FP8X4 = mybir.dt.float8_e4m3fn_x4
ACT = mybir.ActivationFunctionType
ALU = mybir.AluOpType
P = 128
NT = 4
H = 256
ZW = R + 17
GAIN_CUT = 1088


def tile_picked_yivf_cal_p_kernel(tc, x_words, x_scales, hT, e_words, e_scales, gain, offs, cent, cell, out):
    nc = tc.nc
    with ExitStack() as ctx:
        keep = ctx.enter_context(tc.tile_pool(name="keep", bufs=1))
        lay = ctx.enter_context(tc.tile_pool(name="lay", bufs=1))
        psum = ctx.enter_context(tc.psum_pool(name="psum", bufs=1))

        offs_t = keep.tile([P, S // 16], U16, name="offs_t")
        cent_t = keep.tile([P, R // 16], U16, name="cent_t")
        cell_t = keep.tile([P, S // 16], U16, name="cell_t")
        xw = lay.tile([P, T], I32, name="xw", align_bytes=64, offset=0)
        xs = keep.tile([P, T + 4], U8, name="xs", align_bytes=64)
        ew = lay.tile([P, W], I32, name="ew", align_bytes=64, offset=12288)
        es = keep.tile([P, W + 4], U8, name="es", align_bytes=64)
        gwin = lay.tile([P, T + 1], F32, name="gwin", align_bytes=64, offset=20480)
        hraw = keep.tile([P, 4, V], F32, name="hraw", align_bytes=64)
        hsrc = [hraw[:, :, P * i : P * (i + 1)] for i in range(NT)]
        hb = {i: keep.tile([P, P, 4], BF16, name=f"hb{i}", align_bytes=64) for i in range(2)}
        hq = {i: keep.tile([P, P], U32, name=f"hq{i}", align_bytes=64) for i in range(2)}
        hs = [keep.tile([P, P], U8, name=f"hs{i}", align_bytes=64) for i in range(NT)]
        xg = {1: keep.tile([P, H], U32, name="xg1", align_bytes=64)}
        xsg = keep.tile([P, S], U8, name="xsg", align_bytes=64)
        xplane = keep.tile([P, S], U8, name="xplane", align_bytes=64)
        esg = keep.tile([P, R], U8, name="esg", align_bytes=64)
        eplane = keep.tile([P, R + 4], U8, name="eplane", align_bytes=64)
        gg = lay.tile([P, S], F32, name="gg", align_bytes=64, offset=16384)
        gcol = lay.tile([P, NT], F32, name="gcol", align_bytes=64, offset=8192)
        ident = keep.tile([P, P], F32, name="ident", align_bytes=64)
        z = {i: keep.tile([P, ZW], F32, name=f"z{i}", align_bytes=64) for i in range(2)}
        pieces = [(i, d) for d in range(2) for i in range(NT)]
        zg = {key: keep.tile([P, H], F32, name=f"zg{key[0]}{key[1]}", align_bytes=64)[:] for key in pieces if key[0] < 2}
        zrow = {i: keep.tile([P, S], F32, name=f"zrow{i}", align_bytes=64) for i in range(2, NT)}
        sums = {key: keep.tile([P, H], F32, name=f"sum{key[0]}{key[1]}", align_bytes=64) for key in pieces}
        scaled = [keep.tile([P, S], F32, name=f"scaled{i}", align_bytes=64) for i in range(NT)]
        res = [keep.tile([P, S], F32, name=f"res{i}", align_bytes=64) for i in range(NT)]

        nc.vector.memset(z[0][:, R:], 0.0)
        nc.vector.memset(es[0 : P - 16, :].bitcast(I32), 0)
        nc.vector.memset(eplane[:].bitcast(I32), 0)
        nc.vector.memset(gwin[0 : P - 1, GAIN_CUT:], 0.0)
        nc.vector.memset(xs[0 : P - 16, :].bitcast(I32), 0)
        nc.gpsimd.memset(ident[:], 0.0)
        nc.gpsimd.memset(xplane[:].bitcast(I32), 0)
        make_identity(nc, ident[:], nomemset=True)
        nc.gpsimd.memset(gwin[0 : P - 1, 0:GAIN_CUT], 0.0)

        nc.sync.dma_start(offs_t[:], offs)
        nc.scalar.dma_start(es[P - 16 : P, 0:W].bitcast(I32), e_scales[0].bitcast(I32))
        nc.sync.dma_start(cent_t[:], cent)
        nc.scalar.dma_start(gwin[P - 1 : P, 0:T], gain[0:1, :])
        nc.sync.dma_start(xs[P - 16 : P, 0:T].bitcast(I32), x_scales[0].bitcast(I32))
        nc.sync.dma_start(hraw[:], hT.rearrange("(p j) t -> p j t", j=4))
        nc.sync.dma_start(ew[:], e_words[0].rearrange("p n t -> p (n t)").bitcast(I32))
        nc.sync.dma_start(cell_t[:], cell)

        nc.scalar.copy(z[1][:, R:], z[0][:, R:])

        halves = [slice(0, H), slice(H, S)]
        chunks = [slice(P * c, P * (c + 1)) for c in range(NT)]
        lists = [slice(0, H // 16), slice(H // 16, S // 16)]

        def interleaved(i):
            return hb[i][:].rearrange("p (c n) j -> p c j n", n=4), hsrc[i].rearrange("p j (c n) -> p c j n", n=4)

        def quantize(i):
            nc.vector.quantize_mx(out=hq[i][:].bitcast(FP8X4), scales=hs[i][:], in_=hb[i][:].rearrange("p t j -> p (t j)"))

        zps = {}

        def cell_scores(i, tag):
            for part, bank in ((chunks[0], tag), (chunks[1], "b5")) if i == 0 else [(slice(0, R), tag)]:
                zp = psum.tile([P, part.stop - part.start], F32, name="zp", tag=bank)
                nc.tensor.matmul_mx(out=zp[:], lhsT=hq[i][:].bitcast(FP8X4), lhsT_scale=hs[i][:],
                                    rhs=eg[:, part].bitcast(FP8X4), rhs_scale=eplane[:, part], start=True, stop=True)
                zps[i] = zp
                if i in (0, 2):
                    nc.scalar.copy(z[i][:, part], zp[:])
                elif i == 1:
                    nc.vector.tensor_copy(z[i][:, part], zp[:])

        def look_up(i, d, on_vector):
            if on_vector:
                nc.vector.tensor_copy(zg[i, d], z[i][:].indirect(cell_t[:, lists[d]]))
            else:
                nc.scalar.activation(zg[i, d], z[i][:].indirect(cell_t[:, lists[d]]), ACT.Copy)

        yp = {}

        def scores(i, d, tag):
            yp[i, d] = psum.tile([P, H], F32, name="yp", tag=tag)
            nc.tensor.matmul_mx(out=yp[i, d][:], lhsT=hq[i][:].bitcast(FP8X4), lhsT_scale=hs[i][:],
                                rhs=xg[d][:].bitcast(FP8X4), rhs_scale=xplane[:, halves[d]], start=True, stop=True)

        def add(i, d):
            nc.vector.tensor_tensor(sums[i, d][:], zg[i, d], yp[i, d][:], ALU.add)

        def deal_rows(plane, picked, first):
            for q in range(4):
                rows = first + 4 * q
                nc.sync.dma_start(plane[32 * q : 32 * q + 4, 0 : picked.shape[1]].bitcast(I32), picked[rows : rows + 4, :].bitcast(I32))

        nc.vector.tensor_copy(esg[:], es[:, 0:W].indirect(cent_t[:]))
        deal_rows(eplane, esg, P - 16)
        nc.sync.dma_start(xw[:], x_words[0].rearrange("p n t -> p (n t)").bitcast(I32))
        nc.vector.tensor_copy(xsg[:], xs[:, 0:T].indirect(offs_t[:]))
        deal_rows(xplane, xsg, P - 16)
        for d in range(2):
            nc.scalar.activation(gg[:, halves[d]], gwin[:, 0:T].indirect(offs_t[:, lists[d]]), ACT.Copy)
        z[2] = lay.tile([P, S + 16], F32, name="z2", align_bytes=64, offset=20480)
        nc.scalar.copy(z[2][:, R:], z[0][:, R : R + 1].to_broadcast([P, S + 16 - R]))
        for i in range(2):
            nc.vector.tensor_copy(*interleaved(i))
        gT = psum.tile([P, NT, P], F32, name="gT", tag="b0")
        for c in range(NT):
            nc.tensor.transpose(gT[:, c, :], gg[:, chunks[c]], ident[:])
        nc.scalar.copy(gcol[:], gT[:, :, P - 1])
        gb = [psum.tile([P, H], F32, name=f"gb{d}", tag=f"b{1 + d}") for d in range(2)]
        for c in range(NT):
            nc.tensor.transpose(gb[c // 2][:, chunks[c % 2]], gcol[:, c : c + 1].to_broadcast([P, P]), ident[:])
        for i in range(2, NT):
            hb[i] = lay.tile([P, P, 4], BF16, name=f"hb{i}", align_bytes=64, offset=16384 + 1024 * (i - 2))
            nc.scalar.copy(*interleaved(i))
        gsb = keep.tile([P, H], F32, name="gsb", align_bytes=64)
        nc.scalar.copy(gsb[:], gb[0][:])
        for i in range(2):
            quantize(i)
        eg = lay.tile([P, R], U32, name="eg", align_bytes=64, offset=8192)
        for c in range(2):
            nc.vector.tensor_copy(eg[:, chunks[c]], ew[:].bitcast(U32).indirect(cent_t[:, 8 * c : 8 * (c + 1)]))
        cell_scores(0, "b0")
        for i, tag in ((1, "b1"), (2, "b3"), (3, "b4")):
            if i > 1:
                hq[i] = lay.tile([P, P], U32, name=f"hq{i}", align_bytes=64, offset=12288 + 512 * i)
                quantize(i)
            cell_scores(i, tag)
            if i == 1:
                for d in range(2):
                    look_up(0, d, d == 0)
        for d in range(2):
            look_up(1, d, False)
        xg[0] = lay.tile([P, H], U32, name="xg0", align_bytes=64, offset=17408)
        for d in range(2):
            nc.vector.tensor_copy(xg[d][:], xw[:].bitcast(U32).indirect(offs_t[:, lists[d]]))
        z[3] = lay.tile([P, ZW], F32, name="z3", align_bytes=64, offset=0)
        nc.vector.tensor_copy(z[3][:, 0:R], zps[3][:])
        nc.gpsimd.memset(z[3][:, R:], 0.0)
        for i in range(2, NT):
            for d in range(2):
                zg[i, d] = zrow[i][:, halves[d]]
        nc.scalar.activation(zrow[2][:], z[2][:].indirect(cell_t[:]), ACT.Copy)
        for d in range(2):
            look_up(3, d, False)
        for i, d, tag in ((0, 0, "b5"), (1, 0, "b6"), (0, 1, "b7"), (1, 1, "b0"), (2, 0, "b1"), (2, 1, "b3"), (3, 0, "b4")):
            scores(i, d, tag)

        def scale(i, part=slice(0, H)):
            nc.vector.tensor_tensor(scaled[i][:, H + part.start : H + part.stop], sums[i, 1][:, part], gb[1][:, part], ALU.mult)

        def squash(i, part):
            nc.scalar.activation(res[i][:, part], scaled[i][:, part], ACT.Tanh)
            nc.sync.dma_start(out[P * i : P * (i + 1), part], res[i][:, part])

        def scale_on_gpsimd(i):
            nc.gpsimd.tensor_tensor(scaled[i][:, halves[0]], sums[i, 0][:], gsb[:], ALU.mult)

        add(0, 0)
        scale_on_gpsimd(0)
        scores(3, 1, "b5")
        add(1, 0)
        scale_on_gpsimd(1)
        add(0, 1)
        add(1, 1)
        scale(0)
        add(2, 0)
        scale_on_gpsimd(2)
        scale(1)
        add(2, 1)
        add(3, 0)
        scale_on_gpsimd(3)
        scale(2)
        add(3, 1)
        for c in range(2):
            scale(3, chunks[c])
        for i in range(3):
            squash(i, slice(0, S))
        squash(3, slice(0, 3 * P))
        squash(3, chunks[3])
